import numpy as np, ml_dtypes
CORES = [2,6,10,14,18,22,26,30]
N = 8
BF = ml_dtypes.bfloat16
W, Q, TV, HOP, M = 4096, 192, 6, 3, 8
def parts(rng):
    hi = rng.choice(np.array([64, 128, 192, 256]), (N, 8, 1, W)); p = np.floor(hi * rng.random((N, 8, 16, W)))
    lo = rng.choice(np.array([0, 32, 64, 128, 192]), (N, 8, 1, Q)); y = lo + np.floor((256 - lo) * rng.random((N, 8, 16, Q)))
    L = rng.integers(0, W, (N, 8, 16, Q)); share = rng.choice(np.array([0.0, 0.1, 0.3, 0.7, 1.0]), (N, 8, 1, Q))
    C = np.where(rng.random((N, 8, 16, Q)) < share, rng.integers(0, W, (N, 8, 16, Q)), -1)
    o = rng.integers(0, 16, (N, 8, 16, Q)); b = np.minimum(rng.integers(0, 8, (N, 8, 16, Q)), rng.integers(0, 8, (N, 8, 16, Q)))
    return p, y, L, C, o, b, rng.integers(0, 4, (N, 8, 16, TV))
def pack(p, y, L, C, o, b, lim):
    def half(a): return np.ascontiguousarray(np.asarray(a, np.float32).reshape(N, 128, -1)).astype(BF)
    def whole(a): return np.ascontiguousarray(np.asarray(a).reshape(N, 128, -1)).astype(np.int32)
    return {"prop": half(p), "lem": whole(L), "con": whole(C), "org": half(o), "cnt": half(b), "ex": half(y), "lim": whole(lim)}
def setup_inputs(rng):
    return pack(*parts(rng))
def setup_inputs_spread(rng):
    p, y, L, C, o, b, lim = parts(rng)
    p = np.minimum(np.floor(np.exp2(8 * rng.random((N, 8, 1, W))) * rng.random((N, 8, 16, W))), 255)
    y = np.minimum(np.floor(np.exp2(2 + 6 * rng.random((N, 8, 1, Q))) * rng.random((N, 8, 16, Q))), 255)
    y = np.where(rng.random((N, 8, 1, Q)) < 0.5, 255 - y, y)
    L = np.minimum(np.floor(W * rng.random((N, 8, 16, Q)) ** 3), W - 1)
    C = np.where(C >= 0, W - 1 - np.minimum(np.floor(W * rng.random((N, 8, 16, Q)) ** 3), W - 1), -1)
    o = np.minimum(np.floor(16 * rng.random((N, 8, 16, Q)) ** 2), 15); b = rng.integers(0, 8, (N, 8, 16, Q))
    return pack(p, y, L, C, o, b, lim)
def setup_inputs_ends(rng):
    p = 255 * (rng.random((N, 8, 16, W)) < rng.choice(np.array([0.0, 0.5, 1.0]), (N, 8, 1, W))).astype(np.int64)
    y = 255 * (rng.random((N, 8, 16, Q)) < rng.choice(np.array([0.0, 0.5, 1.0]), (N, 8, 1, Q))).astype(np.int64)
    just = np.argsort(rng.random((N, 8, 16, Q)), axis=2) < 16 - M
    y = np.where(rng.random((N, 8, 1, Q)) < 0.25, 255 * just, y)
    L = (W - 1) * rng.integers(0, 2, (N, 8, 16, Q)); share = rng.choice(np.array([0.0, 0.5, 1.0]), (N, 8, 1, Q))
    C = np.where(rng.random((N, 8, 16, Q)) < share, W - 1, -1)
    o = 15 * rng.integers(0, 2, (N, 8, 16, Q)); b = 7 * rng.integers(0, 2, (N, 8, 16, Q)); lim = 3 * rng.integers(0, 2, (N, 8, 16, TV))
    turn = int(rng.integers(0, 4))
    for r in range(N):
        for g in range(8):
            w = (r + g + turn) % 4
            if (r, g) in ((0, 0), (N - 1, 7)): w = 3
            if (r, g) in ((0, 7), (N - 1, 6)): w = 1
            pm = rng.permutation(16)
            p[r, g, :, 0] = (0 * pm, 0 * pm + 255, 255 * (pm < M), 0 * pm)[w]
            p[r, g, :, W - 1] = (0 * pm + 255, 0 * pm, 255 * (pm < M - 1), 0 * pm)[w]
            for c in (0, Q - 1):
                if w == 3: y[r, g, :, c] = 255
                if w == 1:
                    y[r, g, :, c] = 0; L[r, g, :, c] = W - 1; L[r, g, 15, c] = 0; C[r, g, :, c] = W - 1; C[r, g, 15, c] = -1
                if w == 0:
                    y[r, g, :, c] = 254 + (pm < 16 - M); L[r, g, :, c] = 0; L[r, g, 15, c] = W - 1; C[r, g, :, c] = 0
    return pack(p, y, L, C, o, b, lim)
def setup_inputs_corners(rng):
    p, y, L, C, o, b, lim = parts(rng)
    p[..., :W // 4] = np.floor(0.125 * p[..., :W // 4]); p[..., W // 2:] = 96 + np.floor(160 * rng.random((N, 8, 16, W - W // 2))); p[..., W - 1] = 255
    y = 32 + np.floor(224 * rng.random((N, 8, 16, Q))); y = np.where(rng.random((N, 8, 1, Q)) < 0.125, 255, y)
    e = (np.arange(Q).reshape(1, 1, 1, Q) + rng.integers(0, 6, (N, 8, 1, 1))) % 6; k = np.arange(16).reshape(1, 1, 16, 1)
    name = np.where(rng.random((N, 8, 1, Q)) < 0.6, rng.integers(0, W // 4, (N, 8, 16, Q)), rng.integers(0, W, (N, 8, 16, Q)))
    hole = rng.choice(np.array([0, 15, 15, 6]), (N, 8, 1, Q))
    has = np.where(e == 0, False, np.where(e == 2, k != hole, np.where(e == 3, k == 15, True)))
    C = np.where(has, name, -1)
    L = np.where(rng.random((N, 8, 1, Q)) < 0.5, rng.integers(W // 2, W, (N, 8, 16, Q)), L)
    mode = rng.integers(0, 4, (N, 8, 1, Q)); o = np.where(mode == 0, k, np.where(mode == 1, 0, np.where(mode == 2, 15, o)))
    b = rng.choice(np.array([0, 0, 1, 3, 6, 7]), (N, 8, 16, Q)); b = np.where(e == 4, 7, np.where(e == 5, 7 * (k == 15), b))
    lim = 3 * rng.integers(0, 2, (N, 8, 16, TV))
    for c in (Q - 2, Q - 1):
        y[:, :, :, c] = 0; C[:, :, :, c] = -1; C[:, :, 15, c] = W - 1; b[:, :, 15, c] = 0
    y[:, 0, :, Q - 2] = 255; C[:, 0, :, Q - 2] = -1
    return pack(p, y, L, C, o, b, lim)
def setup_inputs_ties(rng):
    p, y, L, C, o, b, lim = parts(rng)
    base = rng.integers(2, 254, (1, 8, 16, 1))
    m = np.where(rng.random((N, 8, 1, W)) < 0.06, M + rng.integers(0, 2, (N, 8, 1, W)), rng.choice(np.array([M - 1, M - 1, M - 2, 0]), (N, 8, 1, W)))
    up = np.argsort(rng.random((N, 8, 16, W)), axis=2) < m
    p = base + np.where(m == 0, 0, np.where(up, 1, 0 - rng.integers(0, 2, (N, 8, 16, W))))
    y = base + np.where(rng.random((N, 8, 1, Q)) < 0.6, 0, rng.integers(-1, 2, (N, 8, 16, Q)))
    b = rng.integers(0, 3, (N, 8, 16, Q))
    p[..., :80] = (np.arange(80).reshape(1, 80) + np.arange(16).reshape(16, 1)) >> 4
    y[..., Q - 16:] = 255; L[..., Q - 16:] = rng.integers(0, 80, (N, 8, 16, 16)); L[..., Q - 8:] = rng.integers(0, 2, (N, 8, 16, 8))
    L[:, :, 0, Q - 16:] = 0; L[:, :, 15, Q - 8:] = 1
    us = np.arange(2048, 4081 - M).reshape(-1, 1); names = np.arange(2048, W).reshape(1, -1); x = us * names
    iu, ia = np.nonzero(((x & 63) == 32) & (x > 2 ** 23) & ((((x >> 5) + names + 97) & 255) == 0) & ((names & 255) < Q - 16))
    if len(iu) > 0:
        for g in range(8):
            s = int(rng.integers(0, len(iu))); u = int(us[iu[s], 0]); a = int(names[0, ia[s]]); c = a & 255
            p[:, g, :, a] = 255; y[:, g, :, c] = (u + np.argsort(rng.random((N, 16)), axis=1)) >> 4
            C[:, g, :, c] = -1; C[:, g, 0, c] = a; o[:, g, 0, c] = 0; b[:, g, 0, c] = 7
    return pack(p, y, L, C, o, b, lim)
def setup_inputs_alike(rng):
    p, y, L, C, o, b, lim = parts(rng); c = np.arange(Q).reshape(1, 1, 1, Q)
    few = np.array([0, W - 1, W // 2, 3])
    L[:, 0::4] = rng.choice(few, (N, 2, 16, Q))
    L[:, 1::4] = np.repeat(L[:, 1::4, :1], 16, axis=2)
    L[:, 2::4] = 256 * rng.integers(0, W // 256, (N, 2, 16, Q)) + c
    L[:, 3::4] = 256 * rng.integers(0, W // 256, (N, 2, 16, Q)) + (c + 1) % Q
    own = rng.random((N, 8, 1, Q)) < 0.5
    C = np.where((C >= 0) & own, L[:, :, ::-1], C); b[:, ::2] = 2
    return pack(p, y, L, C, o, b, lim)
def check_inputs(d):
    bad = []
    for k, lo, hi in (("prop", 0, 255), ("lem", 0, W - 1), ("con", -1, W - 1), ("org", 0, 15), ("cnt", 0, 7), ("ex", 0, 255), ("lim", 0, 3)):
        a = np.asarray(d[k]).astype(np.float64)
        if not (np.min(a) >= lo and np.max(a) <= hi): bad.append("range of " + k)
        elif not np.all(a == np.floor(a)): bad.append("whole numbers in " + k)
    return bad
def pick(p, a):
    return np.take_along_axis(p, a.reshape(N, 8, 1, 16 * Q), 3).reshape(N, 8, 16, 16, Q)
def at(a, k):
    return np.take_along_axis(a, k[:, :, None, :], 2)[:, :, 0]
def reference(prop, lem, con, org, cnt, ex, lim):
    p = prop.astype(np.float32).astype(np.int16).reshape(N, 8, 16, W); y = ex.astype(np.float32).astype(np.int16).reshape(N, 8, 16, Q)
    L = lem.astype(np.int64).reshape(N, 8, 16, Q); C = con.astype(np.int64).reshape(N, 8, 16, Q)
    o = org.astype(np.float32).astype(np.int64).reshape(N, 8, 16, Q); b = cnt.astype(np.float32).astype(np.int64).reshape(N, 8, 16, Q)
    lm = lim.astype(np.int64).reshape(N, 8, 16, TV); w = np.zeros((N, Q), np.int64)
    rows = np.arange(16).reshape(1, 1, 16, 1); lane = np.arange(Q).reshape(1, 1, Q)
    for t in range(TV):
        y5 = y[:, :, :, None, :]; pl = pick(p, L); pc = pick(p, np.maximum(C, 0))
        bar = (np.add.reduce(pc > y5, axis=2, dtype=np.int64) >= M) & (C >= 0)
        gui = np.add.reduce(pl > y5, axis=2, dtype=np.int64) >= M
        score = np.add.reduce(np.abs(pl - y5), axis=2, dtype=np.int64); u = np.add.reduce(y, axis=2, dtype=np.int64)
        barred = np.any(bar, axis=2); some = np.any(gui, axis=2); guilty = ~barred & some; clear = ~barred & ~some
        kb = np.argmax(bar, axis=2); hit = barred[:, :, None] & (rows == kb[:, :, None]); b1 = b + hit
        over = hit & (b1 > lm[:, :, :, t:t + 1] + w[:, None, None, :]); back = np.any(over, axis=2)
        L1 = np.where(back[:, :, None] & (rows == at(o, kb)[:, :, None]), at(C, kb)[:, :, None], L)
        C1 = np.where(over, -1, C); b1 = np.where(over, 0, b1)
        kg = np.argmax(gui, axis=2); old = at(L, kg); empty = C < 0
        slot = np.where(np.any(empty, axis=2), np.argmax(empty, axis=2), np.argmax(b, axis=2)); put = guilty[:, :, None] & (rows == slot[:, :, None])
        n = ((((u * old) >> 5) + old + 97 * t) & (W - 256)) + lane
        C1 = np.where(put, old[:, :, None], C1); o1 = np.where(put, kg[:, :, None], o); b1 = np.where(put, 0, b1)
        L1 = np.where(guilty[:, :, None] & (rows == kg[:, :, None]), n[:, :, None], L1)
        pv = np.take_along_axis(pl, kg[:, :, None, None, :], 3)[:, :, :, 0]
        np.put_along_axis(p, n[:, :, None, :], np.where(guilty[:, :, None], np.minimum(pv, y), np.take_along_axis(p, n[:, :, None, :], 3)), 3)
        y = np.where(guilty[:, :, None], np.abs(y - pv), y)
        ks = np.argmin(score, axis=2); new = (((u * u) >> 5) + 37 * u + t) & (W - 1)
        L1 = np.where(clear[:, :, None] & (rows == ks[:, :, None]), new[:, :, None], L1)
        w = np.add.reduce(barred, axis=1, dtype=np.int64) & 3
        L, C, o, b = L1, C1, o1, b1
        if t < TV - 1: L, C, o, b = [np.roll(a, HOP, axis=0) for a in (L, C, o, b)]
    def half(a): return a.reshape(N, 128, -1).astype(np.float32).astype(BF)
    return {"zp": half(p), "zl": L.reshape(N, 128, Q).astype(np.float32), "zc": C.reshape(N, 128, Q).astype(np.float32), "zo": half(o), "zb": half(b), "zy": half(y)}

@@ -1,0 +1,543 @@
+from concourse.mybir import AluOpType, ActivationFunctionType
+
+N, W, Q, TV, HOP = 8, 4096, 192, 6, 3
+NPOS = 16 * Q
+PW = 4608
+DUMP = 4352
+LCH = [(0, 64), (64, 128), (128, 192)]
+CCH = [(0, 64), (64, 128)]
+SCH = [(128, 160), (160, 192)]
+
+F32, BF, I32, U16 = "float32", "bfloat16", "int32", "uint16"
+SCRATCH = {}
+for _n, _w, _d in (
+        ("P", PW, BF), ("D", NPOS + Q, BF), ("AB0", NPOS + Q, BF), ("AB1", NPOS + Q, BF), ("SG", NPOS, BF), ("IC", NPOS, BF),
+        ("YE", NPOS, BF), ("CR", NPOS, BF), ("YL", Q, U16),
+        ("inL", Q, I32), ("inC", Q, I32), ("inO", Q, BF), ("inB", Q, BF), ("inLim", 8, I32), ("limF", 8, F32),
+        ("MSK", Q, F32), ("RSTL", Q, F32), ("RSTC", Q, F32), ("KT", Q, BF), ("CL", Q, BF), ("CC", Q, BF), ("ONE", 128, BF),
+        ("Z1", 144, BF), ("ZL", 144, BF), ("ZC", 144, BF), ("ZS", 144, BF), ("GW", 128, BF), ("BO", 128, BF), ("EY", 128, BF), ("NE", 128, BF),
+        ("PM", Q, BF), ("S00", 128, F32), ("S01", 128, F32), ("S10", 128, F32), ("S11", 128, F32),
+        ("pI", Q, I32), ("qI", Q, I32), ("kI", Q, I32), ("nI", 144, I32), ("mpI", 128, I32), ("c16I", Q, I32),
+        ("b4", 8, I32), ("bF", 8, F32), ("cF", 48, F32), ("c256", 12, I32),
+        ("X0", 384, F32), ("X1", 384, BF), ("ML0", Q, F32), ("ML1", Q, F32), ("MV0", Q, F32), ("MV1", Q, F32), ("MO0", 384, BF), ("MO1", 384, BF),
+        ("TL0", 256, F32), ("TL1", 256, F32), ("TV0", 256, F32), ("TV1", 256, F32), ("TO0", 448, BF), ("TO1", 448, BF), ("E0", 384, F32), ("oB", 384, BF),
+        ("B00", 128, BF), ("B01", 128, BF), ("B10", 128, BF), ("B11", 128, BF), ("KX", 1072, I32), ("TX", 7 * Q, F32), ("tF", Q, I32),
+        ("y_", Q, F32), ("KEYC", Q, F32), ("SLT", Q, F32), ("tS", Q, I32), ("mkL", Q, F32), ("mk", Q, F32), ("hot", Q, F32),
+        ("RLS", 384, F32), ("RC", Q, F32), ("bL", Q, F32), ("bR", Q, F32), ("bN", Q, F32),
+        ("dif", Q, F32), ("sL", Q, I32), ("sM", Q, I32), ("sC", Q, I32), ("LI", 312, I32), ("LF", 480, F32), ("Bf", 12, BF), ("LST", 24, U16),
+        ("md", Q, BF), ("nD", Q, BF)):
+    SCRATCH[_n] = ("sbuf", [128, _w], _d)
+for _n in ("XL", "XS", "XC", "VP1", "VP2", "VT", "OB", "SWP"):
+    SCRATCH[_n] = ("psum", [128, 512], F32)
+for _t in range(TV):
+    SCRATCH["PM1_%d" % (_t % 2)] = ("sbuf", [128, Q], BF)
+    SCRATCH["DL%d" % (_t % 2)] = ("sbuf", [128, Q], F32)
+    SCRATCH["oL%d" % (_t % 2)] = ("sbuf", [128, Q], U16)
+    SCRATCH["oC%d" % (_t % 2)] = ("sbuf", [128, Q], U16)
+    SCRATCH["oV%d" % (_t % 2)] = ("sbuf", [128, 2 * Q], I32)
+    if _t:
+        SCRATCH["aL%d" % _t] = ("sbuf", [128, Q], U16)
+        SCRATCH["aC%d" % _t] = ("sbuf", [128, Q], U16)
+        SCRATCH["aV%d" % _t] = ("sbuf", [128, 2 * Q], I32)
+SEMAPHORES = ["sv", "ss", "st", "sg"] + [k + i for k in ("lL", "lC", "lV") for i in "01"] + ["d%d" % i for i in range(16)] + [k + "%d" % t for k in ("qL", "qC", "qV") for t in range(1, TV)]
+PART = {"cv": ("cF", 0, 12), "cp": ("cF", 12, 12), "cb": ("cF", 24, 24),
+        "k1": ("KX", 0, Q), "k2": ("KX", Q, Q), "k5": ("KX", 384, 128), "k6": ("KX", 512, 128), "k7": ("KX", 640, 128), "k8": ("KX", 768, 12),
+        "k9": ("KX", 784, 144), "k10": ("KX", 928, 144), "tA": ("TX", 0, Q), "tB": ("TX", Q, Q), "tC": ("TX", 2 * Q, Q), "tD": ("TX", 3 * Q, Q),
+        "tE": ("TX", 4 * Q, Q), "k3": ("TX", 5 * Q, Q), "k4": ("TX", 6 * Q, Q),
+        "u": ("XC", 192, 12), "w": ("XC", 208, 12), "lm": ("XC", 224, 192), "RL": ("RLS", 0, 192), "RS": ("RLS", 192, 192)}
+BONUS = 4.0
+CY, FX, WK = 0.00092, 0.03, 0.08
+
+
+def rank_program(g, core, T, topo):
+    rank = T.rank_of(core)
+    if rank is None:
+        return
+    dst = T.cores[(rank + HOP) % N]
+    rid, pid = topo.addr(dst)[:2]
+    emask = topo.mask(core, dst)
+    neng = len(topo.engines(core, dst))
+    op = AluOpType
+    af = ActivationFunctionType
+    queues = {"v": g.vector, "s": g.scalar, "t": g.tensor, "g": g, "y": g.sync}
+    semof = {"v": "sv", "s": "ss", "t": "st", "g": "sg"}
+    ops, wr, rd = [], {}, {}
+    psum = {k for k in SCRATCH if SCRATCH[k][0] == "psum"}
+
+    def A(name, lo=0, hi=None, st=1):
+        if name in PART:
+            name, base, n = PART[name]
+            lo, hi = base + lo, base + (n if hi is None else hi)
+        hi = SCRATCH[name][1][1] if hi is None else hi
+        return (name, lo, hi, T[name][:, lo:hi] if st == 1 else T[name][:, lo:hi:st], len(range(lo, hi, st)))
+
+    def emit(e, fn, R, Wt, cost, sem=None, inc=1, lat=0.0, deps=()):
+        need = list(deps)
+        for x in R:
+            for (l, h, o) in wr.get(x[0], []):
+                if (l < x[2] and x[1] < h) or (x[0] in psum and o["e"] != e):
+                    need.append(o)
+            if x[0] in psum:
+                need += [o for (l, h, o) in rd.get(x[0], []) if o["e"] != e]
+        for x in Wt:
+            for (l, h, o) in wr.get(x[0], []) + rd.get(x[0], []):
+                if (l < x[2] and x[1] < h) or (x[0] in psum and o["e"] != e):
+                    need.append(o)
+        me = {"e": e, "fn": fn, "need": need, "cost": cost, "sem": sem or semof.get(e), "inc": inc, "lat": lat, "i": len(ops), "soft": [], "bonus": 0.0}
+        ops.append(me)
+        for x in R:
+            rd.setdefault(x[0], []).append((x[1], x[2], me))
+        for x in Wt:
+            nm, lo, hi = x[:3]
+            wr[nm] = [y for y in wr.get(nm, []) if not (lo <= y[0] and y[1] <= hi)] + [(lo, hi, me)]
+            rd[nm] = [y for y in rd.get(nm, []) if not (lo <= y[0] and y[1] <= hi) or y[2] is me]
+        return me
+
+    def two(x):
+        return SCRATCH[x[0]][2] in (BF, U16)
+
+    def vc(o, ins):
+        n = max([x[4] for x in [o] + ins])
+        return FX + CY * max(64, n * (0.5 if all(two(x) for x in [o] + ins) else 1))
+
+    def ts(o, i, s1, op0, s2=None, op1=None):
+        if op1 is None:
+            return emit("v", lambda q: q.tensor_scalar(o[3], i[3], s1, None, op0), [i], [o], vc(o, [i]))
+        sc = s2[3] if isinstance(s2, tuple) else s2
+        return emit("v", lambda q: q.tensor_scalar(o[3], i[3], s1, sc, op0, op1), [i] + ([s2] if isinstance(s2, tuple) else []), [o], vc(o, [i]))
+
+    def tt(o, a, b, o_):
+        k = 1 if a[0] in psum or b[0] in psum else 2
+        return emit("v", lambda q: q.tensor_tensor(o[3], a[3], b[3], o_), [a, b], [o], FX + CY * max(64, k * o[4]))
+
+    def cp(o, i):
+        return emit("v", lambda q: q.tensor_copy(o[3], i[3]), [i], [o], vc(o, [i]))
+
+    def fill(o, c):
+        return emit("v", lambda q: q.memset(o[3], c), [], [o], vc(o, []))
+
+    def scan(o, d0, d1, init, p0, p1):
+        return emit("v", lambda q: q.tensor_tensor_scan(o[3], d0[3], d1[3], init, p0, p1), [d0, d1], [o], vc(o, [d0, d1]))
+
+    def vtr(o, i):
+        return emit("v", lambda q: q.transpose(o[3], i[3]), [i], [o], vc(o, [i]))
+
+    def act(o, i, f, bias=0.0, scale=1.0, off=None):
+        src = i[3].indirect(off[3]) if off else i[3]
+        f = af.Identity if f == af.Copy and bias else f
+        sc, extra = (scale[3], [scale]) if isinstance(scale, tuple) else (scale, [])
+        return emit("s", lambda q: q.activation(o[3], src, f, bias=bias, scale=sc), [i] + ([off] if off else []) + extra, [o],
+                    (0.065 + 1.56 * CY * o[4]) if off else FX + CY * max(64, o[4]))
+
+    def pool(o, fn):
+        return emit("g", fn, [], [o], 0.13 + 2 * CY * o[4])
+
+    def iota(o, pattern, base, cm):
+        if SCRATCH[o[0]][2] == I32:
+            return pool(o, lambda q: q.iota(o[3], pattern, base, cm))
+        return pool(o, lambda q: q.iota(o[3], pattern, base, cm, allow_small_or_imprecise_dtypes=True))
+
+    def mms(o, terms):
+        R = [x for t in terms for x in t]
+
+        def go(q):
+            for j, (l, r) in enumerate(terms):
+                ins = q.matmul(o[3], l[3], r[3], j == 0, j == len(terms) - 1)
+            return ins
+        k = 4 if SCRATCH[terms[0][0][0]][2] == F32 else 1
+        return emit("t", go, R, [o], FX + 0.00078 * k * max(64, o[4]) * len(terms))
+
+    nd = [0]
+
+    def dma(e, o, i, R, Wt, lat):
+        s = "d%d" % nd[0]
+        nd[0] += 1
+        return emit(e, lambda q: q.dma_start(o, i), R, Wt, 0.05, sem=s, inc=16, lat=lat)
+
+    def LI(j, n=1):
+        return A("LI", 12 * j, 12 * (j + n))
+
+    def LF(j, n=1):
+        return A("LF", 12 * j, 12 * (j + n))
+
+    def send(k, nxt):
+        o, i = "a%s%d" % (k, nxt), "o%s%d" % (k, nxt % 2)
+        sl = "l%s%d" % (k, nxt % 2)
+        wid = SCRATCH[o][1][1]
+        lat = 1.6 + 128 * wid * (2 if k != "V" else 4) / 60e3
+        me = emit("g", lambda q: q.remote_dma(out_ap=T[o][:, :], in_ap=T[i][:, :], remote_sem=T.sem["q%s%d" % (k, nxt)], local_sem=T.sem[sl],
+                                              pid=pid, routing_id=rid, dma_engine_mask=emask), [A(i)], [], 0.6, sem=sl, inc=-neng, lat=lat)
+        net = {"e": "net", "need": [me], "cost": lat, "sem": "q%s%d" % (k, nxt), "v": neng, "inc": 0, "lat": 0.0, "i": len(ops), "soft": [], "bonus": 0.0}
+        ops.append(net)
+        wr[o] = [(0, wid, net)]
+
+    dma("y", T.inC[:, :], T.con[:, :], [], [A("inC")], 2.0)
+    dma("y", T.inO[:, :], T.org[:, :], [], [A("inO")], 2.0)
+    dma("s", T.inB[:, :], T.cnt[:, :], [], [A("inB")], 2.0)
+    dma("y", T.inL[:, :], T.lem[:, :], [], [A("inL")], 2.2)
+    dma("s", T.AB0[:, NPOS:NPOS + Q], T.ex[:, :], [], [A("AB0", NPOS, NPOS + Q)], 2.2)
+    dma("y", T.inLim[:, 0:TV], T.lim[:, :], [], [A("inLim", 0, TV)], 2.2)
+    dma("y", T.P[:, 0:W], T.prop[:, :], [], [A("P", 0, W)], 6.0)
+
+    iota(A("mpI"), [[1, 128]], 0, -1)
+    iota(A("pI"), [[0, Q]], 0, 1)
+    iota(A("kI"), [[0, 12], [1, 16]], 0, 0)
+    iota(A("nI"), [[1, 144]], 0, 0)
+    iota(A("c16I"), [[16, 12], [0, 16]], 0, 0)
+    iota(A("c256"), [[256, 12]], 0, 0)
+    iota(A("KT"), [[0, 12], [-1, 16]], 15, 0)
+    for x in ("TL0", "TL1", "TV0", "TV1", "TO0", "TO1"):
+        n = SCRATCH[x][1][1]
+        iota(A(x, 0, 32), [[0, 32]], 0, 0)
+        iota(A(x, n - 32, n), [[0, 32]], 0, 0)
+    iota(A("P", W, PW), [[0, PW - W]], 0, 0)
+    iota(A("D", NPOS, NPOS + Q), [[0, Q]], 0, 0)
+    for x in ("bL", "bR", "bN"):
+        iota(A(x), [[0, Q]], 0, 0)
+    kI = A("kI")
+    b0, b1 = A("bF", 0, 1), A("bF", 1, 2)
+    ts(A("b4", 0, 1), A("pI", 0, 1), 16, op.bitwise_and)
+    ts(b0, A("b4", 0, 1), 0, op.is_equal)
+    ts(b1, A("b4", 0, 1), 16, op.is_equal)
+    ts(A("S00"), A("mpI"), 0, op.is_equal, b0, op.mult)
+    ts(A("S11"), A("mpI"), 0, op.is_equal, b1, op.mult)
+    ts(A("S01"), A("mpI"), 16, op.is_equal, b0, op.mult)
+    ts(A("S10"), A("mpI"), -16, op.is_equal, b1, op.mult)
+
+    def turn(x, m, t, s, out):
+        n = x[4]
+        for j, b in ((0, b0), (1, b1)):
+            act(A(m + "%d" % j, 0, n), x, af.Copy, scale=b)
+            vtr(A(t + "%d" % j, 32, 32 + n), A(m + "%d" % j, 0, n))
+        mms(out, [(A(s + "00"), A(t + "0", 32, 32 + n)), (A(s + "11"), A(t + "1", 32, 32 + n)), (A(s + "01"), A(t + "1", 48, 48 + n)), (A(s + "10"), A(t + "0", 16, 16 + n))])
+
+    act(A("XL", 0, Q), A("inO"), af.Copy, scale=-16384.0, bias=15 * 16384.0)
+    act(A("XC", 0, Q), A("inB"), af.Copy, scale=262144.0)
+    act(A("OB", 0, Q), A("inB"), af.Copy, scale=2.0 - 262144.0, bias=2105344.0)
+    cp(A("X0", 0, Q), A("inL"))
+    turn(A("X0", 0, Q), "ML", "TL", "S", A("SWP", 0, Q))
+    ts(A("tB"), A("inC"), 0, op.max, 2, op.mult)
+    ts(A("tD"), A("inC"), 0, op.is_lt)
+    tt(A("tA"), A("XL", 0, Q), A("tB"), op.add)
+    tt(A("tC"), A("XC", 0, Q), A("tA"), op.add)
+    tt(A("tE"), A("OB", 0, Q), A("tD"), op.mult)
+    tt(A("X0", Q, 2 * Q), A("tC"), A("tE"), op.add)
+    turn(A("X0", Q, 2 * Q), "MV", "TV", "S", A("OB", 0, Q))
+    K13, K21 = A("VP1", 0, Q), A("VP1", Q, 2 * Q)
+    KC, TH = A("VP2", 0, Q), A("VP2", Q, 2 * Q)
+    TA, TB = A("VT", 0, Q), A("VT", Q, 2 * Q)
+    ts(K13, kI, -8192, op.mult, 4096 + 15 * 8192, op.add)
+    cp(A("oL0"), A("SWP", 0, Q))
+    act(A("E0", 0, Q), A("SWP", 0, Q), af.Copy)
+    cp(A("oV0", Q, 2 * Q), A("OB", 0, Q))
+    tt(A("oV0", 0, Q), A("E0", 0, Q), K13, op.add)
+    for x in ("00", "01", "10", "11"):
+        act(A("B" + x), A("S" + x), af.Copy)
+
+    def coff(t):
+        ts(A("sC"), A("oV%d" % (t % 2), Q, 2 * Q), 1, op.arith_shift_right, 8191, op.bitwise_and)
+        cp(A("oC%d" % (t % 2)), A("sC"))
+    coff(0)
+    ts(A("qI"), A("pI"), 15, op.bitwise_and)
+    tt(A("k1"), A("c16I"), A("qI"), op.add)
+    cp(A("YL"), A("k1"))
+
+    def chain(seq):
+        for x, y in zip(seq, seq[1:]):
+            y["soft"].append(x)
+
+    def yexp(p):
+        seq = [act(A("YE", 16 * a, 16 * b), A("AB%d" % p, NPOS, NPOS + Q), af.Copy, off=A("YL", a, b)) for a, b in LCH]
+        chain(seq)
+        seq[0]["bonus"] = BONUS
+    yexp(0)
+    ts(A("k9"), A("pI", 0, 144), 240, op.bitwise_and)
+    tt(A("k10"), A("nI"), A("k9"), op.subtract)
+    ts(A("Z1"), A("k10"), 15, op.is_equal)
+    for z, s in (("ZL", 2.0 ** 25), ("ZS", -16.0), ("ZC", 2.0 ** 26)):
+        act(A(z), A("Z1"), af.Copy, scale=s)
+    ts(A("EY"), A("mpI"), 0, op.is_equal)
+    act(A("NE"), A("EY"), af.Copy, scale=-1.0)
+    fill(A("ONE"), 1.0 / 128)
+    fill(A("CL"), 2.0 ** 25)
+    fill(A("CC"), -7.5 * 2.0 ** 26)
+    ts(A("MSK"), kI, 0, op.is_gt)
+    ts(K21, kI, -(1 << 21), op.mult, 15 * (1 << 21) - (1 << 24) + (1 << 13), op.add)
+    ts(KC, kI, -2, op.mult, 30 - (1 << 24) - (1 << 13), op.add)
+    act(A("RSTL"), A("MSK"), af.Copy, scale=2.0 ** 27, bias=-2.0 ** 20)
+    act(A("RSTC"), A("MSK"), af.Copy, scale=2.0 ** 28, bias=-2.0 ** 27)
+    cp(A("limF", 0, TV), A("inLim", 0, TV))
+    tt(A("k2"), kI, A("qI"), op.subtract)
+    ts(A("k3"), A("k2"), 0, op.is_equal)
+    ts(A("k4"), A("k2"), 1, op.is_equal)
+    tt(A("PM"), A("k3"), A("k4"), op.subtract)
+    ts(A("k5"), A("nI", 0, 128), 240, op.bitwise_and)
+    ts(A("k6"), A("pI", 0, 128), 240, op.bitwise_and)
+    tt(A("BO"), A("k5"), A("k6"), op.is_equal)
+    ts(A("k7"), A("mpI"), 15, op.bitwise_and)
+    ts(A("GW"), A("k7"), 0, op.is_equal, 2.0 ** 18, op.mult)
+    tt(A("k8"), A("c16I", 0, Q, 16), A("qI", 0, 12), op.add)
+    cp(A("cv"), A("k8"))
+    ts(A("cb", 0, 12), A("k8"), NPOS, op.add)
+    ts(A("cb", 12, 24), A("k8"), DUMP, op.add)
+    tt(A("tA", 0, 12), A("c256"), A("qI", 0, 12), op.add)
+    ts(A("tB", 0, 12), A("tA", 0, 12), 240, op.add)
+    tt(A("cp"), A("tB", 0, 12), A("cb", 0, 12), op.subtract)
+
+    def cnt(x, src, z, const, a, b):
+        mms(A(x, a, b), [(A("ONE"), A(const, a, b))] + [(A(z, 15 - q, 143 - q), A(src, a * 16 + q, b * 16, 16)) for q in range(16)])
+
+    def gather_l(t):
+        lst, ab = ("aL%d" if t else "oL%d") % t, "AB%d" % (t % 2)
+
+        def one(a, b):
+            off, ye, o = A(lst, a, b), A("YE", 16 * a, 16 * b), A("D", 16 * a, 16 * b)
+            me = emit("v", lambda q: q.tensor_tensor(o[3], T.P[:, :].indirect(off[3]), ye[3], op.subtract), [A("P"), off, ye], [o], 0.05 + 1.56 * CY * o[4])
+            act(A("SG", 16 * a, 16 * b), o, af.Sign, bias=-0.5)
+            act(A(ab, 16 * a, 16 * b), o, af.Abs)
+            cnt("XL", "SG", "ZL", "CL", a, b)
+            cnt("XS", ab, "ZS", "KT", a, b)
+            return me
+        return [one(a, b) for a, b in LCH]
+
+    def gather_c(t):
+        lst = ("aC%d" if t else "oC%d") % t
+
+        def one(a, b):
+            off, ye, o = A(lst, a, b), A("YE", 16 * a, 16 * b), A("IC", 16 * a, 16 * b)
+            me = emit("v", lambda q: q.tensor_tensor(o[3], T.P[:, :].indirect(off[3]), ye[3], op.is_gt), [A("P"), off, ye], [o], 0.05 + 1.56 * CY * o[4])
+            cnt("XC", "IC", "ZC", "CC", a, b)
+            return me
+        return [one(a, b) for a, b in CCH]
+
+    def gather_s(t):
+        lst = ("aC%d" if t else "oC%d") % t
+        for a, b in SCH:
+            act(A("CR", 16 * a, 16 * b), A("P"), af.Copy, off=A(lst, a, b))
+        for j, (a, b) in enumerate(SCH):
+            ps = A(("OB", "SWP")[j % 2], 0, 16 * (b - a))
+            mms(ps, [(A("EY"), A("CR", 16 * a, 16 * b)), (A("NE"), A("YE", 16 * a, 16 * b))])
+            act(A("IC", 16 * a, 16 * b), ps, af.Sign, bias=-0.5)
+        if SCH:
+            cnt("XC", "IC", "ZL", "CL", SCH[0][0], SCH[-1][1])
+
+    def usum(p):
+        mms(A("u"), [(A("Z1", 15 - q, 143 - q), A("AB%d" % p, NPOS + q, NPOS + Q, 16)) for q in range(16)])
+        act(LF(36), A("u"), af.Copy)
+        act(LF(37), A("u"), af.Copy)
+
+    def uint():
+        return cp(LI(2), LF(36))
+
+    def wcount(t):
+        d = "DL%d" % (t % 2)
+        return [cp(LI(21), A("w")), ts(LI(22), LI(21), 3 << 18, op.bitwise_and), tt(starts(d, 0), starts(d, 0), LI(22), op.add),
+                scan(TH, A("MSK"), A(d), 0.0, op.mult, op.add)]
+
+    def lims(t):
+        act(A("PM1_%d" % (t % 2)), A("PM"), af.Copy, scale=A("limF", t, t + 1))
+        mms(A("lm"), [(A("BO"), A("PM1_%d" % (t % 2)))])
+        act(A("DL%d" % (t % 2)), A("lm"), af.Copy, scale=2.0 ** 18)
+
+    def pnew(to, y):
+        return emit("v", lambda q: q.tensor_tensor(T.P[:, :].indirect(to[3]), T.md[:, :], y[3], op.add), [A("md"), y, to], [A("P")], 0.05 + 3.8 * CY * Q)
+
+    def starts(name, a=15):
+        return A(name, a, None, 16) if name not in PART else A(name, a, PART[name][2], 16)
+
+    lims(0)
+    usum(0)
+    for t in range(TV):
+        p = t % 2
+        AB, yv = A("AB%d" % p), A("AB%d" % p, NPOS, NPOS + Q)
+        nxt = t + 1
+        last = nxt == TV
+        pv = ("aV%d" if t else "oV%d") % t
+        Lp, V = A(pv, 0, Q), A(pv, Q, 2 * Q)
+        seq = gather_l(t)
+        wseq = wcount(t) if t else [scan(TH, A("MSK"), A("DL0"), 0.0, op.mult, op.add)]
+        seq += gather_c(t)
+        seq.append(uint())
+        wseq[0]["soft"].append(seq[0])
+        chain(seq)
+        gather_s(t)
+        tt(TA, V, TH, op.is_ge)
+        tt(A("y_"), TA, V, op.add)
+        ts(A("tS"), V, 15 << 18, op.bitwise_and, 9, op.arith_shift_right)
+        tt(A("KEYC"), A("y_"), K21, op.add)
+        tt(A("SLT"), A("tS"), KC, op.add)
+        tt(A("mkL"), A("XL", 0, Q), Lp, op.min)
+        scan(A("RS"), A("RSTL"), A("XS", 0, Q), -2.0 ** 20, op.min, op.max)
+        scan(A("RL"), A("RSTL"), A("mkL"), -2.0 ** 20, op.min, op.max)
+        RL, RC = starts("RL"), starts("RC")
+        act(LF(0), LF(36), af.Copy, scale=37.0, bias=float(t))
+        act(LF(1), RL, af.Copy, bias=97.0 * t)
+        act(LF(10), RL, af.Copy, scale=2.0, bias=-8192.0)
+        cp(LI(0, 2), A("RLS", 15, 384, 16))
+        ts(LI(3), LI(0), 4095, op.bitwise_and)
+        tt(LI(4, 2), LI(2, 2), LF(36, 2), op.mult)
+        ts(LI(6, 2), LI(4, 2), 5, op.arith_shift_right)
+        tt(LI(8, 2), LI(6, 2), LF(0, 2), op.add)
+        ts(LI(10), LI(8), 4095, op.bitwise_and)
+        ts(LI(11), LI(9), 3840, op.bitwise_and)
+        ts(LI(12), LI(1), 15, op.bitwise_and)
+        ts(LF(2), LI(12), 8192, op.mult, 4096, op.add)
+        tt(LF(3), LF(2), LI(10), op.add)
+        tt(LF(4), A("cv"), LI(3), op.subtract)
+        tt(LF(5), LI(11), LF(4), op.add)
+        tt(LF(6), LF(5), RL, op.add)
+        ts(LF(7), RL, 0, op.is_lt)
+        ts(LF(8), RL, 0, op.is_ge)
+        tt(LF(9), LF(7), LF(3), op.mult)
+        tt(LF(11), LF(6), LF(9), op.max)
+        ts(LI(13), LI(0), 9, op.arith_shift_right, 240, op.bitwise_and)
+        tt(LF(12), A("cp"), LI(13), op.subtract)
+        ts(LF(13), LI(11), -DUMP, op.add)
+        tt(TA, A("XC", 0, Q), A("KEYC"), op.min)
+        tt(A("mk"), TA, A("SLT"), op.max)
+        scan(A("RC"), A("RSTC"), A("mk"), -2.0 ** 27, op.min, op.max)
+        if not last:
+            lims(nxt)
+        cp(LI(16), RC)
+        ts(LF(14), RC, -2.0 ** 24, op.is_lt)
+        ts(LF(15), RC, -2.0 ** 24, op.is_ge)
+        ts(LI(17), LI(16), 1, op.bitwise_and)
+        ts(LI(18), LI(16), 0x3FFFE, op.bitwise_and, 1, op.arith_shift_right)
+        tt(LF(16), LF(14), LF(11), op.mult)
+        tt(LF(17), LI(17), LI(18), op.mult)
+        tt(starts("bL", 0), LF(16), LF(17), op.add)
+        scan(TA, A("MSK"), A("bL"), 0.0, op.mult, op.add)
+        tt(A("dif"), TA, Lp, op.subtract)
+        ts(TB, A("dif"), -4096, op.max, 4096, op.min)
+        tt(A("sL"), TB, Lp, op.add)
+        ts(A("sM"), A("sL"), 4095, op.bitwise_and)
+        if not last:
+            cp(A("oL%d" % (nxt % 2)), A("sM"))
+            send("L", nxt)
+        tt(LF(18), LF(14), LF(8), op.mult)
+        tt(LF(20), LF(12), LF(18), op.mult)
+        tt(LF(21), LF(13), LF(18), op.mult)
+        tt(LF(22, 2), LF(20, 2), A("cb"), op.add)
+        cp(A("LST"), LF(22, 2))
+        PL, NL = A("LST", 0, 12), A("LST", 12, 24)
+        act(A("AB%d" % (1 - p), NPOS, NPOS + Q), AB, af.Copy, off=PL)
+        act(A("nD"), A("D"), af.Relu, scale=-1.0, off=PL)
+        act(A("md"), A("nD"), af.Copy, scale=-1.0)
+        tt(LF(24), LF(15), LF(8), op.max)
+        tt(starts("bR", 0), LF(24), RC, op.mult)
+        ts(LI(19), LI(16), 0x1FDFFE, op.bitwise_and)
+        ts(LI(20), LI(16), 0x3C000, op.bitwise_and)
+        ts(LF(25), LI(19), 1 << 18, op.add)
+        ts(LF(26), LI(20), (1 << 21) + (1 << 13), op.add)
+        tt(LF(27), LF(26), LI(17), op.mult)
+        tt(LF(28), LF(25), LF(27), op.max)
+        tt(LF(29), LF(10), LF(14), op.mult)
+        tt(LF(30), LF(28), LF(15), op.mult)
+        tt(starts("bN", 0), LF(29), LF(30), op.add)
+        scan(TA, A("MSK"), A("bR"), 0.0, op.mult, op.add)
+        tt(A("hot"), A("mk"), TA, op.is_equal)
+        scan(TB, A("MSK"), A("bN"), 0.0, op.mult, op.add)
+        tt(A("dif"), TB, V, op.subtract)
+        tt(TA, A("hot"), A("dif"), op.mult)
+        on = "oV%d" % (nxt % 2)
+        tt(A(on, Q, 2 * Q), TA, V, op.add)
+
+        pnew(NL, yv)["bonus"] = BONUS if last else 0.0
+        if last:
+            break
+        coff(nxt)
+        send("C", nxt)
+        tt(A(on, 0, Q), A("sM"), K13, op.add)
+        send("V", nxt)
+        yexp(1 - p)
+        cp(A("Bf"), LF(15))
+        mms(A("w"), [(A("GW"), A("Bf"))])
+        usum(1 - p)
+
+    dma("y", T.zp[:, :], T.P[:, 0:W], [A("P", 0, W)], [], 6.0)
+    pe = TV % 2
+    dma("y", T.zy[:, :], T["AB%d" % pe][:, NPOS:NPOS + Q], [A("AB%d" % pe, NPOS, NPOS + Q)], [], 2.0)
+    VN = A("oV%d" % pe, Q, 2 * Q)
+    cp(A("X0", 0, Q), A("sM"))
+    turn(A("X0", 0, Q), "ML", "TL", "S", A("SWP", 0, Q))
+    act(A("E0", 0, Q), A("SWP", 0, Q), af.Copy)
+    dma("y", T.zl[:, :], T.E0[:, 0:Q], [A("E0", 0, Q)], [], 2.0)
+    ts(A("tF"), VN, 1, op.arith_shift_right, 8191, op.bitwise_and)
+    ts(A("tA"), A("tF"), 4096, op.is_lt)
+    ts(TB, A("tF"), 1, op.add)
+    tt(A("tC"), A("tA"), TB, op.mult)
+    ts(A("X0", Q, 2 * Q), A("tC"), -1, op.add)
+    turn(A("X0", Q, 2 * Q), "MV", "TV", "S", A("OB", 0, Q))
+    ts(A("sL"), VN, 14, op.arith_shift_right, 15, op.bitwise_and)
+    ts(A("X1", 0, Q), A("sL"), -1, op.mult, 15, op.add)
+    ts(A("sC"), VN, 18, op.arith_shift_right, 7, op.bitwise_and)
+    ts(TB, A("tF"), -4096, op.add, 0, op.max)
+    tt(A("X1", Q, 2 * Q), A("sC"), TB, op.add)
+    act(A("E0", Q, 2 * Q), A("OB", 0, Q), af.Copy)
+    dma("y", T.zc[:, :], T.E0[:, Q:2 * Q], [A("E0", Q, 2 * Q)], [], 2.0)
+    turn(A("X1"), "MO", "TO", "B", A("SWP", 0, 384))
+    act(A("oB"), A("SWP", 0, 384), af.Copy)
+    dma("y", T.zo[:, :], T.oB[:, 0:Q], [A("oB", 0, Q)], [], 2.0)
+    dma("y", T.zb[:, :], T.oB[:, Q:2 * Q], [A("oB", Q, 2 * Q)], [], 2.0)
+
+    succ = [[] for _ in ops]
+    for o in ops:
+        o["need"] = list({x["i"]: x for x in o["need"]}.values())
+        o["all"] = list({x["i"]: x for x in o["need"] + o["soft"]}.values())
+        for x in o["all"]:
+            succ[x["i"]].append(o)
+    for o in reversed(ops):
+        o["pri"] = o["bonus"] + o["cost"] + o["lat"] + max([0.0] + [s["pri"] + WK for s in succ[o["i"]]])
+    left = {o["i"]: len(o["all"]) for o in ops}
+    free = {e: 0.0 for e in list(queues) + ["net"]}
+    ready = {e: [] for e in free}
+    for o in ops:
+        if not left[o["i"]]:
+            ready[o["e"]].append((0.0, o))
+    done = []
+    while len(done) < len(ops):
+        best = None
+        for e in ready:
+            for (r, o) in ready[e]:
+                k = (max(r, free[e] if e != "net" else 0.0), -o["pri"], o["i"])
+                if best is None or k < best[0]:
+                    best = (k, e, r, o)
+        k, e, r, o = best
+        ready[e].remove((r, o))
+        o["st"] = k[0]
+        o["fin"] = k[0] + o["cost"] + o["lat"]
+        free[e] = k[0] + o["cost"]
+        done.append(o)
+        for s in succ[o["i"]]:
+            left[s["i"]] -= 1
+            if not left[s["i"]]:
+                ready[s["e"]].append((max([x["fin"] + WK for x in s["need"]] + [x["fin"] for x in s["soft"]]), s))
+    count = {}
+    clock = {e: {} for e in queues}
+    for o in done:
+        e = o["e"]
+        if e == "net":
+            o["c"] = {}
+            continue
+        want = {}
+        for x in o["need"]:
+            if x["v"] > want.get(x["sem"], (0, None))[0]:
+                want[x["sem"]] = (x["v"], x)
+        ck = clock[e]
+        for s in sorted(want, key=lambda s: -len(want[s][1]["c"])):
+            v, x = want[s]
+            if ck.get(s, 0) >= v:
+                continue
+            queues[e].wait_ge(T.sem[s], v)
+            for k, y in x["c"].items():
+                ck[k] = max(ck.get(k, 0), y)
+            ck[s] = v
+        ins = o["fn"](queues[e])
+        if o["inc"] > 0:
+            ins.then_inc(T.sem[o["sem"]], o["inc"])
+        count[o["sem"]] = count.get(o["sem"], 0) + abs(o["inc"])
+        o["v"] = count[o["sem"]]
+        o["c"] = dict(ck)
+    for s in sorted(count):
+        if clock["g"].get(s, 0) < count[s]:
+            g.wait_ge(T.sem[s], count[s])

@@ -1,52 +1,63 @@
+import numpy as np
+from concourse.bass import DstId, RemoteDMATransfer
 from concourse.mybir import AluOpType, ActivationFunctionType
 
 N, W, Q, TV, HOP = 8, 4096, 192, 6, 3
 NPOS = 16 * Q
+HALF = NPOS // 2
 PW = 4608
 DUMP = 4352
-LCH = [(0, 64), (64, 128), (128, 192)]
-CCH = [(0, 64), (64, 128)]
-SCH = [(128, 160), (160, 192)]
+R17 = 12 * 17
+LCH = [(0, 0, 6), (1, 0, 6), (0, 6, 12), (1, 6, 12)]
+LSC = []
+VSG = []
+LSUM = [(0, 6), (6, 12)]
+CCH = [(0, 0, 12), (1, 0, 4)]
+SCH = [(1, 4, 8), (1, 8, 12)]
+CSUM = [(0, 0, 12), (1, 0, 12)]
+YCH = [(0, 6), (6, 12)]
+BIG = 2.0 ** 33
+OFF = 2.0 ** 24
+HOT = 31 * 4096
 
 F32, BF, I32, U16 = "float32", "bfloat16", "int32", "uint16"
 SCRATCH = {}
 for _n, _w, _d in (
-        ("P", PW, BF), ("D", NPOS + Q, BF), ("AB0", NPOS + Q, BF), ("AB1", NPOS + Q, BF), ("SG", NPOS, BF), ("IC", NPOS, BF),
-        ("YE", NPOS, BF), ("CR", NPOS, BF), ("YL", Q, U16),
+        ("P", PW, BF), ("D", NPOS, BF), ("AB", [12, 256], BF), ("SG", [12, 256], BF), ("IC", NPOS, BF), ("y0", Q, BF), ("y1", Q, BF),
+        ("YE", HALF, BF), ("CR", NPOS, BF), ("LR", NPOS, BF), ("YL", 96, U16), ("GL", 4, U16), ("BL", 4, U16), ("EL", 14, U16),
         ("inL", Q, I32), ("inC", Q, I32), ("inO", Q, BF), ("inB", Q, BF), ("inLim", 8, I32), ("limF", 8, F32),
-        ("MSK", Q, F32), ("RSTL", Q, F32), ("RSTC", Q, F32), ("KT", Q, BF), ("CL", Q, BF), ("CC", Q, BF), ("ONE", 128, BF),
+        ("CL", [12, 16], BF), ("CC", Q, BF), ("ONE", 128, BF),
         ("Z1", 144, BF), ("ZL", 144, BF), ("ZC", 144, BF), ("ZS", 144, BF), ("GW", 128, BF), ("BO", 128, BF), ("EY", 128, BF), ("NE", 128, BF),
-        ("PM", Q, BF), ("S00", 128, F32), ("S01", 128, F32), ("S10", 128, F32), ("S11", 128, F32),
-        ("pI", Q, I32), ("qI", Q, I32), ("kI", Q, I32), ("nI", 144, I32), ("mpI", 128, I32), ("c16I", Q, I32),
-        ("b4", 8, I32), ("bF", 8, F32), ("cF", 48, F32), ("c256", 12, I32),
-        ("X0", 384, F32), ("X1", 384, BF), ("ML0", Q, F32), ("ML1", Q, F32), ("MV0", Q, F32), ("MV1", Q, F32), ("MO0", 384, BF), ("MO1", 384, BF),
-        ("TL0", 256, F32), ("TL1", 256, F32), ("TV0", 256, F32), ("TV1", 256, F32), ("TO0", 448, BF), ("TO1", 448, BF), ("E0", 384, F32), ("oB", 384, BF),
-        ("B00", 128, BF), ("B01", 128, BF), ("B10", 128, BF), ("B11", 128, BF), ("KX", 1072, I32), ("TX", 7 * Q, F32), ("tF", Q, I32),
-        ("y_", Q, F32), ("KEYC", Q, F32), ("SLT", Q, F32), ("tS", Q, I32), ("mkL", Q, F32), ("mk", Q, F32), ("hot", Q, F32),
-        ("RLS", 384, F32), ("RC", Q, F32), ("bL", Q, F32), ("bR", Q, F32), ("bN", Q, F32),
-        ("dif", Q, F32), ("sL", Q, I32), ("sM", Q, I32), ("sC", Q, I32), ("LI", 312, I32), ("LF", 480, F32), ("Bf", 12, BF), ("LST", 24, U16),
-        ("md", Q, BF), ("nD", Q, BF)):
-    SCRATCH[_n] = ("sbuf", [128, _w], _d)
-for _n in ("XL", "XS", "XC", "VP1", "VP2", "VT", "OB", "SWP"):
+        ("PM", 24, BF), ("PM1", 144, BF), ("CT", 144, F32), ("LT", 144, F32),
+        ("S00", 128, F32), ("S01", 128, F32), ("S10", 128, F32), ("S11", 128, F32),
+        ("B00", 128, BF), ("B01", 128, BF), ("B10", 128, BF), ("B11", 128, BF),
+        ("mpI", 128, I32), ("gI", 128, I32), ("yI", 96, I32), ("sI", 96, I32), ("KX", 256, I32), ("kI", 128, I32), ("kF", 128, F32),
+        ("cv", 12, F32), ("cD", 24, F32), ("cE", 24, F32), ("X0", 384, F32), ("X1", 384, BF), ("E0", 384, F32), ("oB", 384, BF), ("TX", 5 * Q, F32), ("tF", Q, I32),
+        ("TL", [12, 16], F32), ("TV", [12, 16], F32), ("TO", [24, 16], BF),
+        ("DS", Q, F32), ("mkL", Q, F32), ("mk", R17, F32), ("RLS", 3 * Q, F32), ("RC", R17, F32),
+        ("tS", Q, I32), ("SLT", [12, 17], F32), ("dif", R17, F32), ("sL", [12, 17], I32), ("sC", [12, 16], I32),
+        ("M", 64 * 17, F32), ("Dd", 36 * 17, F32), ("GF", 48, F32),
+        ("LI", 300, I32), ("LF", 144, F32), ("uF", 24, F32), ("Bf", 12, BF), ("LST", 24, U16), ("pa", Q, BF), ("md", Q, BF), ("nD", Q, BF)):
+    SCRATCH[_n] = ("sbuf", [128] + (_w if isinstance(_w, list) else [_w]), _d)
+for _n in ("XL", "XS", "VT", "MS"):
     SCRATCH[_n] = ("psum", [128, 512], F32)
+SCRATCH["XC"] = ("psum", [128, 16, 32], F32)
+for _n in ("S1", "S2", "S3"):
+    SCRATCH[_n] = ("psum", [128, 32, 16], F32)
 for _t in range(TV):
-    SCRATCH["PM1_%d" % (_t % 2)] = ("sbuf", [128, Q], BF)
-    SCRATCH["DL%d" % (_t % 2)] = ("sbuf", [128, Q], F32)
-    SCRATCH["oL%d" % (_t % 2)] = ("sbuf", [128, Q], U16)
-    SCRATCH["oC%d" % (_t % 2)] = ("sbuf", [128, Q], U16)
-    SCRATCH["oV%d" % (_t % 2)] = ("sbuf", [128, 2 * Q], I32)
+    SCRATCH["DC%d" % _t] = ("sbuf", [128, 208], F32)
+    for _k in "LC":
+        SCRATCH["o%s%d" % (_k, _t % 2)] = ("sbuf", [128, Q], U16)
+    for _k in "SVB":
+        SCRATCH["o%s%d" % (_k, _t % 2)] = ("sbuf", [128, 12, 17], I32)
     if _t:
-        SCRATCH["aL%d" % _t] = ("sbuf", [128, Q], U16)
-        SCRATCH["aC%d" % _t] = ("sbuf", [128, Q], U16)
-        SCRATCH["aV%d" % _t] = ("sbuf", [128, 2 * Q], I32)
+        for _k in "LC":
+            SCRATCH["a%s%d" % (_k, _t)] = ("sbuf", [128, Q], U16)
+        for _k in "SV":
+            SCRATCH["a%s%d" % (_k, _t)] = ("sbuf", [128, 12, 17], I32)
 SEMAPHORES = ["sv", "ss", "st", "sg"] + [k + i for k in ("lL", "lC", "lV") for i in "01"] + ["d%d" % i for i in range(16)] + [k + "%d" % t for k in ("qL", "qC", "qV") for t in range(1, TV)]
-PART = {"cv": ("cF", 0, 12), "cp": ("cF", 12, 12), "cb": ("cF", 24, 24),
-        "k1": ("KX", 0, Q), "k2": ("KX", Q, Q), "k5": ("KX", 384, 128), "k6": ("KX", 512, 128), "k7": ("KX", 640, 128), "k8": ("KX", 768, 12),
-        "k9": ("KX", 784, 144), "k10": ("KX", 928, 144), "tA": ("TX", 0, Q), "tB": ("TX", Q, Q), "tC": ("TX", 2 * Q, Q), "tD": ("TX", 3 * Q, Q),
-        "tE": ("TX", 4 * Q, Q), "k3": ("TX", 5 * Q, Q), "k4": ("TX", 6 * Q, Q),
-        "u": ("XC", 192, 12), "w": ("XC", 208, 12), "lm": ("XC", 224, 192), "RL": ("RLS", 0, 192), "RS": ("RLS", 192, 192)}
 BONUS = 4.0
-CY, FX, WK = 0.00092, 0.03, 0.08
+CY, PE, FX, WK = 0.00092, 0.00062, 0.03, 0.08
 
 
 def rank_program(g, core, T, topo):
@@ -56,57 +67,64 @@ def rank_program(g, core, T, topo):
     dst = T.cores[(rank + HOP) % N]
     rid, pid = topo.addr(dst)[:2]
     emask = topo.mask(core, dst)
-    neng = len(topo.engines(core, dst))
+    eng = topo.engines(core, dst)
+    neng = len(eng)
+    halves = [sum(1 << e for e in eng[:neng // 2]), sum(1 << e for e in eng[neng // 2:])]
     op = AluOpType
     af = ActivationFunctionType
     queues = {"v": g.vector, "s": g.scalar, "t": g.tensor, "g": g, "y": g.sync}
     semof = {"v": "sv", "s": "ss", "t": "st", "g": "sg"}
     ops, wr, rd = [], {}, {}
     psum = {k for k in SCRATCH if SCRATCH[k][0] == "psum"}
+    sl = slice
 
-    def A(name, lo=0, hi=None, st=1):
-        if name in PART:
-            name, base, n = PART[name]
-            lo, hi = base + lo, base + (n if hi is None else hi)
-        hi = SCRATCH[name][1][1] if hi is None else hi
-        return (name, lo, hi, T[name][:, lo:hi] if st == 1 else T[name][:, lo:hi:st], len(range(lo, hi, st)))
+    def A(name, *ix):
+        shape = SCRATCH[name][1][1:]
+        if len(shape) == 1:
+            ix = (sl(*ix),) if len(ix) > 1 else (sl(None),)
+        else:
+            ix = tuple(sl(*x) if isinstance(x, tuple) else x for x in ix) + (sl(None),) * (2 - len(ix))
+        at = np.arange(int(np.prod(shape))).reshape(shape)[ix].reshape(-1)
+        return (name, int(at.min()), int(at.max()) + 1, T[name][(sl(None),) + ix], len(at), frozenset(at.tolist()))
 
-    def emit(e, fn, R, Wt, cost, sem=None, inc=1, lat=0.0, deps=()):
-        need = list(deps)
+    def meet(x, y, e):
+        if y[1]["e"] == e:
+            return x[1] < y[0][2] and y[0][1] < x[2] and not x[5].isdisjoint(y[0][5])
+        return x[0] in psum or (x[1] < y[0][2] and y[0][1] < x[2])
+
+    def emit(e, fn, R, Wt, cost, sem=None, inc=1, lat=0.0):
+        need = []
         for x in R:
-            for (l, h, o) in wr.get(x[0], []):
-                if (l < x[2] and x[1] < h) or (x[0] in psum and o["e"] != e):
-                    need.append(o)
+            need += [y[1] for y in wr.get(x[0], []) if meet(x, y, e)]
             if x[0] in psum:
-                need += [o for (l, h, o) in rd.get(x[0], []) if o["e"] != e]
+                need += [y[1] for y in rd.get(x[0], []) if y[1]["e"] != e]
         for x in Wt:
-            for (l, h, o) in wr.get(x[0], []) + rd.get(x[0], []):
-                if (l < x[2] and x[1] < h) or (x[0] in psum and o["e"] != e):
-                    need.append(o)
+            need += [y[1] for y in wr.get(x[0], []) + rd.get(x[0], []) if meet(x, y, e)]
         me = {"e": e, "fn": fn, "need": need, "cost": cost, "sem": sem or semof.get(e), "inc": inc, "lat": lat, "i": len(ops), "soft": [], "bonus": 0.0}
         ops.append(me)
-        for x in R:
-            rd.setdefault(x[0], []).append((x[1], x[2], me))
         for x in Wt:
-            nm, lo, hi = x[:3]
-            wr[nm] = [y for y in wr.get(nm, []) if not (lo <= y[0] and y[1] <= hi)] + [(lo, hi, me)]
-            rd[nm] = [y for y in rd.get(nm, []) if not (lo <= y[0] and y[1] <= hi) or y[2] is me]
+            wr[x[0]] = [y for y in wr.get(x[0], []) if not y[0][5] <= x[5]] + [(x, me)]
+            rd[x[0]] = [y for y in rd.get(x[0], []) if not y[0][5] <= x[5]]
+        for x in R:
+            rd.setdefault(x[0], []).append((x, me))
         return me
-
-    def two(x):
-        return SCRATCH[x[0]][2] in (BF, U16)
 
     def vc(o, ins):
         n = max([x[4] for x in [o] + ins])
-        return FX + CY * max(64, n * (0.5 if all(two(x) for x in [o] + ins) else 1))
+        return FX + CY * max(64, n * (0.5 if all(SCRATCH[x[0]][2] in (BF, U16) for x in [o] + ins) else 1))
 
-    def ts(o, i, s1, op0, s2=None, op1=None):
+    def ts(o, i, s1, op0, s2=None, op1=None, off=None):
+        R = [i] + [s for s in (s1, s2, off) if isinstance(s, tuple)]
+        a1, a2 = [s[3] if isinstance(s, tuple) else s for s in (s1, s2)]
+        src = i[3].indirect(off[3]) if off else i[3]
+        cost = 0.05 + 1.56 * CY * o[4] if off else vc(o, [i])
         if op1 is None:
-            return emit("v", lambda q: q.tensor_scalar(o[3], i[3], s1, None, op0), [i], [o], vc(o, [i]))
-        sc = s2[3] if isinstance(s2, tuple) else s2
-        return emit("v", lambda q: q.tensor_scalar(o[3], i[3], s1, sc, op0, op1), [i] + ([s2] if isinstance(s2, tuple) else []), [o], vc(o, [i]))
+            return emit("v", lambda q: q.tensor_scalar(o[3], src, a1, None, op0), R, [o], cost)
+        return emit("v", lambda q: q.tensor_scalar(o[3], src, a1, a2, op0, op1), R, [o], cost)
 
-    def tt(o, a, b, o_):
+    def tt(o, a, b, o_, off=None):
+        if off:
+            return emit("v", lambda q: q.tensor_tensor(o[3], a[3].indirect(off[3]), b[3], o_), [a, b, off], [o], 0.05 + 1.56 * CY * o[4])
         k = 1 if a[0] in psum or b[0] in psum else 2
         return emit("v", lambda q: q.tensor_tensor(o[3], a[3], b[3], o_), [a, b], [o], FX + CY * max(64, k * o[4]))
 
@@ -116,8 +134,8 @@ def rank_program(g, core, T, topo):
     def fill(o, c):
         return emit("v", lambda q: q.memset(o[3], c), [], [o], vc(o, []))
 
-    def scan(o, d0, d1, init, p0, p1):
-        return emit("v", lambda q: q.tensor_tensor_scan(o[3], d0[3], d1[3], init, p0, p1), [d0, d1], [o], vc(o, [d0, d1]))
+    def scan(o, d0, d1, p0, p1):
+        return emit("v", lambda q: q.tensor_tensor_scan(o[3], d0[3], d1[3], 0.0, p0, p1), [d0, d1], [o], vc(o, [d0, d1]))
 
     def vtr(o, i):
         return emit("v", lambda q: q.transpose(o[3], i[3]), [i], [o], vc(o, [i]))
@@ -129,23 +147,24 @@ def rank_program(g, core, T, topo):
         return emit("s", lambda q: q.activation(o[3], src, f, bias=bias, scale=sc), [i] + ([off] if off else []) + extra, [o],
                     (0.065 + 1.56 * CY * o[4]) if off else FX + CY * max(64, o[4]))
 
-    def pool(o, fn):
-        return emit("g", fn, [], [o], 0.13 + 2 * CY * o[4])
-
-    def iota(o, pattern, base, cm):
+    def iota(o, pattern, base, cm=0):
+        cost = 0.13 + 2 * CY * o[4]
         if SCRATCH[o[0]][2] == I32:
-            return pool(o, lambda q: q.iota(o[3], pattern, base, cm))
-        return pool(o, lambda q: q.iota(o[3], pattern, base, cm, allow_small_or_imprecise_dtypes=True))
+            return emit("g", lambda q: q.iota(o[3], pattern, base, cm), [], [o], cost)
+        return emit("g", lambda q: q.iota(o[3], pattern, base, cm, allow_small_or_imprecise_dtypes=True), [], [o], cost)
 
-    def mms(o, terms):
+    def const(o, c):
+        return iota(o, [[0, o[4]]], c)
+
+    def mms(o, terms, first=True, last=True):
         R = [x for t in terms for x in t]
 
         def go(q):
             for j, (l, r) in enumerate(terms):
-                ins = q.matmul(o[3], l[3], r[3], j == 0, j == len(terms) - 1)
+                ins = q.matmul(o[3], l[3], r[3], first and j == 0, last and j == len(terms) - 1)
             return ins
         k = 4 if SCRATCH[terms[0][0][0]][2] == F32 else 1
-        return emit("t", go, R, [o], FX + 0.00078 * k * max(64, o[4]) * len(terms))
+        return emit("t", go, R, [o], FX + PE * k * max(64, o[4]) * len(terms))
 
     nd = [0]
 
@@ -154,329 +173,332 @@ def rank_program(g, core, T, topo):
         nd[0] += 1
         return emit(e, lambda q: q.dma_start(o, i), R, Wt, 0.05, sem=s, inc=16, lat=lat)
 
+    def chain(seq):
+        for x, y in zip(seq, seq[1:]):
+            y["soft"].append(x)
+
     def LI(j, n=1):
         return A("LI", 12 * j, 12 * (j + n))
 
     def LF(j, n=1):
         return A("LF", 12 * j, 12 * (j + n))
 
-    def send(k, nxt):
-        o, i = "a%s%d" % (k, nxt), "o%s%d" % (k, nxt % 2)
-        sl = "l%s%d" % (k, nxt % 2)
-        wid = SCRATCH[o][1][1]
-        lat = 1.6 + 128 * wid * (2 if k != "V" else 4) / 60e3
-        me = emit("g", lambda q: q.remote_dma(out_ap=T[o][:, :], in_ap=T[i][:, :], remote_sem=T.sem["q%s%d" % (k, nxt)], local_sem=T.sem[sl],
-                                              pid=pid, routing_id=rid, dma_engine_mask=emask), [A(i)], [], 0.6, sem=sl, inc=-neng, lat=lat)
-        net = {"e": "net", "need": [me], "cost": lat, "sem": "q%s%d" % (k, nxt), "v": neng, "inc": 0, "lat": 0.0, "i": len(ops), "soft": [], "bonus": 0.0}
+    def landed(me, k, nxt, names, lat):
+        net = {"e": "net", "need": [me], "cost": 0.0, "sem": "q%s%d" % (k, nxt), "v": neng, "inc": 0, "lat": 0.0, "i": len(ops), "soft": [], "bonus": 0.0}
         ops.append(net)
-        wr[o] = [(0, wid, net)]
+        for o in names:
+            wr[o] = [(A(o), net)]
 
-    dma("y", T.inC[:, :], T.con[:, :], [], [A("inC")], 2.0)
-    dma("y", T.inO[:, :], T.org[:, :], [], [A("inO")], 2.0)
-    dma("s", T.inB[:, :], T.cnt[:, :], [], [A("inB")], 2.0)
-    dma("y", T.inL[:, :], T.lem[:, :], [], [A("inL")], 2.2)
-    dma("s", T.AB0[:, NPOS:NPOS + Q], T.ex[:, :], [], [A("AB0", NPOS, NPOS + Q)], 2.2)
-    dma("y", T.inLim[:, 0:TV], T.lim[:, :], [], [A("inLim", 0, TV)], 2.2)
-    dma("y", T.P[:, 0:W], T.prop[:, :], [], [A("P", 0, W)], 6.0)
+    def send_list(k, nxt):
+        o, i, s = "a%s%d" % (k, nxt), A("o%s%d" % (k, nxt % 2)), "l%s%d" % (k, nxt % 2)
+        me = emit("g", lambda q: q.remote_dma(out_ap=A(o)[3], in_ap=i[3], remote_sem=T.sem["q%s%d" % (k, nxt)], local_sem=T.sem[s],
+                                              pid=pid, routing_id=rid, dma_engine_mask=emask), [i], [], 0.6, sem=s, inc=-neng, lat=2.4)
+        landed(me, k, nxt, [o], 2.4)
+        return me
 
+    def send_rows(nxt):
+        p = nxt % 2
+        oS, oV, oB = A("oS%d" % p), A("oV%d" % p), A("oB%d" % p)
+        to, sem = [DstId(rid=rid, pnc=pid)], T.sem["qV%d" % nxt]
+        tr = [RemoteDMATransfer(dst_ids=to, dma_engine_mask=halves[0], remote_sem=sem, src=oS[3], dst=A("aS%d" % nxt)[3]),
+              RemoteDMATransfer(dst_ids=to, dma_engine_mask=halves[1], remote_sem=sem, srcs=[oV[3], oB[3]], dsts=[A("aV%d" % nxt)[3]], alu_op=1)]
+        me = emit("g", lambda q: q.remote_dma_fused(tr, local_sem=T.sem["lV%d" % p]), [oS, oV, oB], [], 0.6, sem="lV%d" % p, inc=-neng, lat=4.0)
+        landed(me, "V", nxt, ["aS%d" % nxt, "aV%d" % nxt], 4.0)
+        return me
+
+    chain([dma("y", T.inL[:, :], T.lem[:, :], [], [A("inL")], 2.2),
+           dma("y", T.inC[:, :], T.con[:, :], [], [A("inC")], 2.2),
+           dma("y", T.P[:, 0:W], T.prop[:, :], [], [A("P", 0, W)], 6.0),
+           dma("y", T.inLim[:, 0:TV], T.lim[:, :], [], [A("inLim", 0, TV)], 2.2)])
+    chain([dma("s", T.y0[:, :], T.ex[:, :], [], [A("y0")], 2.2),
+           dma("s", T.inO[:, :], T.org[:, :], [], [A("inO")], 2.2),
+           dma("s", T.inB[:, :], T.cnt[:, :], [], [A("inB")], 2.2)])
+
+    def kI(a, n=1):
+        return A("kI", a, a + n)
+
+    def kF(a, n=1):
+        return A("kF", a, a + n)
+
+    def rows(x):
+        return A(x, (0, 12), (0, 16))
     iota(A("mpI"), [[1, 128]], 0, -1)
-    iota(A("pI"), [[0, Q]], 0, 1)
-    iota(A("kI"), [[0, 12], [1, 16]], 0, 0)
-    iota(A("nI"), [[1, 144]], 0, 0)
-    iota(A("c16I"), [[16, 12], [0, 16]], 0, 0)
-    iota(A("c256"), [[256, 12]], 0, 0)
-    iota(A("KT"), [[0, 12], [-1, 16]], 15, 0)
-    for x in ("TL0", "TL1", "TV0", "TV1", "TO0", "TO1"):
-        n = SCRATCH[x][1][1]
-        iota(A(x, 0, 32), [[0, 32]], 0, 0)
-        iota(A(x, n - 32, n), [[0, 32]], 0, 0)
-    iota(A("P", W, PW), [[0, PW - W]], 0, 0)
-    iota(A("D", NPOS, NPOS + Q), [[0, Q]], 0, 0)
-    for x in ("bL", "bR", "bN"):
-        iota(A(x), [[0, Q]], 0, 0)
-    kI = A("kI")
-    b0, b1 = A("bF", 0, 1), A("bF", 1, 2)
-    ts(A("b4", 0, 1), A("pI", 0, 1), 16, op.bitwise_and)
-    ts(b0, A("b4", 0, 1), 0, op.is_equal)
-    ts(b1, A("b4", 0, 1), 16, op.is_equal)
+    iota(A("sI", 0, 1), [[0, 1]], 0, 1)
+    iota(A("yI"), [[16, 12], [0, 8]], 0)
+    iota(A("sI", 16, 25), [[-16, 9]], 0, 1)
+    iota(A("sI", 32, 46), [[16, 14]], 0)
+    iota(A("sI", 48, 72), [[1, 24]], 0)
+    iota(A("gI"), [[16, 8], [0, 16]], 15, -1)
+    b0, b1, qF = kF(0), kF(1), kF(2)
+    ts(kI(0), A("sI", 0, 1), 16, op.bitwise_and)
+    ts(kI(1), A("sI", 0, 1), 15, op.bitwise_and)
+    ts(b0, kI(0), 0, op.is_equal)
+    ts(b1, kI(0), 16, op.is_equal)
+    cp(qF, kI(1))
     ts(A("S00"), A("mpI"), 0, op.is_equal, b0, op.mult)
     ts(A("S11"), A("mpI"), 0, op.is_equal, b1, op.mult)
     ts(A("S01"), A("mpI"), 16, op.is_equal, b0, op.mult)
     ts(A("S10"), A("mpI"), -16, op.is_equal, b1, op.mult)
-
-    def turn(x, m, t, s, out):
-        n = x[4]
-        for j, b in ((0, b0), (1, b1)):
-            act(A(m + "%d" % j, 0, n), x, af.Copy, scale=b)
-            vtr(A(t + "%d" % j, 32, 32 + n), A(m + "%d" % j, 0, n))
-        mms(out, [(A(s + "00"), A(t + "0", 32, 32 + n)), (A(s + "11"), A(t + "1", 32, 32 + n)), (A(s + "01"), A(t + "1", 48, 48 + n)), (A(s + "10"), A(t + "0", 16, 16 + n))])
-
-    act(A("XL", 0, Q), A("inO"), af.Copy, scale=-16384.0, bias=15 * 16384.0)
-    act(A("XC", 0, Q), A("inB"), af.Copy, scale=262144.0)
-    act(A("OB", 0, Q), A("inB"), af.Copy, scale=2.0 - 262144.0, bias=2105344.0)
-    cp(A("X0", 0, Q), A("inL"))
-    turn(A("X0", 0, Q), "ML", "TL", "S", A("SWP", 0, Q))
-    ts(A("tB"), A("inC"), 0, op.max, 2, op.mult)
-    ts(A("tD"), A("inC"), 0, op.is_lt)
-    tt(A("tA"), A("XL", 0, Q), A("tB"), op.add)
-    tt(A("tC"), A("XC", 0, Q), A("tA"), op.add)
-    tt(A("tE"), A("OB", 0, Q), A("tD"), op.mult)
-    tt(A("X0", Q, 2 * Q), A("tC"), A("tE"), op.add)
-    turn(A("X0", Q, 2 * Q), "MV", "TV", "S", A("OB", 0, Q))
-    K13, K21 = A("VP1", 0, Q), A("VP1", Q, 2 * Q)
-    KC, TH = A("VP2", 0, Q), A("VP2", Q, 2 * Q)
-    TA, TB = A("VT", 0, Q), A("VT", Q, 2 * Q)
-    ts(K13, kI, -8192, op.mult, 4096 + 15 * 8192, op.add)
-    cp(A("oL0"), A("SWP", 0, Q))
-    act(A("E0", 0, Q), A("SWP", 0, Q), af.Copy)
-    cp(A("oV0", Q, 2 * Q), A("OB", 0, Q))
-    tt(A("oV0", 0, Q), A("E0", 0, Q), K13, op.add)
-    for x in ("00", "01", "10", "11"):
-        act(A("B" + x), A("S" + x), af.Copy)
-
-    def coff(t):
-        ts(A("sC"), A("oV%d" % (t % 2), Q, 2 * Q), 1, op.arith_shift_right, 8191, op.bitwise_and)
-        cp(A("oC%d" % (t % 2)), A("sC"))
-    coff(0)
-    ts(A("qI"), A("pI"), 15, op.bitwise_and)
-    tt(A("k1"), A("c16I"), A("qI"), op.add)
-    cp(A("YL"), A("k1"))
-
-    def chain(seq):
-        for x, y in zip(seq, seq[1:]):
-            y["soft"].append(x)
-
-    def yexp(p):
-        seq = [act(A("YE", 16 * a, 16 * b), A("AB%d" % p, NPOS, NPOS + Q), af.Copy, off=A("YL", a, b)) for a, b in LCH]
-        chain(seq)
-        seq[0]["bonus"] = BONUS
-    yexp(0)
-    ts(A("k9"), A("pI", 0, 144), 240, op.bitwise_and)
-    tt(A("k10"), A("nI"), A("k9"), op.subtract)
-    ts(A("Z1"), A("k10"), 15, op.is_equal)
-    for z, s in (("ZL", 2.0 ** 25), ("ZS", -16.0), ("ZC", 2.0 ** 26)):
-        act(A(z), A("Z1"), af.Copy, scale=s)
+    ts(A("YL"), A("yI"), qF, op.add)
+    ts(A("cv"), A("yI", 0, 96, 8), qF, op.add)
+    ts(kI(16, 9), A("sI", 16, 25), 4, op.arith_shift_right)
+    for z, s in (("Z1", 1.0), ("ZL", 2.0 ** 26), ("ZS", -2.0 ** 17), ("ZC", 2.0 ** 31)):
+        fill(A(z), 0.0)
+        ts(A(z, 15, 144, 16), kI(16, 9), 0, op.is_equal, s, op.mult)
     ts(A("EY"), A("mpI"), 0, op.is_equal)
     act(A("NE"), A("EY"), af.Copy, scale=-1.0)
     fill(A("ONE"), 1.0 / 128)
-    fill(A("CL"), 2.0 ** 25)
-    fill(A("CC"), -7.5 * 2.0 ** 26)
-    ts(A("MSK"), kI, 0, op.is_gt)
-    ts(K21, kI, -(1 << 21), op.mult, 15 * (1 << 21) - (1 << 24) + (1 << 13), op.add)
-    ts(KC, kI, -2, op.mult, 30 - (1 << 24) - (1 << 13), op.add)
-    act(A("RSTL"), A("MSK"), af.Copy, scale=2.0 ** 27, bias=-2.0 ** 20)
-    act(A("RSTC"), A("MSK"), af.Copy, scale=2.0 ** 28, bias=-2.0 ** 27)
+    fill(A("CL"), 2.0 ** 26)
+    for h, a, b in VSG:
+        fill(A("CL", (a, b), (8 * h, 8 * h + 8)), -7.5 * 2.0 ** 26)
+    fill(A("CC"), -7.5 * 2.0 ** 31)
+    for h, a, b in SCH:
+        fill(A("CC", 96 * h + 8 * a, 96 * h + 8 * b), 2.0 ** 31)
+    ts(A("KX", 0, 128), A("mpI"), 15, op.bitwise_and)
+    ts(A("GW"), A("KX", 0, 128), 0, op.is_equal, 2.0 ** 17, op.mult)
+    ts(A("KX", 128, 256), A("gI"), 4, op.arith_shift_right)
+    ts(A("BO"), A("KX", 128, 256), 0, op.is_equal, 2.0 ** 17, op.mult)
+    const(A("P", W, PW), 0)
+
+    ts(kF(16, 14), A("sI", 32, 46), qF, op.add)
+    for n, m, at in ((4, 12, 32), (14, 17, 48)):
+        ts(kI(at, n), kF(16, n), -(m - 1) / 2.0, op.add, 1.0 / m, op.mult)
+        ts(kF(at, n), kI(at, n), -m, op.mult)
+        tt(kF(at + 32, n), kF(at, n), kF(16, n), op.add)
+    ts(A("GL"), kF(64, 4), 16, op.mult, 15, op.add)
+    ts(A("BL"), kF(64, 4), 17, op.mult, 16, op.add)
+    cp(A("EL"), kF(80, 14))
+
+    const(A("DS"), 8192)
+    fill(A("DS", 0, Q, 16), -BIG)
+    fill(A("SLT", (0, 12), 16), -2 * BIG)
     cp(A("limF", 0, TV), A("inLim", 0, TV))
-    tt(A("k2"), kI, A("qI"), op.subtract)
-    ts(A("k3"), A("k2"), 0, op.is_equal)
-    ts(A("k4"), A("k2"), 1, op.is_equal)
-    tt(A("PM"), A("k3"), A("k4"), op.subtract)
-    ts(A("k5"), A("nI", 0, 128), 240, op.bitwise_and)
-    ts(A("k6"), A("pI", 0, 128), 240, op.bitwise_and)
-    tt(A("BO"), A("k5"), A("k6"), op.is_equal)
-    ts(A("k7"), A("mpI"), 15, op.bitwise_and)
-    ts(A("GW"), A("k7"), 0, op.is_equal, 2.0 ** 18, op.mult)
-    tt(A("k8"), A("c16I", 0, Q, 16), A("qI", 0, 12), op.add)
-    cp(A("cv"), A("k8"))
-    ts(A("cb", 0, 12), A("k8"), NPOS, op.add)
-    ts(A("cb", 12, 24), A("k8"), DUMP, op.add)
-    tt(A("tA", 0, 12), A("c256"), A("qI", 0, 12), op.add)
-    ts(A("tB", 0, 12), A("tA", 0, 12), 240, op.add)
-    tt(A("cp"), A("tB", 0, 12), A("cb", 0, 12), op.subtract)
-
-    def cnt(x, src, z, const, a, b):
-        mms(A(x, a, b), [(A("ONE"), A(const, a, b))] + [(A(z, 15 - q, 143 - q), A(src, a * 16 + q, b * 16, 16)) for q in range(16)])
-
-    def gather_l(t):
-        lst, ab = ("aL%d" if t else "oL%d") % t, "AB%d" % (t % 2)
-
-        def one(a, b):
-            off, ye, o = A(lst, a, b), A("YE", 16 * a, 16 * b), A("D", 16 * a, 16 * b)
-            me = emit("v", lambda q: q.tensor_tensor(o[3], T.P[:, :].indirect(off[3]), ye[3], op.subtract), [A("P"), off, ye], [o], 0.05 + 1.56 * CY * o[4])
-            act(A("SG", 16 * a, 16 * b), o, af.Sign, bias=-0.5)
-            act(A(ab, 16 * a, 16 * b), o, af.Abs)
-            cnt("XL", "SG", "ZL", "CL", a, b)
-            cnt("XS", ab, "ZS", "KT", a, b)
-            return me
-        return [one(a, b) for a, b in LCH]
-
-    def gather_c(t):
-        lst = ("aC%d" if t else "oC%d") % t
-
-        def one(a, b):
-            off, ye, o = A(lst, a, b), A("YE", 16 * a, 16 * b), A("IC", 16 * a, 16 * b)
-            me = emit("v", lambda q: q.tensor_tensor(o[3], T.P[:, :].indirect(off[3]), ye[3], op.is_gt), [A("P"), off, ye], [o], 0.05 + 1.56 * CY * o[4])
-            cnt("XC", "IC", "ZC", "CC", a, b)
-            return me
-        return [one(a, b) for a, b in CCH]
-
-    def gather_s(t):
-        lst = ("aC%d" if t else "oC%d") % t
-        for a, b in SCH:
-            act(A("CR", 16 * a, 16 * b), A("P"), af.Copy, off=A(lst, a, b))
-        for j, (a, b) in enumerate(SCH):
-            ps = A(("OB", "SWP")[j % 2], 0, 16 * (b - a))
-            mms(ps, [(A("EY"), A("CR", 16 * a, 16 * b)), (A("NE"), A("YE", 16 * a, 16 * b))])
-            act(A("IC", 16 * a, 16 * b), ps, af.Sign, bias=-0.5)
-        if SCH:
-            cnt("XC", "IC", "ZL", "CL", SCH[0][0], SCH[-1][1])
-
-    def usum(p):
-        mms(A("u"), [(A("Z1", 15 - q, 143 - q), A("AB%d" % p, NPOS + q, NPOS + Q, 16)) for q in range(16)])
-        act(LF(36), A("u"), af.Copy)
-        act(LF(37), A("u"), af.Copy)
-
-    def uint():
-        return cp(LI(2), LF(36))
-
-    def wcount(t):
-        d = "DL%d" % (t % 2)
-        return [cp(LI(21), A("w")), ts(LI(22), LI(21), 3 << 18, op.bitwise_and), tt(starts(d, 0), starts(d, 0), LI(22), op.add),
-                scan(TH, A("MSK"), A(d), 0.0, op.mult, op.add)]
-
-    def lims(t):
-        act(A("PM1_%d" % (t % 2)), A("PM"), af.Copy, scale=A("limF", t, t + 1))
-        mms(A("lm"), [(A("BO"), A("PM1_%d" % (t % 2)))])
-        act(A("DL%d" % (t % 2)), A("lm"), af.Copy, scale=2.0 ** 18)
-
-    def pnew(to, y):
-        return emit("v", lambda q: q.tensor_tensor(T.P[:, :].indirect(to[3]), T.md[:, :], y[3], op.add), [A("md"), y, to], [A("P")], 0.05 + 3.8 * CY * Q)
-
-    def starts(name, a=15):
-        return A(name, a, None, 16) if name not in PART else A(name, a, PART[name][2], 16)
-
-    lims(0)
-    usum(0)
+    ts(kF(96, 24), A("sI", 48, 72), qF, op.subtract)
+    ts(A("TX", 0, 24), kF(96, 24), 0, op.is_equal)
+    ts(A("TX", 24, 48), kF(96, 24), 1, op.is_equal)
+    tt(A("PM"), A("TX", 0, 24), A("TX", 24, 48), op.subtract)
     for t in range(TV):
-        p = t % 2
-        AB, yv = A("AB%d" % p), A("AB%d" % p, NPOS, NPOS + Q)
-        nxt = t + 1
-        last = nxt == TV
-        pv = ("aV%d" if t else "oV%d") % t
-        Lp, V = A(pv, 0, Q), A(pv, Q, 2 * Q)
-        seq = gather_l(t)
-        wseq = wcount(t) if t else [scan(TH, A("MSK"), A("DL0"), 0.0, op.mult, op.add)]
-        seq += gather_c(t)
-        seq.append(uint())
-        wseq[0]["soft"].append(seq[0])
-        chain(seq)
-        gather_s(t)
-        tt(TA, V, TH, op.is_ge)
-        tt(A("y_"), TA, V, op.add)
-        ts(A("tS"), V, 15 << 18, op.bitwise_and, 9, op.arith_shift_right)
-        tt(A("KEYC"), A("y_"), K21, op.add)
-        tt(A("SLT"), A("tS"), KC, op.add)
-        tt(A("mkL"), A("XL", 0, Q), Lp, op.min)
-        scan(A("RS"), A("RSTL"), A("XS", 0, Q), -2.0 ** 20, op.min, op.max)
-        scan(A("RL"), A("RSTL"), A("mkL"), -2.0 ** 20, op.min, op.max)
-        RL, RC = starts("RL"), starts("RC")
-        act(LF(0), LF(36), af.Copy, scale=37.0, bias=float(t))
-        act(LF(1), RL, af.Copy, bias=97.0 * t)
-        act(LF(10), RL, af.Copy, scale=2.0, bias=-8192.0)
-        cp(LI(0, 2), A("RLS", 15, 384, 16))
-        ts(LI(3), LI(0), 4095, op.bitwise_and)
-        tt(LI(4, 2), LI(2, 2), LF(36, 2), op.mult)
-        ts(LI(6, 2), LI(4, 2), 5, op.arith_shift_right)
-        tt(LI(8, 2), LI(6, 2), LF(0, 2), op.add)
-        ts(LI(10), LI(8), 4095, op.bitwise_and)
-        ts(LI(11), LI(9), 3840, op.bitwise_and)
-        ts(LI(12), LI(1), 15, op.bitwise_and)
-        ts(LF(2), LI(12), 8192, op.mult, 4096, op.add)
-        tt(LF(3), LF(2), LI(10), op.add)
-        tt(LF(4), A("cv"), LI(3), op.subtract)
-        tt(LF(5), LI(11), LF(4), op.add)
-        tt(LF(6), LF(5), RL, op.add)
-        ts(LF(7), RL, 0, op.is_lt)
-        ts(LF(8), RL, 0, op.is_ge)
-        tt(LF(9), LF(7), LF(3), op.mult)
-        tt(LF(11), LF(6), LF(9), op.max)
-        ts(LI(13), LI(0), 9, op.arith_shift_right, 240, op.bitwise_and)
-        tt(LF(12), A("cp"), LI(13), op.subtract)
-        ts(LF(13), LI(11), -DUMP, op.add)
-        tt(TA, A("XC", 0, Q), A("KEYC"), op.min)
-        tt(A("mk"), TA, A("SLT"), op.max)
-        scan(A("RC"), A("RSTC"), A("mk"), -2.0 ** 27, op.min, op.max)
-        if not last:
-            lims(nxt)
-        cp(LI(16), RC)
-        ts(LF(14), RC, -2.0 ** 24, op.is_lt)
-        ts(LF(15), RC, -2.0 ** 24, op.is_ge)
-        ts(LI(17), LI(16), 1, op.bitwise_and)
-        ts(LI(18), LI(16), 0x3FFFE, op.bitwise_and, 1, op.arith_shift_right)
-        tt(LF(16), LF(14), LF(11), op.mult)
-        tt(LF(17), LI(17), LI(18), op.mult)
-        tt(starts("bL", 0), LF(16), LF(17), op.add)
-        scan(TA, A("MSK"), A("bL"), 0.0, op.mult, op.add)
-        tt(A("dif"), TA, Lp, op.subtract)
-        ts(TB, A("dif"), -4096, op.max, 4096, op.min)
-        tt(A("sL"), TB, Lp, op.add)
-        ts(A("sM"), A("sL"), 4095, op.bitwise_and)
-        if not last:
-            cp(A("oL%d" % (nxt % 2)), A("sM"))
-            send("L", nxt)
-        tt(LF(18), LF(14), LF(8), op.mult)
-        tt(LF(20), LF(12), LF(18), op.mult)
-        tt(LF(21), LF(13), LF(18), op.mult)
-        tt(LF(22, 2), LF(20, 2), A("cb"), op.add)
-        cp(A("LST"), LF(22, 2))
-        PL, NL = A("LST", 0, 12), A("LST", 12, 24)
-        act(A("AB%d" % (1 - p), NPOS, NPOS + Q), AB, af.Copy, off=PL)
-        act(A("nD"), A("D"), af.Relu, scale=-1.0, off=PL)
-        act(A("md"), A("nD"), af.Copy, scale=-1.0)
-        tt(LF(24), LF(15), LF(8), op.max)
-        tt(starts("bR", 0), LF(24), RC, op.mult)
-        ts(LI(19), LI(16), 0x1FDFFE, op.bitwise_and)
-        ts(LI(20), LI(16), 0x3C000, op.bitwise_and)
-        ts(LF(25), LI(19), 1 << 18, op.add)
-        ts(LF(26), LI(20), (1 << 21) + (1 << 13), op.add)
-        tt(LF(27), LF(26), LI(17), op.mult)
-        tt(LF(28), LF(25), LF(27), op.max)
-        tt(LF(29), LF(10), LF(14), op.mult)
-        tt(LF(30), LF(28), LF(15), op.mult)
-        tt(starts("bN", 0), LF(29), LF(30), op.add)
-        scan(TA, A("MSK"), A("bR"), 0.0, op.mult, op.add)
-        tt(A("hot"), A("mk"), TA, op.is_equal)
-        scan(TB, A("MSK"), A("bN"), 0.0, op.mult, op.add)
-        tt(A("dif"), TB, V, op.subtract)
-        tt(TA, A("hot"), A("dif"), op.mult)
-        on = "oV%d" % (nxt % 2)
-        tt(A(on, Q, 2 * Q), TA, V, op.add)
+        act(A("PM1", 24 * t, 24 * t + 24), A("PM"), af.Copy, scale=A("limF", t, t + 1))
+    mms(A("MS", 64, 208), [(A("BO"), A("PM1"))])
+    const(A("CT"), 1 << 21)
+    const(A("CT", 16, 144, 24), (8 << 17) + 4096)
+    fill(A("CT", 0, 144, 24), -BIG)
+    tt(A("LT"), A("MS", 64, 208), A("CT"), op.add)
+    for t in range(TV):
+        act(A("DC%d" % t), A("LT", 24 * t, 24 * t + 24), af.Copy, off=A("EL", 0, 13))
 
-        pnew(NL, yv)["bonus"] = BONUS if last else 0.0
+    def Z(x, j, c=None, n=1):
+        return A(x, R17 * j, R17 * (j + n)) if c is None else A(x, R17 * j + c, R17 * (j + n), 17)
+    const(Z("M", 0, None, 3), 1)
+    const(Z("M", 0, 0, 3), 0)
+    const(Z("Dd", 0), 8192)
+    const(Z("Dd", 1), 0)
+    const(Z("Dd", 2), 2)
+    const(Z("Dd", 2, 9), -30)
+    const(A("cD", 0, 12), W)
+    ts(A("cD", 12, 24), A("cv"), DUMP, op.add)
+    fill(A("cE", 0, 12), -OFF)
+    fill(A("cE", 12, 24), 0.0)
+    for x in ("oS0", "oS1"):
+        const(A(x, (0, 12), 16), 0)
+    fill(A("oV0", (0, 12), 16), -(1 << 30))
+
+    def turn(x, t, s, out):
+        n = x[4] // 16
+        vtr(A(t), x)
+        mms(A(out, (0, n, 2)), [(A(s + "00"), A(t, (0, n, 2))), (A(s + "01"), A(t, (1, n, 2)))])
+        mms(A(out, (1, n, 2)), [(A(s + "10"), A(t, (0, n, 2))), (A(s + "11"), A(t, (1, n, 2)))])
+        return A(out, (0, n))
+
+    def lists(o, x):
+        return [cp(A(o, 96 * h, 96 * h + 96), A(x, (0, 12), (8 * h, 8 * h + 8))) for h in (0, 1)]
+
+    cp(A("X0", 0, Q), A("inL"))
+    turn(A("X0", 0, Q), "TL", "S", "S1")
+    lists("oL0", "S1")
+    cp(rows("oS0"), A("S1", (0, 12)))
+    TXs = [A("TX", Q * j, Q * j + Q) for j in range(5)]
+    act(A("XL", 0, Q), A("inO"), af.Copy, scale=-8192.0, bias=15 * 8192.0 - OFF)
+    act(A("XS", 0, Q), A("inB"), af.Copy, scale=2.0 ** 17)
+    act(A("S3", (0, 12)), A("inB"), af.Copy, scale=1.0 - 2.0 ** 17, bias=2.0 ** 20 + 4096)
+    ts(TXs[1], A("inC"), 0, op.max)
+    ts(TXs[3], A("inC"), 0, op.is_lt)
+    tt(TXs[0], A("XL", 0, Q), TXs[1], op.add)
+    tt(TXs[2], A("XS", 0, Q), TXs[0], op.add)
+    tt(A("VT", 0, Q), A("S3", (0, 12)), TXs[3], op.mult)
+    tt(A("X0", Q, 2 * Q), A("VT", 0, Q), TXs[2], op.add)
+    cp(rows("oV0"), turn(A("X0", Q, 2 * Q), "TV", "S", "S2"))
+    fill(A("XC", (0, 12), 16), -2 * BIG)
+    for x in ("VT", "XL", "XS"):
+        fill(A(x, R17, R17 + 1), 0.0)
+
+    def clist(t):
+        ts(A("sC"), rows("oV%d" % (t % 2)), 8191, op.bitwise_and)
+        lists("oC%d" % (t % 2), "sC")
+    clist(0)
+    for x in ("00", "01", "10", "11"):
+        act(A("B" + x), A("S" + x), af.Copy)
+
+    def yexp(p):
+        seq = [act(A("YE", 128 * a, 128 * b), A("y%d" % p), af.Copy, off=A("YL", 8 * a, 8 * b)) for a, b in YCH]
+        chain(seq)
+        seq[0]["bonus"] = BONUS
+
+    def span(x, h, a, b):
+        return A(x, HALF * h + 128 * a, HALF * h + 128 * b)
+
+    def piece(x, h, a, b):
+        return A(x, (a, b), (128 * h, 128 * h + 128))
+
+    def weights(z):
+        return [A(z, 15 - q, 143 - q) for q in range(16)]
+
+    def usum(p, t):
+        mms(A("MS", 0, 12), [(z, A("y%d" % p, q, Q, 16)) for q, z in enumerate(weights("Z1"))])
+        act(A("RLS", 15, Q, 16), A("MS", 0, 12), af.Copy)
+        act(LF(0), A("MS", 0, 12), af.Copy, scale=37.0, bias=float(t))
+        act(A("uF", 0, 12), A("MS", 0, 12), af.Copy)
+        act(A("uF", 12, 24), A("MS", 0, 12), af.Copy)
+
+    def by_scalar(pieces, raw, lst, banks, sq):
+        ps = [A(banks[j], (0, 8 * (b - a))) for j, (h, a, b) in enumerate(pieces)]
+        for j, (h, a, b) in enumerate(pieces):
+            mms(ps[j], [(A("NE"), A("YE", 128 * a, 128 * b))], last=False)
+            sq.append(act(span(raw, h, a, b), A("P"), af.Copy, off=A(lst, 96 * h + 8 * a, 96 * h + 8 * b)))
+            mms(ps[j], [(A("EY"), span(raw, h, a, b))], first=False)
+        return ps
+
+    yexp(0)
+    usum(0, 0)
+    for t in range(TV):
+        p, nxt = t % 2, t + 1
+        last = nxt == TV
+        lL, lC, L, V = [("a%s%d" if t else "o%s%d") % (k, t) for k in "LCSV"]
+        seq, sq = [], []
+        late = list(zip(LSC, by_scalar(LSC, "LR", lL, ("S1", "S2"), sq)))
+        for h, a, b in LCH:
+            d = span("D", h, a, b)
+            seq.append(tt(d, A("P"), A("YE", 128 * a, 128 * b), op.subtract, off=A(lL, 96 * h + 8 * a, 96 * h + 8 * b)))
+            for x, src in [((h, a, b), d)] + late:
+                sq.append(act(piece("AB", *x), src, af.Abs))
+                if x in VSG:
+                    seq.append(ts(piece("SG", *x), src, 0, op.is_gt))
+                else:
+                    sq.append(act(piece("SG", *x), src, af.Sign, bias=-0.5))
+            late = []
+        for a, b in LSUM:
+            mms(A("XS", 16 * a, 16 * b), [(z, A("AB", (a, b), (q, 256, 16))) for q, z in enumerate(weights("ZS"))])
+            mms(A("XL", 16 * a, 16 * b), [(A("ONE"), A("CL", (a, b)))] + [(z, A("SG", (a, b), (q, 256, 16))) for q, z in enumerate(weights("ZL"))])
+        for h, a, b in CCH:
+            seq.append(tt(span("IC", h, a, b), A("P"), A("YE", 128 * a, 128 * b), op.is_gt, off=A(lC, 96 * h + 8 * a, 96 * h + 8 * b)))
+        chain(seq)
+        for x, ps in zip(SCH, by_scalar(SCH, "CR", lC, ("S1", "S2", "S3"), sq)):
+            sq.append(act(span("IC", *x), ps, af.Sign, bias=-0.5))
+        chain(sq)
+        for h, a, b in CSUM:
+            lo, hi = HALF * h + 128 * a, HALF * h + 128 * b
+            mms(A("XC", (a, b), (8 * h, 8 * h + 8)), [(A("ONE"), A("CC", 96 * h + 8 * a, 96 * h + 8 * b))] + [(z, A("IC", lo + q, hi, 16)) for q, z in enumerate(weights("ZC"))])
+        RL = A("RLS", Q + 15, 2 * Q, 16)
+        tt(A("mkL"), A("XL", 0, Q), rows(L), op.min)
+        scan(A("RLS", Q, 2 * Q), A("DS"), A("mkL"), op.add, op.max)
+        scan(A("RLS", 2 * Q, 3 * Q), A("DS"), A("XS", 0, Q), op.add, op.max)
+        cp(LI(0, 3), A("RLS", 15, 3 * Q, 16))
+        ts(LF(1), RL, 97.0 * t, op.add)
+        ts(LI(3, 2), LI(0, 2), 4095, op.bitwise_and)
+        tt(LI(7, 2), LI(3, 2), A("uF"), op.mult)
+        ts(LI(9, 2), LI(7, 2), 5, op.arith_shift_right)
+        tt(LI(11, 2), LI(9, 2), LF(0, 2), op.add)
+        ts(LI(13), LI(12), 3840, op.bitwise_and)
+        ts(LI(6), LI(11), 4095, op.bitwise_and)
+        tt(LI(5), LI(13), A("cv"), op.add)
+        ts(LI(14, 2), LI(1, 2), 15 << 13, op.bitwise_and)
+        ts(A("GF"), A("RLS", Q, 2 * Q), 0, op.is_ge, off=A("GL", 0, 3))
+        tt(LF(2, 2), LI(14, 2), LI(5, 2), op.add)
+        tt(LF(5, 2), LI(4, 2), A("cD"), op.subtract)
+        tt(LF(4), LF(2), LF(3), op.subtract)
+        tt(LF(7, 3), LF(4, 3), A("GF", 0, 36), op.mult)
+        tt(Z("Dd", 0, 0), LF(7), LF(3), op.add)
+        act(Z("Dd", 1, 0), RL, af.Copy, bias=-4096.0 - 2.0 ** 20)
+        act(Z("Dd", 2, 0), RL, af.Relu, scale=-2.0 ** -19)
+        ts(A("tS"), rows(V), 17, op.arith_shift_right)
+        ts(rows("SLT"), A("tS"), 110 - 0.5 + 6.0 / 256, op.add, 2.0 ** 25, op.mult)
+        tt(rows("XC"), rows("XC"), rows(V), op.min)
+        tt(A("mk"), A("XC", (0, 12), (0, 17)), A("SLT"), op.max)
+        scan(A("RC"), A("DC%d" % t, 0, R17), A("mk"), op.add, op.max)
+        RC = A("RC", 16, R17, 17)
+        ts(A("M", 1, 64 * 17, 17), A("RC"), -2 * OFF, op.is_lt, off=A("BL"))
+        if t:
+            cp(LI(22), A("MS", 16, 28))
+            ts(LI(23), LI(22), 3 << 17, op.bitwise_and)
+            tt(LI(16), RC, LI(23), op.subtract)
+        else:
+            cp(LI(16), RC)
+        tt(LF(10, 2), LF(8, 2), Z("M", 3, 1, 2), op.mult)
+        tt(LF(5, 2), LF(10, 2), A("cD"), op.add)
+        cp(A("LST"), LF(5, 2))
+        PL, NL = A("LST", 0, 12), A("LST", 12, 24)
+        yv, dy = A("y%d" % p), A("S3", (0, 12))
+        mms(dy, [(A("NE"), yv)], last=False)
+        act(A("pa"), A("P"), af.Copy, off=PL)
+        mms(dy, [(A("EY"), A("pa"))], first=False)
+        act(A("y%d" % (1 - p)), dy, af.Abs)
+        act(A("nD"), dy, af.Relu, scale=-1.0)
+        act(A("md"), A("nD"), af.Copy, scale=-1.0)
+        oS, oV, oB = ["o%s%d" % (k, nxt % 2) for k in "SVB"]
+        ts(LI(19), LI(16), 20, op.arith_shift_right, 1, op.bitwise_and)
+        ts(LI(20), LI(16), (1 << 17) - 1, op.bitwise_and)
+        tt(Z("Dd", 0, 1), LI(19), LI(20), op.mult)
+        scan(A("VT", 0, R17), Z("M", 0), Z("Dd", 0), op.mult, op.add)
+        zl = A("VT", 1, R17 + 1)
+        tt(zl, zl, A(L), op.subtract)
+        ts(zl, zl, HOT - 4096, op.max, HOT + 4096, op.min)
+        tt(A("sL"), zl, A(L), op.add)
+        ts(rows(oS), rows("sL"), 4095, op.bitwise_and)
+        if not last:
+            lists("oL%d" % (nxt % 2), oS)
+            send_list("L", nxt)
+        ts(LI(17), LI(16), (1 << 20) + (31 << 12), op.bitwise_and)
+        ts(LI(18), LI(16), 20, op.arith_shift_right, 31, op.bitwise_and)
+        tt(Z("Dd", 1, 1, 2), LI(17, 2), A("cE"), op.add)
+        scan(A("XS", 0, R17), Z("M", 1), Z("Dd", 1), op.mult, op.add)
+        scan(A("XL", 0, R17), Z("M", 2), Z("Dd", 2), op.mult, op.add)
+        zr = A("XL", 1, R17 + 1)
+        tt(A("dif"), A("XS", 1, R17 + 1), A(V), op.subtract)
+        ts(A(oB), zr, 14, op.is_equal, 2.0 ** 17, op.mult)
+        ts(zr, zr, 15, op.is_equal)
+        tt(zr, zr, A("dif"), op.mult)
+        tt(A(oV), zr, A(V), op.add)
+        me = emit("v", lambda q, to=NL, y=yv: q.tensor_tensor(T.P[:, :].indirect(to[3]), T.md[:, :], y[3], op.add), [A("md"), yv, NL], [A("P")], 0.05 + 3.8 * CY * Q)
+        me["bonus"] = BONUS if last else 0.0
         if last:
             break
-        coff(nxt)
-        send("C", nxt)
-        tt(A(on, 0, Q), A("sM"), K13, op.add)
-        send("V", nxt)
+        clist(nxt)
+        chain([send_list("C", nxt), send_rows(nxt)])
         yexp(1 - p)
-        cp(A("Bf"), LF(15))
-        mms(A("w"), [(A("GW"), A("Bf"))])
-        usum(1 - p)
+        act(A("Bf"), Z("M", 0, 1), af.Copy, scale=-1.0, bias=1.0)
+        mms(A("MS", 16, 28), [(A("GW"), A("Bf"))])
+        usum(1 - p, nxt)
 
     dma("y", T.zp[:, :], T.P[:, 0:W], [A("P", 0, W)], [], 6.0)
-    pe = TV % 2
-    dma("y", T.zy[:, :], T["AB%d" % pe][:, NPOS:NPOS + Q], [A("AB%d" % pe, NPOS, NPOS + Q)], [], 2.0)
-    VN = A("oV%d" % pe, Q, 2 * Q)
-    cp(A("X0", 0, Q), A("sM"))
-    turn(A("X0", 0, Q), "ML", "TL", "S", A("SWP", 0, Q))
-    act(A("E0", 0, Q), A("SWP", 0, Q), af.Copy)
+    dma("y", T.zy[:, :], T["y%d" % (TV % 2)][:, :], [A("y%d" % (TV % 2))], [], 2.0)
+    TB = A("VT", 0, Q)
+    cp(A("X0", 0, Q), rows(oS))
+    act(A("E0", 0, Q), turn(A("X0", 0, Q), "TL", "S", "S1"), af.Copy)
     dma("y", T.zl[:, :], T.E0[:, 0:Q], [A("E0", 0, Q)], [], 2.0)
-    ts(A("tF"), VN, 1, op.arith_shift_right, 8191, op.bitwise_and)
-    ts(A("tA"), A("tF"), 4096, op.is_lt)
-    ts(TB, A("tF"), 1, op.add)
-    tt(A("tC"), A("tA"), TB, op.mult)
-    ts(A("X0", Q, 2 * Q), A("tC"), -1, op.add)
-    turn(A("X0", Q, 2 * Q), "MV", "TV", "S", A("OB", 0, Q))
-    ts(A("sL"), VN, 14, op.arith_shift_right, 15, op.bitwise_and)
-    ts(A("X1", 0, Q), A("sL"), -1, op.mult, 15, op.add)
-    ts(A("sC"), VN, 18, op.arith_shift_right, 7, op.bitwise_and)
-    ts(TB, A("tF"), -4096, op.add, 0, op.max)
-    tt(A("X1", Q, 2 * Q), A("sC"), TB, op.add)
-    act(A("E0", Q, 2 * Q), A("OB", 0, Q), af.Copy)
+    ts(A("tF"), rows(oV), 8191, op.bitwise_and)
+    ts(TXs[0], A("tF"), 4096, op.min)
+    ts(TB, A("tF"), 4096, op.is_ge, -4097, op.mult)
+    tt(A("X0", Q, 2 * Q), TB, TXs[0], op.add)
+    act(A("E0", Q, 2 * Q), turn(A("X0", Q, 2 * Q), "TV", "S", "S2"), af.Copy)
     dma("y", T.zc[:, :], T.E0[:, Q:2 * Q], [A("E0", Q, 2 * Q)], [], 2.0)
-    turn(A("X1"), "MO", "TO", "B", A("SWP", 0, 384))
-    act(A("oB"), A("SWP", 0, 384), af.Copy)
+    ts(A("tS"), rows(oV), 13, op.arith_shift_right, 15, op.bitwise_and)
+    ts(A("X1", 0, Q), A("tS"), -1, op.mult, 15, op.add)
+    ts(A("sC"), rows(oV), 17, op.arith_shift_right, 7, op.bitwise_and)
+    ts(TB, A("tF"), -4096, op.add, 0, op.max)
+    tt(TB, TB, A("sC"), op.add)
+    ts(TXs[1], rows(oB), 2.0 ** -17, op.mult)
+    tt(A("X1", Q, 2 * Q), TB, TXs[1], op.add)
+    act(A("oB"), turn(A("X1"), "TO", "B", "S3"), af.Copy)
     dma("y", T.zo[:, :], T.oB[:, 0:Q], [A("oB", 0, Q)], [], 2.0)
     dma("y", T.zb[:, :], T.oB[:, Q:2 * Q], [A("oB", Q, 2 * Q)], [], 2.0)
 
@@ -511,7 +533,7 @@ def rank_program(g, core, T, topo):
         for s in succ[o["i"]]:
             left[s["i"]] -= 1
             if not left[s["i"]]:
-                ready[s["e"]].append((max([x["fin"] + WK for x in s["need"]] + [x["fin"] for x in s["soft"]]), s))
+                ready[s["e"]].append((max([0.0] + [x["fin"] + WK for x in s["need"]] + [x["st"] + x["cost"] for x in s["soft"]]), s))
     count = {}
     clock = {e: {} for e in queues}
     for o in done:

@@ -5,16 +5,10 @@ from concourse.mybir import AluOpType, ActivationFunctionType
 N, W, Q, TV, HOP = 8, 4096, 192, 6, 3
 NPOS = 16 * Q
 HALF = NPOS // 2
-PW = 4608
-DUMP = 4352
+PW = 4304
+DUMP = 4112
 R17 = 12 * 17
-LCH = [(0, 0, 6), (1, 0, 6), (0, 6, 12), (1, 6, 12)]
-LSC = []
-VSG = []
-LSUM = [(0, 6), (6, 12)]
-CCH = [(0, 0, 12), (1, 0, 4)]
-SCH = [(1, 4, 8), (1, 8, 12)]
-CSUM = [(0, 0, 12), (1, 0, 12)]
+PLAN = [("l1", 0, 0, 4), ("L", 1, 0, 4), ("abs", 1, 0, 4), ("sign", 1, 0, 4), ("abs", 0, 0, 4), ("sign", 0, 0, 4), ("XS", 0, 0, 4), ("XL", 0, 0, 4), ("L", 0, 4, 8), ("abs", 0, 4, 8), ("sign", 0, 4, 8), ("L", 1, 4, 8), ("abs", 1, 4, 8), ("sign", 1, 4, 8), ("XS", 0, 4, 8), ("XL", 0, 4, 8), ("L", 0, 8, 12), ("abs", 0, 8, 12), ("over", 0, 8, 12), ("L", 1, 8, 12), ("abs", 1, 8, 12), ("over", 1, 8, 12), ("XL", 0, 8, 12), ("XS", 0, 8, 12), ("C", 0, 0, 12), ("C", 1, 0, 4), ("c2", 1, 4, 8), ("c1", 1, 8, 12), ("said", 1, 4, 8), ("XC", 0, 0, 12), ("said", 1, 8, 12), ("XC", 1, 0, 12)]
 YCH = [(0, 6), (6, 12)]
 BIG = 2.0 ** 33
 OFF = 2.0 ** 24
@@ -26,18 +20,18 @@ for _n, _w, _d in (
         ("P", PW, BF), ("D", NPOS, BF), ("AB", [12, 256], BF), ("SG", [12, 256], BF), ("IC", NPOS, BF), ("y0", Q, BF), ("y1", Q, BF),
         ("YE", HALF, BF), ("CR", NPOS, BF), ("LR", NPOS, BF), ("YL", 96, U16), ("GL", 4, U16), ("BL", 4, U16), ("EL", 14, U16),
         ("inL", Q, I32), ("inC", Q, I32), ("inO", Q, BF), ("inB", Q, BF), ("inLim", 8, I32), ("limF", 8, F32),
-        ("CL", [12, 16], BF), ("CC", Q, BF), ("ONE", 128, BF),
-        ("Z1", 144, BF), ("ZL", 144, BF), ("ZC", 144, BF), ("ZS", 144, BF), ("GW", 128, BF), ("BO", 128, BF), ("EY", 128, BF), ("NE", 128, BF),
+        ("CL", [12, 16], BF), ("CC", [12, 16], BF), ("ONE", 128, BF),
+        ("ZF", 144, BF), ("Z1", 144, BF), ("ZL", 144, BF), ("ZC", 144, BF), ("ZS", 144, BF),
+        ("GW", 128, BF), ("NW", 128, BF), ("BO", 128, BF), ("EY", 128, BF), ("NE", 128, BF),
         ("PM", 24, BF), ("PM1", 144, BF), ("CT", 144, F32), ("LT", 144, F32),
-        ("S00", 128, F32), ("S01", 128, F32), ("S10", 128, F32), ("S11", 128, F32),
-        ("B00", 128, BF), ("B01", 128, BF), ("B10", 128, BF), ("B11", 128, BF),
-        ("mpI", 128, I32), ("gI", 128, I32), ("yI", 96, I32), ("sI", 96, I32), ("KX", 256, I32), ("kI", 128, I32), ("kF", 128, F32),
-        ("cv", 12, F32), ("cD", 24, F32), ("cE", 24, F32), ("X0", 384, F32), ("X1", 384, BF), ("E0", 384, F32), ("oB", 384, BF), ("TX", 5 * Q, F32), ("tF", Q, I32),
+        ("ID", 160, F32), ("SM", [4, 128], F32), ("BM", [4, 128], BF),
+        ("mpI", 160, I32), ("gI", 128, I32), ("yI", 96, I32), ("sI", 96, I32), ("KX", 256, I32), ("kI", 128, I32), ("kF", 128, F32),
+        ("cv", 12, F32), ("cD", 24, F32), ("cE", 36, F32), ("X0", 384, F32), ("X1", 384, BF), ("E0", 384, F32), ("oB", 384, BF), ("TX", 3 * Q, F32), ("tF", Q, I32),
         ("TL", [12, 16], F32), ("TV", [12, 16], F32), ("TO", [24, 16], BF),
         ("DS", Q, F32), ("mkL", Q, F32), ("mk", R17, F32), ("RLS", 3 * Q, F32), ("RC", R17, F32),
-        ("tS", Q, I32), ("SLT", [12, 17], F32), ("dif", R17, F32), ("sL", [12, 17], I32), ("sC", [12, 16], I32),
+        ("tS", Q, I32), ("SLT", [12, 17], F32), ("hot", R17, F32), ("sL", [12, 17], I32), ("sC", [12, 16], I32),
         ("M", 64 * 17, F32), ("Dd", 36 * 17, F32), ("GF", 48, F32),
-        ("LI", 300, I32), ("LF", 144, F32), ("uF", 24, F32), ("Bf", 12, BF), ("LST", 24, U16), ("pa", Q, BF), ("md", Q, BF), ("nD", Q, BF)):
+        ("LI", 240, I32), ("LF", 144, F32), ("uF", 24, F32), ("Bf", 48, BF), ("LST", 24, U16), ("pa", Q, BF), ("md", Q, BF), ("nD", Q, BF)):
     SCRATCH[_n] = ("sbuf", [128] + (_w if isinstance(_w, list) else [_w]), _d)
 for _n in ("XL", "XS", "VT", "MS"):
     SCRATCH[_n] = ("psum", [128, 512], F32)
@@ -45,7 +39,7 @@ SCRATCH["XC"] = ("psum", [128, 16, 32], F32)
 for _n in ("S1", "S2", "S3"):
     SCRATCH[_n] = ("psum", [128, 32, 16], F32)
 for _t in range(TV):
-    SCRATCH["DC%d" % _t] = ("sbuf", [128, 208], F32)
+    SCRATCH["DC%d" % (_t % 2)] = ("sbuf", [128, 208], F32)
     for _k in "LC":
         SCRATCH["o%s%d" % (_k, _t % 2)] = ("sbuf", [128, Q], U16)
     for _k in "SVB":
@@ -55,9 +49,15 @@ for _t in range(TV):
             SCRATCH["a%s%d" % (_k, _t)] = ("sbuf", [128, Q], U16)
         for _k in "SV":
             SCRATCH["a%s%d" % (_k, _t)] = ("sbuf", [128, 12, 17], I32)
-SEMAPHORES = ["sv", "ss", "st", "sg"] + [k + i for k in ("lL", "lC", "lV") for i in "01"] + ["d%d" % i for i in range(16)] + [k + "%d" % t for k in ("qL", "qC", "qV") for t in range(1, TV)]
-BONUS = 4.0
+SEMAPHORES = (["sv", "ss", "st", "sg"] + ["l" + k + i for k in "LCSV" for i in "01"] + ["d%d" % i for i in range(16)]
+              + ["q%s%d" % (k, t) for k in "LCSV" for t in range(1, TV)])
 CY, PE, FX, WK = 0.00092, 0.00062, 0.03, 0.08
+BONUS = 4.0
+LBON = 1.5
+EARLY = 10.0
+TURN = 2.0
+PLAT = 7.0
+VLAT = 6.0
 
 
 def rank_program(g, core, T, topo):
@@ -67,9 +67,7 @@ def rank_program(g, core, T, topo):
     dst = T.cores[(rank + HOP) % N]
     rid, pid = topo.addr(dst)[:2]
     emask = topo.mask(core, dst)
-    eng = topo.engines(core, dst)
-    neng = len(eng)
-    halves = [sum(1 << e for e in eng[:neng // 2]), sum(1 << e for e in eng[neng // 2:])]
+    neng = len(topo.engines(core, dst))
     op = AluOpType
     af = ActivationFunctionType
     queues = {"v": g.vector, "s": g.scalar, "t": g.tensor, "g": g, "y": g.sync}
@@ -88,7 +86,7 @@ def rank_program(g, core, T, topo):
         return (name, int(at.min()), int(at.max()) + 1, T[name][(sl(None),) + ix], len(at), frozenset(at.tolist()))
 
     def meet(x, y, e):
-        if y[1]["e"] == e:
+        if y[1]["e"] == e or (x[0] not in psum and e in "vst" and y[1]["e"] in "vst"):
             return x[1] < y[0][2] and y[0][1] < x[2] and not x[5].isdisjoint(y[0][5])
         return x[0] in psum or (x[1] < y[0][2] and y[0][1] < x[2])
 
@@ -147,6 +145,9 @@ def rank_program(g, core, T, topo):
         return emit("s", lambda q: q.activation(o[3], src, f, bias=bias, scale=sc), [i] + ([off] if off else []) + extra, [o],
                     (0.065 + 1.56 * CY * o[4]) if off else FX + CY * max(64, o[4]))
 
+    def sfill(o, c):
+        return act(o, A("X1", 0, o[4]), af.Identity, scale=0.0, bias=c)
+
     def iota(o, pattern, base, cm=0):
         cost = 0.13 + 2 * CY * o[4]
         if SCRATCH[o[0]][2] == I32:
@@ -183,32 +184,22 @@ def rank_program(g, core, T, topo):
     def LF(j, n=1):
         return A("LF", 12 * j, 12 * (j + n))
 
-    def landed(me, k, nxt, names, lat):
-        net = {"e": "net", "need": [me], "cost": 0.0, "sem": "q%s%d" % (k, nxt), "v": neng, "inc": 0, "lat": 0.0, "i": len(ops), "soft": [], "bonus": 0.0}
+    def send(k, nxt, lat, more=None):
+        o, i, s, r = A("a%s%d" % (k, nxt)), A("o%s%d" % (k, nxt % 2)), "l%s%d" % (k, nxt % 2), "q%s%d" % (k, nxt)
+        if more:
+            tr = [RemoteDMATransfer(dst_ids=[DstId(rid=rid, pnc=pid)], dma_engine_mask=emask, remote_sem=T.sem[r], srcs=[i[3], more[3]], dsts=[o[3]], alu_op=1)]
+            me = emit("g", lambda q: q.remote_dma_fused(tr, local_sem=T.sem[s]), [i, more], [], 0.6, sem=s, inc=-neng, lat=lat)
+        else:
+            me = emit("g", lambda q: q.remote_dma(out_ap=o[3], in_ap=i[3], remote_sem=T.sem[r], local_sem=T.sem[s],
+                                                  pid=pid, routing_id=rid, dma_engine_mask=emask), [i], [], 0.6, sem=s, inc=-neng, lat=lat)
+        net = {"e": "net", "need": [me], "cost": 0.0, "sem": r, "v": neng, "inc": 0, "lat": 0.0, "i": len(ops), "soft": [], "bonus": 0.0}
         ops.append(net)
-        for o in names:
-            wr[o] = [(A(o), net)]
-
-    def send_list(k, nxt):
-        o, i, s = "a%s%d" % (k, nxt), A("o%s%d" % (k, nxt % 2)), "l%s%d" % (k, nxt % 2)
-        me = emit("g", lambda q: q.remote_dma(out_ap=A(o)[3], in_ap=i[3], remote_sem=T.sem["q%s%d" % (k, nxt)], local_sem=T.sem[s],
-                                              pid=pid, routing_id=rid, dma_engine_mask=emask), [i], [], 0.6, sem=s, inc=-neng, lat=2.4)
-        landed(me, k, nxt, [o], 2.4)
-        return me
-
-    def send_rows(nxt):
-        p = nxt % 2
-        oS, oV, oB = A("oS%d" % p), A("oV%d" % p), A("oB%d" % p)
-        to, sem = [DstId(rid=rid, pnc=pid)], T.sem["qV%d" % nxt]
-        tr = [RemoteDMATransfer(dst_ids=to, dma_engine_mask=halves[0], remote_sem=sem, src=oS[3], dst=A("aS%d" % nxt)[3]),
-              RemoteDMATransfer(dst_ids=to, dma_engine_mask=halves[1], remote_sem=sem, srcs=[oV[3], oB[3]], dsts=[A("aV%d" % nxt)[3]], alu_op=1)]
-        me = emit("g", lambda q: q.remote_dma_fused(tr, local_sem=T.sem["lV%d" % p]), [oS, oV, oB], [], 0.6, sem="lV%d" % p, inc=-neng, lat=4.0)
-        landed(me, "V", nxt, ["aS%d" % nxt, "aV%d" % nxt], 4.0)
+        wr[o[0]] = [(o, net)]
         return me
 
     chain([dma("y", T.inL[:, :], T.lem[:, :], [], [A("inL")], 2.2),
            dma("y", T.inC[:, :], T.con[:, :], [], [A("inC")], 2.2),
-           dma("y", T.P[:, 0:W], T.prop[:, :], [], [A("P", 0, W)], 6.0),
+           dma("y", T.P[:, 0:W], T.prop[:, :], [], [A("P", 0, W)], PLAT),
            dma("y", T.inLim[:, 0:TV], T.lim[:, :], [], [A("inLim", 0, TV)], 2.2)])
     chain([dma("s", T.y0[:, :], T.ex[:, :], [], [A("y0")], 2.2),
            dma("s", T.inO[:, :], T.org[:, :], [], [A("inO")], 2.2),
@@ -222,7 +213,7 @@ def rank_program(g, core, T, topo):
 
     def rows(x):
         return A(x, (0, 12), (0, 16))
-    iota(A("mpI"), [[1, 128]], 0, -1)
+    iota(A("mpI"), [[1, 160]], -16, -1)
     iota(A("sI", 0, 1), [[0, 1]], 0, 1)
     iota(A("yI"), [[16, 12], [0, 8]], 0)
     iota(A("sI", 16, 25), [[-16, 9]], 0, 1)
@@ -230,31 +221,35 @@ def rank_program(g, core, T, topo):
     iota(A("sI", 48, 72), [[1, 24]], 0)
     iota(A("gI"), [[16, 8], [0, 16]], 15, -1)
     b0, b1, qF = kF(0), kF(1), kF(2)
+    fill(A("X1", 0, Q), 0.0)
     ts(kI(0), A("sI", 0, 1), 16, op.bitwise_and)
     ts(kI(1), A("sI", 0, 1), 15, op.bitwise_and)
     ts(b0, kI(0), 0, op.is_equal)
     ts(b1, kI(0), 16, op.is_equal)
     cp(qF, kI(1))
-    ts(A("S00"), A("mpI"), 0, op.is_equal, b0, op.mult)
-    ts(A("S11"), A("mpI"), 0, op.is_equal, b1, op.mult)
-    ts(A("S01"), A("mpI"), 16, op.is_equal, b0, op.mult)
-    ts(A("S10"), A("mpI"), -16, op.is_equal, b1, op.mult)
+    ts(A("ID"), A("mpI"), 0, op.is_equal)
+    for j, (at, b) in enumerate(((16, b0), (0, b0), (32, b1), (16, b1))):
+        act(A("SM", j), A("ID", at, at + 128), af.Copy, scale=b)
     ts(A("YL"), A("yI"), qF, op.add)
     ts(A("cv"), A("yI", 0, 96, 8), qF, op.add)
     ts(kI(16, 9), A("sI", 16, 25), 4, op.arith_shift_right)
+    fill(A("ZF"), 0.0)
+    ts(A("ZF", 15, 144, 16), kI(16, 9), 0, op.is_equal)
     for z, s in (("Z1", 1.0), ("ZL", 2.0 ** 26), ("ZS", -2.0 ** 17), ("ZC", 2.0 ** 31)):
-        fill(A(z), 0.0)
-        ts(A(z, 15, 144, 16), kI(16, 9), 0, op.is_equal, s, op.mult)
-    ts(A("EY"), A("mpI"), 0, op.is_equal)
+        act(A(z), A("ZF"), af.Copy, scale=s)
+    act(A("EY"), A("ID", 16, 144), af.Copy)
     act(A("NE"), A("EY"), af.Copy, scale=-1.0)
-    fill(A("ONE"), 1.0 / 128)
-    fill(A("CL"), 2.0 ** 26)
-    for h, a, b in VSG:
-        fill(A("CL", (a, b), (8 * h, 8 * h + 8)), -7.5 * 2.0 ** 26)
-    fill(A("CC"), -7.5 * 2.0 ** 31)
-    for h, a, b in SCH:
-        fill(A("CC", 96 * h + 8 * a, 96 * h + 8 * b), 2.0 ** 31)
-    ts(A("KX", 0, 128), A("mpI"), 15, op.bitwise_and)
+    act(A("NW"), A("EY"), af.Copy, scale=-2.0 ** 18)
+    const(A("Bf", 36, 48), 2)
+    sfill(A("ONE"), 1.0 / 128)
+    sfill(A("CL"), 2.0 ** 26)
+    sfill(A("CC"), -7.5 * 2.0 ** 31)
+    for kind, h, a, b in PLAN:
+        if kind == "over":
+            sfill(A("CL", (a, b), (8 * h, 8 * h + 8)), -7.5 * 2.0 ** 26)
+        if kind == "said":
+            sfill(A("CC", (a, b), (8 * h, 8 * h + 8)), 2.0 ** 31)
+    ts(A("KX", 0, 128), A("mpI", 16, 144), 15, op.bitwise_and)
     ts(A("GW"), A("KX", 0, 128), 0, op.is_equal, 2.0 ** 17, op.mult)
     ts(A("KX", 128, 256), A("gI"), 4, op.arith_shift_right)
     ts(A("BO"), A("KX", 128, 256), 0, op.is_equal, 2.0 ** 17, op.mult)
@@ -270,8 +265,8 @@ def rank_program(g, core, T, topo):
     cp(A("EL"), kF(80, 14))
 
     const(A("DS"), 8192)
-    fill(A("DS", 0, Q, 16), -BIG)
-    fill(A("SLT", (0, 12), 16), -2 * BIG)
+    sfill(A("DS", 0, Q, 16), -BIG)
+    sfill(A("SLT", (0, 12), 16), -2 * BIG)
     cp(A("limF", 0, TV), A("inLim", 0, TV))
     ts(kF(96, 24), A("sI", 48, 72), qF, op.subtract)
     ts(A("TX", 0, 24), kF(96, 24), 0, op.is_equal)
@@ -282,10 +277,12 @@ def rank_program(g, core, T, topo):
     mms(A("MS", 64, 208), [(A("BO"), A("PM1"))])
     const(A("CT"), 1 << 21)
     const(A("CT", 16, 144, 24), (8 << 17) + 4096)
-    fill(A("CT", 0, 144, 24), -BIG)
+    sfill(A("CT", 0, 144, 24), -BIG)
     tt(A("LT"), A("MS", 64, 208), A("CT"), op.add)
-    for t in range(TV):
-        act(A("DC%d" % t), A("LT", 24 * t, 24 * t + 24), af.Copy, off=A("EL", 0, 13))
+
+    def steps(t):
+        return act(A("DC%d" % (t % 2)), A("LT", 24 * t, 24 * t + 24), af.Copy, off=A("EL", 0, 13))
+    steps(0)["bonus"] = EARLY
 
     def Z(x, j, c=None, n=1):
         return A(x, R17 * j, R17 * (j + n)) if c is None else A(x, R17 * j + c, R17 * (j + n), 17)
@@ -297,8 +294,9 @@ def rank_program(g, core, T, topo):
     const(Z("Dd", 2, 9), -30)
     const(A("cD", 0, 12), W)
     ts(A("cD", 12, 24), A("cv"), DUMP, op.add)
-    fill(A("cE", 0, 12), -OFF)
-    fill(A("cE", 12, 24), 0.0)
+    const(A("cE", 0, 12), -(1 << 20))
+    sfill(A("cE", 12, 24), -OFF)
+    const(A("cE", 24, 36), 0)
     for x in ("oS0", "oS1"):
         const(A(x, (0, 12), 16), 0)
     fill(A("oV0", (0, 12), 16), -(1 << 30))
@@ -306,43 +304,42 @@ def rank_program(g, core, T, topo):
     def turn(x, t, s, out):
         n = x[4] // 16
         vtr(A(t), x)
-        mms(A(out, (0, n, 2)), [(A(s + "00"), A(t, (0, n, 2))), (A(s + "01"), A(t, (1, n, 2)))])
-        mms(A(out, (1, n, 2)), [(A(s + "10"), A(t, (0, n, 2))), (A(s + "11"), A(t, (1, n, 2)))])
+        mms(A(out, (0, n, 2)), [(A(s, 0), A(t, (0, n, 2))), (A(s, 1), A(t, (1, n, 2)))])
+        mms(A(out, (1, n, 2)), [(A(s, 2), A(t, (0, n, 2))), (A(s, 3), A(t, (1, n, 2)))])
         return A(out, (0, n))
 
     def lists(o, x):
         return [cp(A(o, 96 * h, 96 * h + 96), A(x, (0, 12), (8 * h, 8 * h + 8))) for h in (0, 1)]
 
     cp(A("X0", 0, Q), A("inL"))
-    turn(A("X0", 0, Q), "TL", "S", "S1")
+    turn(A("X0", 0, Q), "TL", "SM", "S1")
     lists("oL0", "S1")
     cp(rows("oS0"), A("S1", (0, 12)))
-    TXs = [A("TX", Q * j, Q * j + Q) for j in range(5)]
-    act(A("XL", 0, Q), A("inO"), af.Copy, scale=-8192.0, bias=15 * 8192.0 - OFF)
-    act(A("XS", 0, Q), A("inB"), af.Copy, scale=2.0 ** 17)
-    act(A("S3", (0, 12)), A("inB"), af.Copy, scale=1.0 - 2.0 ** 17, bias=2.0 ** 20 + 4096)
-    ts(TXs[1], A("inC"), 0, op.max)
-    ts(TXs[3], A("inC"), 0, op.is_lt)
-    tt(TXs[0], A("XL", 0, Q), TXs[1], op.add)
-    tt(TXs[2], A("XS", 0, Q), TXs[0], op.add)
-    tt(A("VT", 0, Q), A("S3", (0, 12)), TXs[3], op.mult)
-    tt(A("X0", Q, 2 * Q), A("VT", 0, Q), TXs[2], op.add)
-    cp(rows("oV0"), turn(A("X0", Q, 2 * Q), "TV", "S", "S2"))
-    fill(A("XC", (0, 12), 16), -2 * BIG)
+    TXs = [A("TX", Q * j, Q * j + Q) for j in range(3)]
+    early = [act(A("XS", 0, Q), A("inB"), af.Copy, scale=2.0 ** 17),
+             act(A("S3", (0, 12)), A("inB"), af.Copy, bias=2.0 ** 20 + 4096),
+             act(A("XL", 0, Q), A("inO"), af.Copy, scale=-8192.0, bias=15 * 8192.0 - OFF)]
+    ts(TXs[1], A("inC"), -2.0 ** 22, op.mult)
+    tt(TXs[0], A("XS", 0, Q), A("inC"), op.add)
+    tt(A("VT", 0, Q), A("S3", (0, 12)), TXs[1], op.min)
+    tt(TXs[2], A("VT", 0, Q), TXs[0], op.max)
+    tt(A("X0", Q, 2 * Q), A("XL", 0, Q), TXs[2], op.add)
+    cp(rows("oV0"), turn(A("X0", Q, 2 * Q), "TV", "SM", "S2"))
+    sfill(A("XC", (0, 12), 16), -2 * BIG)
     for x in ("VT", "XL", "XS"):
-        fill(A(x, R17, R17 + 1), 0.0)
+        sfill(A(x, R17, R17 + 1), 0.0)
 
     def clist(t):
         ts(A("sC"), rows("oV%d" % (t % 2)), 8191, op.bitwise_and)
-        lists("oC%d" % (t % 2), "sC")
-    clist(0)
-    for x in ("00", "01", "10", "11"):
-        act(A("B" + x), A("S" + x), af.Copy)
+        return lists("oC%d" % (t % 2), "sC")
+    for x in clist(0):
+        x["bonus"] = EARLY
 
     def yexp(p):
         seq = [act(A("YE", 128 * a, 128 * b), A("y%d" % p), af.Copy, off=A("YL", 8 * a, 8 * b)) for a, b in YCH]
         chain(seq)
         seq[0]["bonus"] = BONUS
+        return seq
 
     def span(x, h, a, b):
         return A(x, HALF * h + 128 * a, HALF * h + 128 * b)
@@ -360,44 +357,47 @@ def rank_program(g, core, T, topo):
         act(A("uF", 0, 12), A("MS", 0, 12), af.Copy)
         act(A("uF", 12, 24), A("MS", 0, 12), af.Copy)
 
-    def by_scalar(pieces, raw, lst, banks, sq):
-        ps = [A(banks[j], (0, 8 * (b - a))) for j, (h, a, b) in enumerate(pieces)]
-        for j, (h, a, b) in enumerate(pieces):
-            mms(ps[j], [(A("NE"), A("YE", 128 * a, 128 * b))], last=False)
-            sq.append(act(span(raw, h, a, b), A("P"), af.Copy, off=A(lst, 96 * h + 8 * a, 96 * h + 8 * b)))
-            mms(ps[j], [(A("EY"), span(raw, h, a, b))], first=False)
-        return ps
-
-    yexp(0)
+    chain(early + yexp(0)[1:])
     usum(0, 0)
     for t in range(TV):
         p, nxt = t % 2, t + 1
         last = nxt == TV
         lL, lC, L, V = [("a%s%d" if t else "o%s%d") % (k, t) for k in "LCSV"]
-        seq, sq = [], []
-        late = list(zip(LSC, by_scalar(LSC, "LR", lL, ("S1", "S2"), sq)))
-        for h, a, b in LCH:
-            d = span("D", h, a, b)
-            seq.append(tt(d, A("P"), A("YE", 128 * a, 128 * b), op.subtract, off=A(lL, 96 * h + 8 * a, 96 * h + 8 * b)))
-            for x, src in [((h, a, b), d)] + late:
-                sq.append(act(piece("AB", *x), src, af.Abs))
-                if x in VSG:
-                    seq.append(ts(piece("SG", *x), src, 0, op.is_gt))
-                else:
-                    sq.append(act(piece("SG", *x), src, af.Sign, bias=-0.5))
-            late = []
-        for a, b in LSUM:
-            mms(A("XS", 16 * a, 16 * b), [(z, A("AB", (a, b), (q, 256, 16))) for q, z in enumerate(weights("ZS"))])
-            mms(A("XL", 16 * a, 16 * b), [(A("ONE"), A("CL", (a, b)))] + [(z, A("SG", (a, b), (q, 256, 16))) for q, z in enumerate(weights("ZL"))])
-        for h, a, b in CCH:
-            seq.append(tt(span("IC", h, a, b), A("P"), A("YE", 128 * a, 128 * b), op.is_gt, off=A(lC, 96 * h + 8 * a, 96 * h + 8 * b)))
-        chain(seq)
-        for x, ps in zip(SCH, by_scalar(SCH, "CR", lC, ("S1", "S2", "S3"), sq)):
-            sq.append(act(span("IC", *x), ps, af.Sign, bias=-0.5))
-        chain(sq)
-        for h, a, b in CSUM:
-            lo, hi = HALF * h + 128 * a, HALF * h + 128 * b
-            mms(A("XC", (a, b), (8 * h, 8 * h + 8)), [(A("ONE"), A("CC", 96 * h + 8 * a, 96 * h + 8 * b))] + [(z, A("IC", lo + q, hi, 16)) for q, z in enumerate(weights("ZC"))])
+        order, diff, final = {"v": [], "s": [], "t": []}, {}, {x[0]: x for x in PLAN}
+        mms(A("XL", 0, Q), [(A("ONE"), A("CL"))], last=False)
+        mms(rows("XC"), [(A("ONE"), A("CC"))], last=False)
+        for x in PLAN:
+            kind, h, a, b = x
+            ye, at = A("YE", 128 * a, 128 * b), (96 * h + 8 * a, 96 * h + 8 * b)
+            if kind == "L":
+                diff["l", h, a] = span("D", h, a, b)
+                me = tt(diff["l", h, a], A("P"), ye, op.subtract, off=A(lL, *at))
+            elif kind == "C":
+                me = tt(span("IC", h, a, b), A("P"), ye, op.is_gt, off=A(lC, *at))
+            elif kind[0] in "lc":
+                raw, lst = (span("LR", h, a, b), lL) if kind[0] == "l" else (span("CR", h, a, b), lC)
+                diff[kind[0], h, a] = ps = A("S" + kind[1], (0, 8 * (b - a)))
+                mms(ps, [(A("NE"), ye)], last=False)
+                order["s"].append(act(raw, A("P"), af.Copy, off=A(lst, *at)))
+                me = mms(ps, [(A("EY"), raw)], first=False)
+            elif kind == "abs":
+                me = act(piece("AB", h, a, b), diff["l", h, a], af.Abs)
+            elif kind == "sign":
+                me = act(piece("SG", h, a, b), diff["l", h, a], af.Sign, bias=-0.5)
+            elif kind == "over":
+                me = ts(piece("SG", h, a, b), diff["l", h, a], 0, op.is_gt)
+            elif kind == "said":
+                me = act(span("IC", h, a, b), diff["c", h, a], af.Sign, bias=-0.5)
+            elif kind == "XS":
+                me = mms(A("XS", 16 * a, 16 * b), [(z, A("AB", (a, b), (q, 256, 16))) for q, z in enumerate(weights("ZS"))])
+            elif kind == "XL":
+                me = mms(A("XL", 16 * a, 16 * b), [(z, A("SG", (a, b), (q, 256, 16))) for q, z in enumerate(weights("ZL"))], False, x == final[kind])
+            else:
+                lo, hi = span("IC", h, a, b)[1:3]
+                me = mms(A("XC", (a, b), (8 * h, 8 * h + 8)), [(z, A("IC", lo + q, hi, 16)) for q, z in enumerate(weights("ZC"))], False, x == final[kind])
+            order[me["e"]].append(me)
+        for e in order:
+            chain(order[e])
         RL = A("RLS", Q + 15, 2 * Q, 16)
         tt(A("mkL"), A("XL", 0, Q), rows(L), op.min)
         scan(A("RLS", Q, 2 * Q), A("DS"), A("mkL"), op.add, op.max)
@@ -424,13 +424,11 @@ def rank_program(g, core, T, topo):
         ts(rows("SLT"), A("tS"), 110 - 0.5 + 6.0 / 256, op.add, 2.0 ** 25, op.mult)
         tt(rows("XC"), rows("XC"), rows(V), op.min)
         tt(A("mk"), A("XC", (0, 12), (0, 17)), A("SLT"), op.max)
-        scan(A("RC"), A("DC%d" % t, 0, R17), A("mk"), op.add, op.max)
+        scan(A("RC"), A("DC%d" % p, 0, R17), A("mk"), op.add, op.max)
         RC = A("RC", 16, R17, 17)
         ts(A("M", 1, 64 * 17, 17), A("RC"), -2 * OFF, op.is_lt, off=A("BL"))
         if t:
-            cp(LI(22), A("MS", 16, 28))
-            ts(LI(23), LI(22), 3 << 17, op.bitwise_and)
-            tt(LI(16), RC, LI(23), op.subtract)
+            tt(LI(16), RC, A("MS", 32, 44), op.subtract)
         else:
             cp(LI(16), RC)
         tt(LF(10, 2), LF(8, 2), Z("M", 3, 1, 2), op.mult)
@@ -442,65 +440,75 @@ def rank_program(g, core, T, topo):
         act(A("pa"), A("P"), af.Copy, off=PL)
         mms(dy, [(A("EY"), A("pa"))], first=False)
         act(A("y%d" % (1 - p)), dy, af.Abs)
-        act(A("nD"), dy, af.Relu, scale=-1.0)
-        act(A("md"), A("nD"), af.Copy, scale=-1.0)
+        if last:
+            tt(A("md"), A("P"), yv, op.min, off=PL)["bonus"] = BONUS
+            emit("v", lambda q, to=NL: q.tensor_copy(T.P[:, :].indirect(to[3]), T.md[:, :]), [A("md"), NL], [A("P")], 0.05 + 3.8 * CY * Q)["bonus"] = BONUS
+        else:
+            act(A("nD"), dy, af.Relu, scale=-1.0)
+            act(A("md"), A("nD"), af.Copy, scale=-1.0)
         oS, oV, oB = ["o%s%d" % (k, nxt % 2) for k in "SVB"]
-        ts(LI(19), LI(16), 20, op.arith_shift_right, 1, op.bitwise_and)
-        ts(LI(20), LI(16), (1 << 17) - 1, op.bitwise_and)
-        tt(Z("Dd", 0, 1), LI(19), LI(20), op.mult)
+        ts(LI(17), LI(16), (1 << 20) + (1 << 17) - 1, op.bitwise_and)
+        ts(LI(18), LI(16), (1 << 20) + (31 << 12), op.bitwise_and)
+        ts(LI(19), LI(16), 20, op.arith_shift_right, 31, op.bitwise_and)
+        tt(Z("Dd", 0, 1, 3), LI(17, 3), A("cE"), op.add)
         scan(A("VT", 0, R17), Z("M", 0), Z("Dd", 0), op.mult, op.add)
         zl = A("VT", 1, R17 + 1)
         tt(zl, zl, A(L), op.subtract)
         ts(zl, zl, HOT - 4096, op.max, HOT + 4096, op.min)
         tt(A("sL"), zl, A(L), op.add)
         ts(rows(oS), rows("sL"), 4095, op.bitwise_and)
+        way = []
         if not last:
-            lists("oL%d" % (nxt % 2), oS)
-            send_list("L", nxt)
-        ts(LI(17), LI(16), (1 << 20) + (31 << 12), op.bitwise_and)
-        ts(LI(18), LI(16), 20, op.arith_shift_right, 31, op.bitwise_and)
-        tt(Z("Dd", 1, 1, 2), LI(17, 2), A("cE"), op.add)
-        scan(A("XS", 0, R17), Z("M", 1), Z("Dd", 1), op.mult, op.add)
-        scan(A("XL", 0, R17), Z("M", 2), Z("Dd", 2), op.mult, op.add)
-        zr = A("XL", 1, R17 + 1)
-        tt(A("dif"), A("XS", 1, R17 + 1), A(V), op.subtract)
-        ts(A(oB), zr, 14, op.is_equal, 2.0 ** 17, op.mult)
-        ts(zr, zr, 15, op.is_equal)
-        tt(zr, zr, A("dif"), op.mult)
-        tt(A(oV), zr, A(V), op.add)
-        me = emit("v", lambda q, to=NL, y=yv: q.tensor_tensor(T.P[:, :].indirect(to[3]), T.md[:, :], y[3], op.add), [A("md"), yv, NL], [A("P")], 0.05 + 3.8 * CY * Q)
-        me["bonus"] = BONUS if last else 0.0
+            way = lists("oL%d" % (nxt % 2), oS)[:1]
+            sends = [send("L", nxt, 2.4), send("S", nxt, 4.0)]
+            sends[0]["bonus"] = LBON
+        for x, j in (("XS", 1), ("XL", 2)):
+            chain(way + [scan(A(x, 0, R17), Z("M", j), Z("Dd", j), op.mult, op.add)])
+        zn, zr = A("XS", 1, R17 + 1), A("XL", 1, R17 + 1)
+        if last:
+            ts(A("VT", 256, 256 + R17), zr, 14, op.is_equal, 2.0 ** 17, op.mult)
+            tt(A(oB), A("VT", 256, 256 + R17), A(V), op.add)
+        else:
+            ts(A(oB), zr, 14, op.is_equal, 2.0 ** 17, op.mult)
+        tt(zn, zn, A(V), op.subtract)
+        ts(A("hot"), zr, 15, op.is_equal)
+        tt(zn, zn, A("hot"), op.mult)
+        tt(A(oV), zn, A(oB if last else V), op.add)
         if last:
             break
+        emit("v", lambda q, to=NL, y=yv: q.tensor_tensor(T.P[:, :].indirect(to[3]), T.md[:, :], y[3], op.add), [A("md"), yv, NL], [A("P")], 0.05 + 3.8 * CY * Q)
         clist(nxt)
-        chain([send_list("C", nxt), send_rows(nxt)])
-        yexp(1 - p)
-        act(A("Bf"), Z("M", 0, 1), af.Copy, scale=-1.0, bias=1.0)
-        mms(A("MS", 16, 28), [(A("GW"), A("Bf"))])
+        chain(sends + [send("C", nxt, 2.4), send("V", nxt, VLAT, A(oB))])
+        chain(yexp(1 - p) + [steps(nxt)])
+        act(A("Bf", 0, 12), Z("M", 0, 1), af.Copy, scale=-1.0, bias=1.0)
+        mms(A("MS", 16, 28), [(A("GW"), A("Bf", 0, 12))])
+        act(A("Bf", 12, 24), A("MS", 16, 28), af.Sign, bias=-3.5 * 2 ** 17)
+        act(A("Bf", 24, 36), A("MS", 16, 28), af.Sign, bias=-7.5 * 2 ** 17)
+        mms(A("MS", 32, 44), [(A("GW"), A("Bf", 0, 12))] + [(A("NW"), A("Bf", 12 * j, 12 * j + 12)) for j in (1, 2, 3)])
         usum(1 - p, nxt)
 
     dma("y", T.zp[:, :], T.P[:, 0:W], [A("P", 0, W)], [], 6.0)
     dma("y", T.zy[:, :], T["y%d" % (TV % 2)][:, :], [A("y%d" % (TV % 2))], [], 2.0)
     TB = A("VT", 0, Q)
-    cp(A("X0", 0, Q), rows(oS))
-    act(A("E0", 0, Q), turn(A("X0", 0, Q), "TL", "S", "S1"), af.Copy)
+    for j in range(4):
+        chain([order["s"][-1], act(A("BM", j), A("SM", j), af.Copy)])
+    cp(A("X0", 0, Q), rows(oS))["bonus"] = 2 * TURN
+    act(A("E0", 0, Q), turn(A("X0", 0, Q), "TL", "SM", "S1"), af.Copy)
     dma("y", T.zl[:, :], T.E0[:, 0:Q], [A("E0", 0, Q)], [], 2.0)
     ts(A("tF"), rows(oV), 8191, op.bitwise_and)
-    ts(TXs[0], A("tF"), 4096, op.min)
-    ts(TB, A("tF"), 4096, op.is_ge, -4097, op.mult)
-    tt(A("X0", Q, 2 * Q), TB, TXs[0], op.add)
-    act(A("E0", Q, 2 * Q), turn(A("X0", Q, 2 * Q), "TV", "S", "S2"), af.Copy)
+    ts(TB, A("tF"), 4096, op.is_ge, -8192, op.mult)
+    tt(A("X0", Q, 2 * Q), TB, A("tF"), op.add)["bonus"] = TURN
+    act(TXs[0], turn(A("X0", Q, 2 * Q), "TV", "SM", "S2"), af.Relu, bias=1.0)
+    act(A("E0", Q, 2 * Q), TXs[0], af.Copy, bias=-1.0)
     dma("y", T.zc[:, :], T.E0[:, Q:2 * Q], [A("E0", Q, 2 * Q)], [], 2.0)
     ts(A("tS"), rows(oV), 13, op.arith_shift_right, 15, op.bitwise_and)
     ts(A("X1", 0, Q), A("tS"), -1, op.mult, 15, op.add)
     ts(A("sC"), rows(oV), 17, op.arith_shift_right, 7, op.bitwise_and)
     ts(TB, A("tF"), -4096, op.add, 0, op.max)
-    tt(TB, TB, A("sC"), op.add)
-    ts(TXs[1], rows(oB), 2.0 ** -17, op.mult)
-    tt(A("X1", Q, 2 * Q), TB, TXs[1], op.add)
-    act(A("oB"), turn(A("X1"), "TO", "B", "S3"), af.Copy)
+    tt(A("X1", Q, 2 * Q), TB, A("sC"), op.add)
+    act(A("oB"), turn(A("X1"), "TO", "BM", "S3"), af.Copy)
     dma("y", T.zo[:, :], T.oB[:, 0:Q], [A("oB", 0, Q)], [], 2.0)
-    dma("y", T.zb[:, :], T.oB[:, Q:2 * Q], [A("oB", Q, 2 * Q)], [], 2.0)
+    dma("s", T.zb[:, :], T.oB[:, Q:2 * Q], [A("oB", Q, 2 * Q)], [], 2.0)
 
     succ = [[] for _ in ops]
     for o in ops:

@@ -8,30 +8,32 @@ HALF = NPOS // 2
 PW = 4304
 DUMP = 4112
 R17 = 12 * 17
-PLAN = [("l1", 0, 0, 4), ("L", 1, 0, 4), ("abs", 1, 0, 4), ("sign", 1, 0, 4), ("abs", 0, 0, 4), ("sign", 0, 0, 4), ("XS", 0, 0, 4), ("XL", 0, 0, 4), ("L", 0, 4, 8), ("abs", 0, 4, 8), ("sign", 0, 4, 8), ("L", 1, 4, 8), ("abs", 1, 4, 8), ("sign", 1, 4, 8), ("XS", 0, 4, 8), ("XL", 0, 4, 8), ("L", 0, 8, 12), ("abs", 0, 8, 12), ("over", 0, 8, 12), ("L", 1, 8, 12), ("abs", 1, 8, 12), ("over", 1, 8, 12), ("XL", 0, 8, 12), ("XS", 0, 8, 12), ("C", 0, 0, 12), ("C", 1, 0, 4), ("c2", 1, 4, 8), ("c1", 1, 8, 12), ("said", 1, 4, 8), ("XC", 0, 0, 12), ("said", 1, 8, 12), ("XC", 1, 0, 12)]
-YCH = [(0, 6), (6, 12)]
+PLAN = [("l1", 0, 4, 8), ("l2", 0, 8, 12), ("L", 0, 0, 4), ("L", 1, 0, 4), ("over", 0, 0, 4), ("over", 1, 0, 4), ("XL", 0, 0, 4), ("abs", 0, 0, 4), ("abs", 1, 0, 4), ("XS", 0, 0, 4), ("l3", 1, 8, 12), ("L", 1, 4, 8), ("over", 1, 4, 8), ("sign", 0, 4, 8), ("XL", 0, 4, 8), ("abs", 0, 4, 8), ("abs", 1, 4, 8), ("XS", 0, 4, 8), ("C", 0, 0, 12), ("sign", 0, 8, 12), ("sign", 1, 8, 12), ("XD", 0, 0, 12), ("XL", 0, 8, 12), ("XE", 0, 0, 12), ("abs", 0, 8, 12), ("abs", 1, 8, 12), ("XS", 0, 8, 12), ("C", 1, 0, 12), ("XC", 1, 0, 12)]
+YB = [(0, "S1"), (4, "S3"), (8, "S2")]
+TAIL = "B p y 0 m 1 2 v"
+TT = "0 m 1 2 u"
 BIG = 2.0 ** 33
 OFF = 2.0 ** 24
-HOT = 31 * 4096
+LOW = 30 * 4096
 
 F32, BF, I32, U16 = "float32", "bfloat16", "int32", "uint16"
 SCRATCH = {}
 for _n, _w, _d in (
         ("P", PW, BF), ("D", NPOS, BF), ("AB", [12, 256], BF), ("SG", [12, 256], BF), ("IC", NPOS, BF), ("y0", Q, BF), ("y1", Q, BF),
-        ("YE", HALF, BF), ("CR", NPOS, BF), ("LR", NPOS, BF), ("YL", 96, U16), ("GL", 4, U16), ("BL", 4, U16), ("EL", 14, U16),
+        ("YE", HALF, BF), ("LR", NPOS, BF), ("GL", 4, U16), ("BL", 4, U16), ("EL", 14, U16),
         ("inL", Q, I32), ("inC", Q, I32), ("inO", Q, BF), ("inB", Q, BF), ("inLim", 8, I32), ("limF", 8, F32),
         ("CL", [12, 16], BF), ("CC", [12, 16], BF), ("ONE", 128, BF),
         ("ZF", 144, BF), ("Z1", 144, BF), ("ZL", 144, BF), ("ZC", 144, BF), ("ZS", 144, BF),
         ("GW", 128, BF), ("NW", 128, BF), ("BO", 128, BF), ("EY", 128, BF), ("NE", 128, BF),
         ("PM", 24, BF), ("PM1", 144, BF), ("CT", 144, F32), ("LT", 144, F32),
         ("ID", 160, F32), ("SM", [4, 128], F32), ("BM", [4, 128], BF),
-        ("mpI", 160, I32), ("gI", 128, I32), ("yI", 96, I32), ("sI", 96, I32), ("KX", 256, I32), ("kI", 128, I32), ("kF", 128, F32),
-        ("cv", 12, F32), ("cD", 24, F32), ("cE", 36, F32), ("X0", 384, F32), ("X1", 384, BF), ("E0", 384, F32), ("oB", 384, BF), ("TX", 3 * Q, F32), ("tF", Q, I32),
-        ("TL", [12, 16], F32), ("TV", [12, 16], F32), ("TO", [24, 16], BF),
+        ("mpI", 160, I32), ("gI", 128, I32), ("sI", 96, I32), ("KX", 256, I32), ("kI", 128, I32), ("kF", 128, F32),
+        ("cv", 24, F32), ("cD", 48, F32), ("cE", 24, F32), ("X0", 384, F32), ("X1", 384, BF), ("E0", 384, F32), ("oB", 384, BF), ("TX", 3 * Q, F32), ("tF", Q, I32),
+        ("TL", [12, 16], F32), ("TV", [12, 16], F32), ("TO", [12, 16], BF), ("TP", [12, 16], BF), ("LH", [72, 17], I32),
         ("DS", Q, F32), ("mkL", Q, F32), ("mk", R17, F32), ("RLS", 3 * Q, F32), ("RC", R17, F32),
-        ("tS", Q, I32), ("SLT", [12, 17], F32), ("hot", R17, F32), ("sL", [12, 17], I32), ("sC", [12, 16], I32),
-        ("M", 64 * 17, F32), ("Dd", 36 * 17, F32), ("GF", 48, F32),
-        ("LI", 240, I32), ("LF", 144, F32), ("uF", 24, F32), ("Bf", 48, BF), ("LST", 24, U16), ("pa", Q, BF), ("md", Q, BF), ("nD", Q, BF)):
+        ("tS", Q, I32), ("tB", Q, BF), ("aV0", [12, 17], F32), ("sV", [12, 17], I32), ("bp", [12, 17], F32), ("SLT", [12, 17], F32), ("hot", R17, F32),
+        ("sL", [12, 17], I32), ("sC", [12, 16], I32), ("M", 48 * 17, F32), ("Dd", 36 * 17, F32), ("GF", 64, F32),
+        ("LI", 240, I32), ("LF", 144, F32), ("uF", 24, F32), ("Bf", 48, BF), ("LST", 24, U16), ("pa", Q, BF), ("md", Q, BF)):
     SCRATCH[_n] = ("sbuf", [128] + (_w if isinstance(_w, list) else [_w]), _d)
 for _n in ("XL", "XS", "VT", "MS"):
     SCRATCH[_n] = ("psum", [128, 512], F32)
@@ -42,20 +44,19 @@ for _t in range(TV):
     SCRATCH["DC%d" % (_t % 2)] = ("sbuf", [128, 208], F32)
     for _k in "LC":
         SCRATCH["o%s%d" % (_k, _t % 2)] = ("sbuf", [128, Q], U16)
-    for _k in "SVB":
-        SCRATCH["o%s%d" % (_k, _t % 2)] = ("sbuf", [128, 12, 17], I32)
+    for _k, _d in (("S", I32), ("V", F32), ("B", F32)):
+        SCRATCH["o%s%d" % (_k, _t % 2)] = ("sbuf", [128, 12, 17], _d)
     if _t:
         for _k in "LC":
             SCRATCH["a%s%d" % (_k, _t)] = ("sbuf", [128, Q], U16)
-        for _k in "SV":
-            SCRATCH["a%s%d" % (_k, _t)] = ("sbuf", [128, 12, 17], I32)
-SEMAPHORES = (["sv", "ss", "st", "sg"] + ["l" + k + i for k in "LCSV" for i in "01"] + ["d%d" % i for i in range(16)]
+        for _k, _d in (("S", I32), ("V", F32)):
+            SCRATCH["a%s%d" % (_k, _t)] = ("sbuf", [128, 12, 17], _d)
+SEMAPHORES = (["sv", "ss", "st", "sg", "dA"] + ["d%s%d" % (k, t) for k in "BC" for t in range(1, TV)] + ["l" + k + i for k in "LCSV" for i in "01"] + ["d%d" % i for i in range(16)]
               + ["q%s%d" % (k, t) for k in "LCSV" for t in range(1, TV)])
-CY, PE, FX, WK = 0.00092, 0.00062, 0.03, 0.08
+CY, PE, FX, FS, WK, WX = 0.00085, 0.00062, 0.04, 0.06, 0.06, 0.12
 BONUS = 4.0
 LBON = 1.5
 EARLY = 10.0
-TURN = 2.0
 PLAT = 7.0
 VLAT = 6.0
 
@@ -143,7 +144,7 @@ def rank_program(g, core, T, topo):
         f = af.Identity if f == af.Copy and bias else f
         sc, extra = (scale[3], [scale]) if isinstance(scale, tuple) else (scale, [])
         return emit("s", lambda q: q.activation(o[3], src, f, bias=bias, scale=sc), [i] + ([off] if off else []) + extra, [o],
-                    (0.065 + 1.56 * CY * o[4]) if off else FX + CY * max(64, o[4]))
+                    (0.065 + 1.56 * CY * o[4]) if off else FS + CY * max(64, o[4]))
 
     def sfill(o, c):
         return act(o, A("X1", 0, o[4]), af.Identity, scale=0.0, bias=c)
@@ -184,11 +185,11 @@ def rank_program(g, core, T, topo):
     def LF(j, n=1):
         return A("LF", 12 * j, 12 * (j + n))
 
-    def send(k, nxt, lat, more=None):
+    def send(k, nxt, lat, more=()):
         o, i, s, r = A("a%s%d" % (k, nxt)), A("o%s%d" % (k, nxt % 2)), "l%s%d" % (k, nxt % 2), "q%s%d" % (k, nxt)
         if more:
-            tr = [RemoteDMATransfer(dst_ids=[DstId(rid=rid, pnc=pid)], dma_engine_mask=emask, remote_sem=T.sem[r], srcs=[i[3], more[3]], dsts=[o[3]], alu_op=1)]
-            me = emit("g", lambda q: q.remote_dma_fused(tr, local_sem=T.sem[s]), [i, more], [], 0.6, sem=s, inc=-neng, lat=lat)
+            tr = [RemoteDMATransfer(dst_ids=[DstId(rid=rid, pnc=pid)], dma_engine_mask=emask, remote_sem=T.sem[r], srcs=[i[3]] + [x[3] for x in more], dsts=[o[3]], alu_op=1)]
+            me = emit("g", lambda q: q.remote_dma_fused(tr, local_sem=T.sem[s]), [i] + more, [], 0.6, sem=s, inc=-neng, lat=lat)
         else:
             me = emit("g", lambda q: q.remote_dma(out_ap=o[3], in_ap=i[3], remote_sem=T.sem[r], local_sem=T.sem[s],
                                                   pid=pid, routing_id=rid, dma_engine_mask=emask), [i], [], 0.6, sem=s, inc=-neng, lat=lat)
@@ -215,7 +216,6 @@ def rank_program(g, core, T, topo):
         return A(x, (0, 12), (0, 16))
     iota(A("mpI"), [[1, 160]], -16, -1)
     iota(A("sI", 0, 1), [[0, 1]], 0, 1)
-    iota(A("yI"), [[16, 12], [0, 8]], 0)
     iota(A("sI", 16, 25), [[-16, 9]], 0, 1)
     iota(A("sI", 32, 46), [[16, 14]], 0)
     iota(A("sI", 48, 72), [[1, 24]], 0)
@@ -230,8 +230,6 @@ def rank_program(g, core, T, topo):
     ts(A("ID"), A("mpI"), 0, op.is_equal)
     for j, (at, b) in enumerate(((16, b0), (0, b0), (32, b1), (16, b1))):
         act(A("SM", j), A("ID", at, at + 128), af.Copy, scale=b)
-    ts(A("YL"), A("yI"), qF, op.add)
-    ts(A("cv"), A("yI", 0, 96, 8), qF, op.add)
     ts(kI(16, 9), A("sI", 16, 25), 4, op.arith_shift_right)
     fill(A("ZF"), 0.0)
     ts(A("ZF", 15, 144, 16), kI(16, 9), 0, op.is_equal)
@@ -247,8 +245,6 @@ def rank_program(g, core, T, topo):
     for kind, h, a, b in PLAN:
         if kind == "over":
             sfill(A("CL", (a, b), (8 * h, 8 * h + 8)), -7.5 * 2.0 ** 26)
-        if kind == "said":
-            sfill(A("CC", (a, b), (8 * h, 8 * h + 8)), 2.0 ** 31)
     ts(A("KX", 0, 128), A("mpI", 16, 144), 15, op.bitwise_and)
     ts(A("GW"), A("KX", 0, 128), 0, op.is_equal, 2.0 ** 17, op.mult)
     ts(A("KX", 128, 256), A("gI"), 4, op.arith_shift_right)
@@ -256,6 +252,7 @@ def rank_program(g, core, T, topo):
     const(A("P", W, PW), 0)
 
     ts(kF(16, 14), A("sI", 32, 46), qF, op.add)
+    act(A("cv", 0, 12), kF(16, 12), af.Copy)
     for n, m, at in ((4, 12, 32), (14, 17, 48)):
         ts(kI(at, n), kF(16, n), -(m - 1) / 2.0, op.add, 1.0 / m, op.mult)
         ts(kF(at, n), kI(at, n), -m, op.mult)
@@ -293,13 +290,14 @@ def rank_program(g, core, T, topo):
     const(Z("Dd", 2), 2)
     const(Z("Dd", 2, 9), -30)
     const(A("cD", 0, 12), W)
-    ts(A("cD", 12, 24), A("cv"), DUMP, op.add)
-    const(A("cE", 0, 12), -(1 << 20))
-    sfill(A("cE", 12, 24), -OFF)
-    const(A("cE", 24, 36), 0)
+    act(A("cD", 12, 24), kF(16, 12), af.Copy, bias=float(DUMP))
+    const(A("cD", 24, 36), W)
+    const(A("cD", 36, 48), DUMP)
+    sfill(A("cE", 0, 12), -OFF)
+    const(A("cE", 12, 24), 0)
     for x in ("oS0", "oS1"):
         const(A(x, (0, 12), 16), 0)
-    fill(A("oV0", (0, 12), 16), -(1 << 30))
+    sfill(A("aV0", (0, 12), 16), -2.0 ** 30)
 
     def turn(x, t, s, out):
         n = x[4] // 16
@@ -324,20 +322,29 @@ def rank_program(g, core, T, topo):
     tt(A("VT", 0, Q), A("S3", (0, 12)), TXs[1], op.min)
     tt(TXs[2], A("VT", 0, Q), TXs[0], op.max)
     tt(A("X0", Q, 2 * Q), A("XL", 0, Q), TXs[2], op.add)
-    cp(rows("oV0"), turn(A("X0", Q, 2 * Q), "TV", "SM", "S2"))
+    cp(rows("sV"), turn(A("X0", Q, 2 * Q), "TV", "SM", "S2"))
+    act(rows("aV0"), A("S2", (0, 12)), af.Copy)
     sfill(A("XC", (0, 12), 16), -2 * BIG)
     for x in ("VT", "XL", "XS"):
         sfill(A(x, R17, R17 + 1), 0.0)
 
     def clist(t):
-        ts(A("sC"), rows("oV%d" % (t % 2)), 8191, op.bitwise_and)
+        ts(A("sC"), rows("sV"), 8191, op.bitwise_and)
         return lists("oC%d" % (t % 2), "sC")
     for x in clist(0):
         x["bonus"] = EARLY
 
+    pe = {}
+
     def yexp(p):
-        seq = [act(A("YE", 128 * a, 128 * b), A("y%d" % p), af.Copy, off=A("YL", 8 * a, 8 * b)) for a, b in YCH]
-        chain(seq)
+        seq = []
+        for j, (a, bank) in enumerate(YB):
+            def go(q, a=a, bank=bank):
+                for k in range(8):
+                    ins = q.matmul(A(bank, (k, 32, 8))[3], A("NE")[3], A("y%d" % p, 16 * a, 16 * a + 64)[3], k == 0, k == 7)
+                return ins
+            pe["%d" % j] = emit("t", go, [A("NE"), A("y%d" % p)], [A(bank)], FX + PE * 512)
+            seq.append(act(A("YE", 128 * a, 128 * a + 512), A(bank), af.Copy, scale=-1.0))
         seq[0]["bonus"] = BONUS
         return seq
 
@@ -350,165 +357,174 @@ def rank_program(g, core, T, topo):
     def weights(z):
         return [A(z, 15 - q, 143 - q) for q in range(16)]
 
-    def usum(p, t):
-        mms(A("MS", 0, 12), [(z, A("y%d" % p, q, Q, 16)) for q, z in enumerate(weights("Z1"))])
-        act(A("RLS", 15, Q, 16), A("MS", 0, 12), af.Copy)
-        act(LF(0), A("MS", 0, 12), af.Copy, scale=37.0, bias=float(t))
-        act(A("uF", 0, 12), A("MS", 0, 12), af.Copy)
-        act(A("uF", 12, 24), A("MS", 0, 12), af.Copy)
+    def usum(p):
+        pe["u"] = mms(A("MS", 0, 12), [(z, A("y%d" % p, q, Q, 16)) for q, z in enumerate(weights("Z1"))])
 
     chain(early + yexp(0)[1:])
-    usum(0, 0)
+    usum(0)
+    sbefore = []
     for t in range(TV):
         p, nxt = t % 2, t + 1
         last = nxt == TV
-        lL, lC, L, V = [("a%s%d" if t else "o%s%d") % (k, t) for k in "LCSV"]
-        order, diff, final = {"v": [], "s": [], "t": []}, {}, {x[0]: x for x in PLAN}
+        lL, lC, L = [("a%s%d" if t else "o%s%d") % (k, t) for k in "LCS"]
+        V = "aV%d" % t
+        LH = A("LH", (12 * t, 12 * t + 12))
+        const(LH, 8192)
+        emit("g", lambda q, x=A(L), o=LH: q.dma_start(o[3], x[3], accum_op=op.add), [A(L), LH], [LH], 0.3, sem="dA", inc=16, lat=3.0)
+        order, diff, final = {"v": [], "s": list(sbefore), "t": []}, {}, {x[0]: x for x in PLAN}
         mms(A("XL", 0, Q), [(A("ONE"), A("CL"))], last=False)
         mms(rows("XC"), [(A("ONE"), A("CC"))], last=False)
         for x in PLAN:
             kind, h, a, b = x
             ye, at = A("YE", 128 * a, 128 * b), (96 * h + 8 * a, 96 * h + 8 * b)
             if kind == "L":
-                diff["l", h, a] = span("D", h, a, b)
-                me = tt(diff["l", h, a], A("P"), ye, op.subtract, off=A(lL, *at))
+                diff[h, a] = span("D", h, a, b)
+                me = tt(diff[h, a], A("P"), ye, op.subtract, off=A(lL, *at))
             elif kind == "C":
                 me = tt(span("IC", h, a, b), A("P"), ye, op.is_gt, off=A(lC, *at))
-            elif kind[0] in "lc":
-                raw, lst = (span("LR", h, a, b), lL) if kind[0] == "l" else (span("CR", h, a, b), lC)
-                diff[kind[0], h, a] = ps = A("S" + kind[1], (0, 8 * (b - a)))
+            elif kind[0] == "l":
+                diff[h, a] = ps = A("S" + kind[1], (0, 8 * (b - a)))
                 mms(ps, [(A("NE"), ye)], last=False)
-                order["s"].append(act(raw, A("P"), af.Copy, off=A(lst, *at)))
-                me = mms(ps, [(A("EY"), raw)], first=False)
+                order["s"].append(act(span("LR", h, a, b), A("P"), af.Copy, off=A(lL, *at)))
+                me = mms(ps, [(A("EY"), span("LR", h, a, b))], first=False)
             elif kind == "abs":
-                me = act(piece("AB", h, a, b), diff["l", h, a], af.Abs)
+                me = act(piece("AB", h, a, b), diff[h, a], af.Abs)
             elif kind == "sign":
-                me = act(piece("SG", h, a, b), diff["l", h, a], af.Sign, bias=-0.5)
+                me = act(piece("SG", h, a, b), diff[h, a], af.Sign, bias=-0.5)
             elif kind == "over":
-                me = ts(piece("SG", h, a, b), diff["l", h, a], 0, op.is_gt)
-            elif kind == "said":
-                me = act(span("IC", h, a, b), diff["c", h, a], af.Sign, bias=-0.5)
+                me = ts(piece("SG", h, a, b), diff[h, a], 0, op.is_gt)
             elif kind == "XS":
                 me = mms(A("XS", 16 * a, 16 * b), [(z, A("AB", (a, b), (q, 256, 16))) for q, z in enumerate(weights("ZS"))])
             elif kind == "XL":
                 me = mms(A("XL", 16 * a, 16 * b), [(z, A("SG", (a, b), (q, 256, 16))) for q, z in enumerate(weights("ZL"))], False, x == final[kind])
             else:
                 lo, hi = span("IC", h, a, b)[1:3]
-                me = mms(A("XC", (a, b), (8 * h, 8 * h + 8)), [(z, A("IC", lo + q, hi, 16)) for q, z in enumerate(weights("ZC"))], False, x == final[kind])
+                part = sl(*{"XC": (0, 16), "XD": (0, 8), "XE": (8, 16)}[kind])
+                me = mms(A("XC", (a, b), (8 * h, 8 * h + 8)), [(z, A("IC", lo + q, hi, 16)) for q, z in enumerate(weights("ZC"))][part], False, x == PLAN[-1])
             order[me["e"]].append(me)
         for e in order:
             chain(order[e])
+        idle = [act(A("RLS", 15, Q, 16), A("MS", 0, 12), af.Copy), act(LF(0), A("MS", 0, 12), af.Copy, scale=37.0, bias=float(t))]
+        idle += [act(A("uF", 12 * j, 12 * j + 12), A("MS", 0, 12), af.Copy) for j in (0, 1)]
+        if t:
+            idle += [act(A("Bf", 12 * j, 12 * j + 12), A("MS", 48, 60), af.Sign, bias=(0.5 - 4 * j) * 2 ** 17) for j in (1, 2)]
+        chain(order["s"][-1:] + idle)
         RL = A("RLS", Q + 15, 2 * Q, 16)
         tt(A("mkL"), A("XL", 0, Q), rows(L), op.min)
         scan(A("RLS", Q, 2 * Q), A("DS"), A("mkL"), op.add, op.max)
         scan(A("RLS", 2 * Q, 3 * Q), A("DS"), A("XS", 0, Q), op.add, op.max)
-        cp(LI(0, 3), A("RLS", 15, 3 * Q, 16))
-        ts(LF(1), RL, 97.0 * t, op.add)
+        cp(LI(0, 2), A("RLS", 15, 2 * Q, 16))
+        cp(LI(2), A("RLS", 2 * Q + 15, 3 * Q, 16))
+        act(LF(1), RL, af.Identity, bias=97.0 * t)["bonus"] = 1.0
         ts(LI(3, 2), LI(0, 2), 4095, op.bitwise_and)
         tt(LI(7, 2), LI(3, 2), A("uF"), op.mult)
         ts(LI(9, 2), LI(7, 2), 5, op.arith_shift_right)
         tt(LI(11, 2), LI(9, 2), LF(0, 2), op.add)
-        ts(LI(13), LI(12), 3840, op.bitwise_and)
+        ts(LI(5), LI(12), 3840 - (1 << 31), op.bitwise_and)
         ts(LI(6), LI(11), 4095, op.bitwise_and)
-        tt(LI(5), LI(13), A("cv"), op.add)
         ts(LI(14, 2), LI(1, 2), 15 << 13, op.bitwise_and)
-        ts(A("GF"), A("RLS", Q, 2 * Q), 0, op.is_ge, off=A("GL", 0, 3))
-        tt(LF(2, 2), LI(14, 2), LI(5, 2), op.add)
-        tt(LF(5, 2), LI(4, 2), A("cD"), op.subtract)
-        tt(LF(4), LF(2), LF(3), op.subtract)
-        tt(LF(7, 3), LF(4, 3), A("GF", 0, 36), op.mult)
-        tt(Z("Dd", 0, 0), LF(7), LF(3), op.add)
+        act(A("GF", 32, 64), A("RLS", Q, 2 * Q), af.Sign, bias=0.5, off=A("GL", 0, 2))
+        flag = act(A("cv", 12, 24), A("GF", 32, 44), af.Identity, scale=-2.0 ** 19, bias=-2.0 ** 19)
+        act(A("GF", 0, 32), A("GF", 32, 64), af.Relu)
+        tt(LF(4, 2), LI(14, 2), A("cv"), op.add)
+        tt(LF(2, 2), LF(4, 2), LI(5, 2), op.add)
+        tt(Z("Dd", 0, 0), LF(2), LF(3), op.max)
+        tt(LF(6, 2), LI(4, 2), A("cD", 24, 48), op.subtract)
+        tt(LF(8, 2), LF(6, 2), A("GF", 0, 24), op.mult)
         act(Z("Dd", 1, 0), RL, af.Copy, bias=-4096.0 - 2.0 ** 20)
-        act(Z("Dd", 2, 0), RL, af.Relu, scale=-2.0 ** -19)
-        ts(A("tS"), rows(V), 17, op.arith_shift_right)
-        ts(rows("SLT"), A("tS"), 110 - 0.5 + 6.0 / 256, op.add, 2.0 ** 25, op.mult)
+        chain([act(Z("Dd", 2, 0), RL, af.Relu, scale=-2.0 ** -19)] + [steps(j) for j in range(nxt, TV)[:1]])
+        chain([flag, act(A("tB"), rows(V), af.Identity, scale=2.0 ** -17, bias=260 - 0.5 + 1.0 / 64)])
+        act(rows("SLT"), A("tB"), af.Identity, scale=2.0 ** 25, bias=(-150 - 0.5 + 6.0 / 256) * 2.0 ** 25)
         tt(rows("XC"), rows("XC"), rows(V), op.min)
         tt(A("mk"), A("XC", (0, 12), (0, 17)), A("SLT"), op.max)
         scan(A("RC"), A("DC%d" % p, 0, R17), A("mk"), op.add, op.max)
         RC = A("RC", 16, R17, 17)
-        ts(A("M", 1, 64 * 17, 17), A("RC"), -2 * OFF, op.is_lt, off=A("BL"))
+        ts(A("M", 1, 48 * 17, 17), A("RC"), -2 * OFF, op.is_lt, off=A("BL", 0, 3))
         if t:
+            chain([order["t"][-1], mms(A("MS", 32, 44), [(A("GW"), A("Bf", 0, 12))] + [(A("NW"), A("Bf", 12 * j, 12 * j + 12)) for j in (1, 2, 3)])])
             tt(LI(16), RC, A("MS", 32, 44), op.subtract)
         else:
             cp(LI(16), RC)
-        tt(LF(10, 2), LF(8, 2), Z("M", 3, 1, 2), op.mult)
-        tt(LF(5, 2), LF(10, 2), A("cD"), op.add)
-        cp(A("LST"), LF(5, 2))
+        tt(LF(10, 2), LF(8, 2), Z("M", 0, 1, 2), op.mult)
+        tt(LF(6, 2), LF(10, 2), A("cD", 0, 24), op.add)
+        cp(A("LST"), LF(6, 2))
         PL, NL = A("LST", 0, 12), A("LST", 12, 24)
-        yv, dy = A("y%d" % p), A("S3", (0, 12))
-        mms(dy, [(A("NE"), yv)], last=False)
-        act(A("pa"), A("P"), af.Copy, off=PL)
-        mms(dy, [(A("EY"), A("pa"))], first=False)
-        act(A("y%d" % (1 - p)), dy, af.Abs)
+        yv, dy = A("y%d" % p), rows("XC")
+        tail = {"p": act(A("pa"), A("P"), af.Copy, off=PL)}
+        mms(dy, [(A("NE"), yv), (A("EY"), A("pa"))])
+        tail["y"] = act(A("y%d" % (1 - p)), dy, af.Abs)
         if last:
-            tt(A("md"), A("P"), yv, op.min, off=PL)["bonus"] = BONUS
-            emit("v", lambda q, to=NL: q.tensor_copy(T.P[:, :].indirect(to[3]), T.md[:, :]), [A("md"), NL], [A("P")], 0.05 + 3.8 * CY * Q)["bonus"] = BONUS
+            tt(A("md"), A("P"), yv, op.min, off=PL)
         else:
-            act(A("nD"), dy, af.Relu, scale=-1.0)
-            act(A("md"), A("nD"), af.Copy, scale=-1.0)
+            pe["m"] = mms(dy, [(A("EY"), yv), (A("EY"), A("pa")), (A("NE"), A("y%d" % (1 - p)))])
+            tail["m"] = act(A("md"), dy, af.Copy, scale=0.5)
+        write = emit("v", lambda q, to=NL: q.tensor_copy(T.P[:, :].indirect(to[3]), T.md[:, :]), [A("md"), NL], [A("P")], 0.05 + 3.8 * CY * Q)
+        write["bonus"] = 2 * BONUS * last
         oS, oV, oB = ["o%s%d" % (k, nxt % 2) for k in "SVB"]
         ts(LI(17), LI(16), (1 << 20) + (1 << 17) - 1, op.bitwise_and)
         ts(LI(18), LI(16), (1 << 20) + (31 << 12), op.bitwise_and)
         ts(LI(19), LI(16), 20, op.arith_shift_right, 31, op.bitwise_and)
-        tt(Z("Dd", 0, 1, 3), LI(17, 3), A("cE"), op.add)
+        ts(Z("Dd", 0, 1), LI(17), -(1 << 20) - LOW, op.add)
+        tt(Z("Dd", 1, 1, 2), LI(18, 2), A("cE"), op.add)
         scan(A("VT", 0, R17), Z("M", 0), Z("Dd", 0), op.mult, op.add)
         zl = A("VT", 1, R17 + 1)
-        tt(zl, zl, A(L), op.subtract)
-        ts(zl, zl, HOT - 4096, op.max, HOT + 4096, op.min)
-        tt(A("sL"), zl, A(L), op.add)
+        tt(zl, zl, A(L), op.max)
+        tt(A("sL"), zl, LH, op.min)
         ts(rows(oS), rows("sL"), 4095, op.bitwise_and)
         way = []
         if not last:
             way = lists("oL%d" % (nxt % 2), oS)[:1]
             sends = [send("L", nxt, 2.4), send("S", nxt, 4.0)]
             sends[0]["bonus"] = LBON
-        for x, j in (("XS", 1), ("XL", 2)):
-            chain(way + [scan(A(x, 0, R17), Z("M", j), Z("Dd", j), op.mult, op.add)])
+        chain(way + [scan(A(x, 0, R17), Z("M", j), Z("Dd", j), op.mult, op.add) for x, j in (("XL", 2), ("XS", 1))])
         zn, zr = A("XS", 1, R17 + 1), A("XL", 1, R17 + 1)
+        tt(zn, zn, A(V), op.subtract)
         if last:
             ts(A("VT", 256, 256 + R17), zr, 14, op.is_equal, 2.0 ** 17, op.mult)
             tt(A(oB), A("VT", 256, 256 + R17), A(V), op.add)
+            ts(A("hot"), zr, 15, op.is_equal)
         else:
-            ts(A(oB), zr, 14, op.is_equal, 2.0 ** 17, op.mult)
-        tt(zn, zn, A(V), op.subtract)
-        ts(A("hot"), zr, 15, op.is_equal)
+            ts(A("hot"), zr, 15, op.is_equal)
+            ts(A("bp"), zr, 14, op.is_equal, 2.0 ** 17, op.mult)
         tt(zn, zn, A("hot"), op.mult)
-        tt(A(oV), zn, A(oB if last else V), op.add)
+        tt(A("sV"), zn, A(oB if last else V), op.add)
         if last:
             break
-        emit("v", lambda q, to=NL, y=yv: q.tensor_tensor(T.P[:, :].indirect(to[3]), T.md[:, :], y[3], op.add), [A("md"), yv, NL], [A("P")], 0.05 + 3.8 * CY * Q)
+        tail["v"] = act(A(oV), zn, af.Copy)
         clist(nxt)
-        chain(sends + [send("C", nxt, 2.4), send("V", nxt, VLAT, A(oB))])
-        chain(yexp(1 - p) + [steps(nxt)])
-        act(A("Bf", 0, 12), Z("M", 0, 1), af.Copy, scale=-1.0, bias=1.0)
-        mms(A("MS", 16, 28), [(A("GW"), A("Bf", 0, 12))])
-        act(A("Bf", 12, 24), A("MS", 16, 28), af.Sign, bias=-3.5 * 2 ** 17)
-        act(A("Bf", 24, 36), A("MS", 16, 28), af.Sign, bias=-7.5 * 2 ** 17)
-        mms(A("MS", 32, 44), [(A("GW"), A("Bf", 0, 12))] + [(A("NW"), A("Bf", 12 * j, 12 * j + 12)) for j in (1, 2, 3)])
-        usum(1 - p, nxt)
+        emit("y", lambda q, o=A(oB), i=A(V): q.dma_start(o[3], i[3]), [A(V)], [A(oB)], 0.05, sem="dC%d" % nxt, inc=16, lat=2.5)
+        sends.append(emit("g", lambda q, o=A(oB): q.dma_start(o[3], A("bp")[3], accum_op=op.add), [A("bp"), A(oB)], [A(oB)], 0.3, sem="dB%d" % nxt, inc=16, lat=2.5))
+        chain(sends + [send("C", nxt, 2.4), send("V", nxt, VLAT, [A(oB)])])
+        for j, x in enumerate(yexp(1 - p)):
+            tail["%d" % j] = x
+        tail["B"] = act(A("Bf", 0, 12), Z("M", 0, 1), af.Copy, scale=-1.0, bias=1.0)
+        mms(A("MS", 48, 60), [(A("GW"), A("Bf", 0, 12))])
+        usum(1 - p)
+        chain([pe[k] for k in TT.split()])
+        sbefore = [tail[k] for k in TAIL.split()]
 
     dma("y", T.zp[:, :], T.P[:, 0:W], [A("P", 0, W)], [], 6.0)
     dma("y", T.zy[:, :], T["y%d" % (TV % 2)][:, :], [A("y%d" % (TV % 2))], [], 2.0)
-    TB = A("VT", 0, Q)
+    TB, TC = A("VT", 0, Q), A("VT", 256, 256 + Q)
     for j in range(4):
         chain([order["s"][-1], act(A("BM", j), A("SM", j), af.Copy)])
-    cp(A("X0", 0, Q), rows(oS))["bonus"] = 2 * TURN
+    cp(A("X0", 0, Q), rows(oS))
     act(A("E0", 0, Q), turn(A("X0", 0, Q), "TL", "SM", "S1"), af.Copy)
     dma("y", T.zl[:, :], T.E0[:, 0:Q], [A("E0", 0, Q)], [], 2.0)
-    ts(A("tF"), rows(oV), 8191, op.bitwise_and)
+    ts(A("tF"), rows("sV"), 8191, op.bitwise_and)
     ts(TB, A("tF"), 4096, op.is_ge, -8192, op.mult)
-    tt(A("X0", Q, 2 * Q), TB, A("tF"), op.add)["bonus"] = TURN
-    act(TXs[0], turn(A("X0", Q, 2 * Q), "TV", "SM", "S2"), af.Relu, bias=1.0)
-    act(A("E0", Q, 2 * Q), TXs[0], af.Copy, bias=-1.0)
+    tt(A("X0", Q, 2 * Q), TB, A("tF"), op.add)
+    ts(A("E0", Q, 2 * Q), turn(A("X0", Q, 2 * Q), "TV", "SM", "S2"), -1, op.max)
     dma("y", T.zc[:, :], T.E0[:, Q:2 * Q], [A("E0", Q, 2 * Q)], [], 2.0)
-    ts(A("tS"), rows(oV), 13, op.arith_shift_right, 15, op.bitwise_and)
+    ts(A("tS"), rows("sV"), 13, op.arith_shift_right, 15, op.bitwise_and)
     ts(A("X1", 0, Q), A("tS"), -1, op.mult, 15, op.add)
-    ts(A("sC"), rows(oV), 17, op.arith_shift_right, 7, op.bitwise_and)
-    ts(TB, A("tF"), -4096, op.add, 0, op.max)
-    tt(A("X1", Q, 2 * Q), TB, A("sC"), op.add)
-    act(A("oB"), turn(A("X1"), "TO", "BM", "S3"), af.Copy)
-    dma("y", T.zo[:, :], T.oB[:, 0:Q], [A("oB", 0, Q)], [], 2.0)
-    dma("s", T.zb[:, :], T.oB[:, Q:2 * Q], [A("oB", Q, 2 * Q)], [], 2.0)
+    act(A("oB", 0, Q), turn(A("X1", 0, Q), "TO", "BM", "S3"), af.Copy)
+    dma("s", T.zo[:, :], T.oB[:, 0:Q], [A("oB", 0, Q)], [], 2.0)
+    ts(A("sC"), rows("sV"), 17, op.arith_shift_right, 7, op.bitwise_and)
+    ts(TC, A("tF"), -4096, op.add, 0, op.max)
+    tt(A("X1", Q, 2 * Q), TC, A("sC"), op.add)
+    act(A("oB", Q, 2 * Q), turn(A("X1", Q, 2 * Q), "TP", "BM", "S1"), af.Copy)
+    dma("y", T.zb[:, :], T.oB[:, Q:2 * Q], [A("oB", Q, 2 * Q)], [], 2.0)
 
     succ = [[] for _ in ops]
     for o in ops:
@@ -516,8 +532,14 @@ def rank_program(g, core, T, topo):
         o["all"] = list({x["i"]: x for x in o["need"] + o["soft"]}.values())
         for x in o["all"]:
             succ[x["i"]].append(o)
-    for o in reversed(ops):
-        o["pri"] = o["bonus"] + o["cost"] + o["lat"] + max([0.0] + [s["pri"] + WK for s in succ[o["i"]]])
+    left, line = {o["i"]: len(o["all"]) for o in ops}, [o for o in ops if not o["all"]]
+    for o in line:
+        for s in succ[o["i"]]:
+            left[s["i"]] -= 1
+            if not left[s["i"]]:
+                line.append(s)
+    for o in reversed(line):
+        o["pri"] = o["bonus"] + o["cost"] + o["lat"] + max([0.0] + [s["pri"] + (WK if s["e"] == o["e"] else WX) for s in succ[o["i"]]])
     left = {o["i"]: len(o["all"]) for o in ops}
     free = {e: 0.0 for e in list(queues) + ["net"]}
     ready = {e: [] for e in free}
@@ -541,7 +563,7 @@ def rank_program(g, core, T, topo):
         for s in succ[o["i"]]:
             left[s["i"]] -= 1
             if not left[s["i"]]:
-                ready[s["e"]].append((max([0.0] + [x["fin"] + WK for x in s["need"]] + [x["st"] + x["cost"] for x in s["soft"]]), s))
+                ready[s["e"]].append((max([0.0] + [x["fin"] + (WK if s["e"] == x["e"] else WX) for x in s["need"]] + [x["st"] + x["cost"] for x in s["soft"]]), s))
     count = {}
     clock = {e: {} for e in queues}
     for o in done:

@@ -7,58 +7,55 @@ NPOS = 16 * Q
 HALF = NPOS // 2
 PW = 4304
 DUMP = 4112
-R17 = 12 * 17
-PLAN = [("l1", 0, 4, 8), ("l2", 0, 8, 12), ("L", 0, 0, 4), ("L", 1, 0, 4), ("over", 0, 0, 4), ("over", 1, 0, 4), ("XL", 0, 0, 4), ("abs", 0, 0, 4), ("abs", 1, 0, 4), ("XS", 0, 0, 4), ("l3", 1, 8, 12), ("L", 1, 4, 8), ("over", 1, 4, 8), ("sign", 0, 4, 8), ("XL", 0, 4, 8), ("abs", 0, 4, 8), ("abs", 1, 4, 8), ("XS", 0, 4, 8), ("C", 0, 0, 12), ("sign", 0, 8, 12), ("sign", 1, 8, 12), ("XD", 0, 0, 12), ("XL", 0, 8, 12), ("XE", 0, 0, 12), ("abs", 0, 8, 12), ("abs", 1, 8, 12), ("XS", 0, 8, 12), ("C", 1, 0, 12), ("XC", 1, 0, 12)]
-YB = [(0, "S1"), (4, "S3"), (8, "S2")]
-TAIL = "B p y 0 m 1 2 v"
-TT = "0 m 1 2 u"
+R17, R18 = 12 * 17, 12 * 18
+PLAN = [("l1", 0, 8, 12), ("l2", 1, 8, 12), ("sign", 0, 8, 12), ("sign", 1, 8, 12), ("L", 0, 0, 4), ("L", 0, 4, 8), ("L", 1, 0, 4), ("L", 1, 4, 8),
+        ("sign", 0, 0, 4), ("over", 1, 0, 4), ("over", 0, 4, 8), ("over", 1, 4, 8), ("XL", 0, 8, 12), ("XL", 0, 0, 4), ("XL", 0, 4, 8),
+        ("c3", 0, 8, 12), ("csign", 0, 8, 12), ("c4", 1, 8, 12), ("csign", 1, 8, 12), ("C", 0, 0, 4), ("C", 0, 4, 8), ("C", 1, 0, 4), ("C", 1, 4, 8), ("XC", 0, 0, 12), ("XC", 1, 0, 12),
+        ("abs", 0, 8, 12), ("abs", 1, 8, 12), ("abs", 0, 0, 4), ("abs", 0, 4, 8), ("abs", 1, 0, 4), ("abs", 1, 4, 8), ("XS", 0, 8, 12), ("XS", 0, 0, 4), ("XS", 0, 4, 8)]
+YB = [(0, 4, "S1"), (4, 8, "S2")]
+ORDER = {
+    "v": "L10 L00 word L04 cz gz name over10 wL az list0 L14 list1 lz wz over04 over14 N min overN C00 C04 C14 C10 mkL lL0 mkN lL1 scanL cpu cmin and2 mk mul rc shf k16 nb add a2 a23 a1 n5 m6 "
+         "of conv2 conv m7 an wC adr scanS LST cps d cod md0 w2 end md w0 cmn z out andC write lC1 lC0",
+    "s": "l18 abs10 sign00 abs00 AL sign08 DL fz c08 sign18 c18 csign08 abs04 u csign18 r0 absN r uu u37 r1 abs08 a97 abs18 G abs14 B flag A D1 y y0 b4+ y4 l08+",
+    "t": "el08 nl18 nc08 XL00 el18 tE XL04 nc18 ec08 XL08 ec18 xL XC00 xS XC10 slot XS00 kC+ XS08 bb XS04 kL+ tB tV tD ty0 ty4 nl08+ tw+ tL+",
+    "g": "sendL sendZ nL1+ nL0+ sendC gV sendV"}
 BIG = 2.0 ** 33
-OFF = 2.0 ** 24
-LOW = 30 * 4096
+KEEP = 10 << 16
+MID = 15 << 19
 
 F32, BF, I32, U16 = "float32", "bfloat16", "int32", "uint16"
 SCRATCH = {}
 for _n, _w, _d in (
-        ("P", PW, BF), ("D", NPOS, BF), ("AB", [12, 256], BF), ("SG", [12, 256], BF), ("IC", NPOS, BF), ("y0", Q, BF), ("y1", Q, BF),
-        ("YE", HALF, BF), ("LR", NPOS, BF), ("GL", 4, U16), ("BL", 4, U16), ("EL", 14, U16),
+        ("P", PW, BF), ("D", NPOS, BF), ("AB", [12, 272], BF), ("SG", [15, 272], BF), ("IC", NPOS, BF),
+        ("YE", HALF, BF), ("LR", NPOS, BF), ("CR", NPOS, BF), ("BL", 2, U16),
         ("inL", Q, I32), ("inC", Q, I32), ("inO", Q, BF), ("inB", Q, BF), ("inLim", 8, I32), ("limF", 8, F32),
-        ("CL", [12, 16], BF), ("CC", [12, 16], BF), ("ONE", 128, BF),
-        ("ZF", 144, BF), ("Z1", 144, BF), ("ZL", 144, BF), ("ZC", 144, BF), ("ZS", 144, BF),
+        ("CL", [15, 17], BF), ("CC", [12, 16], BF), ("ONE", 128, BF), ("CK", R17, BF), ("I2", 128, F32),
+        ("ZF", 144, BF), ("ZL", 144, BF), ("ZC", 144, BF), ("ZS", 144, BF),
         ("GW", 128, BF), ("NW", 128, BF), ("BO", 128, BF), ("EY", 128, BF), ("NE", 128, BF),
-        ("PM", 24, BF), ("PM1", 144, BF), ("CT", 144, F32), ("LT", 144, F32),
-        ("ID", 160, F32), ("SM", [4, 128], F32), ("BM", [4, 128], BF),
+        ("PM", 24, BF), ("PM1", 102, BF), ("CT", 102, F32), ("DC", [TV, R17], F32),
+        ("ID", 160, F32), ("SM", [4, 128], F32),
         ("mpI", 160, I32), ("gI", 128, I32), ("sI", 96, I32), ("KX", 256, I32), ("kI", 128, I32), ("kF", 128, F32),
-        ("cv", 24, F32), ("cD", 48, F32), ("cE", 24, F32), ("X0", 384, F32), ("X1", 384, BF), ("E0", 384, F32), ("oB", 384, BF), ("TX", 3 * Q, F32), ("tF", Q, I32),
-        ("TL", [12, 16], F32), ("TV", [12, 16], F32), ("TO", [12, 16], BF), ("TP", [12, 16], BF), ("LH", [72, 17], I32),
-        ("DS", Q, F32), ("mkL", Q, F32), ("mk", R17, F32), ("RLS", 3 * Q, F32), ("RC", R17, F32),
-        ("tS", Q, I32), ("tB", Q, BF), ("aV0", [12, 17], F32), ("sV", [12, 17], I32), ("bp", [12, 17], F32), ("SLT", [12, 17], F32), ("hot", R17, F32),
-        ("sL", [12, 17], I32), ("sC", [12, 16], I32), ("M", 48 * 17, F32), ("Dd", 36 * 17, F32), ("GF", 64, F32),
-        ("LI", 240, I32), ("LF", 144, F32), ("uF", 24, F32), ("Bf", 48, BF), ("LST", 24, U16), ("pa", Q, BF), ("md", Q, BF)):
+        ("cB", 24, BF), ("cD", 24, F32), ("X0", 384, F32), ("X1", 384, BF), ("E0", 384, F32), ("oB", 384, BF), ("TX", 3 * Q, F32),
+        ("TL", [12, 16], F32), ("TV", [12, 16], F32),
+        ("DS", 2 * R17, F32), ("mkL", R17, F32), ("mk", R17, F32), ("RLS", 2 * R17, F32), ("RS", R17, F32), ("RC", R17, F32),
+        ("tS", Q, I32), ("rF", [12, 17], F32), ("sV", [12, 16], I32), ("D1", Q, BF), ("zC", [12, 18], F32), ("wC", R18 + 2, F32),
+        ("ML", Q, F32), ("DdL", Q, F32), ("wL", Q, F32), ("zL", Q, F32), ("DL", [12, 17], BF), ("Lf", [12, 16], F32), ("L2", [12, 17], F32),
+        ("DN", Q, BF), ("rB", [12, 17], BF), ("NL", 12, U16), ("sC", [12, 16], I32), ("M", 6 + 32 * 18, F32), ("uF", 32, F32),
+        ("LI", 336, I32), ("LF", 96, F32), ("Bf", 48, BF), ("LST", 24, U16), ("pa", Q, BF), ("md", Q, BF)):
     SCRATCH[_n] = ("sbuf", [128] + (_w if isinstance(_w, list) else [_w]), _d)
-for _n in ("XL", "XS", "VT", "MS"):
+for _n in ("XL", "XS", "MS"):
     SCRATCH[_n] = ("psum", [128, 512], F32)
 SCRATCH["XC"] = ("psum", [128, 16, 32], F32)
-for _n in ("S1", "S2", "S3"):
+for _n in ("S1", "S2", "S3", "S4"):
     SCRATCH[_n] = ("psum", [128, 32, 16], F32)
 for _t in range(TV):
-    SCRATCH["DC%d" % (_t % 2)] = ("sbuf", [128, 208], F32)
-    for _k in "LC":
-        SCRATCH["o%s%d" % (_k, _t % 2)] = ("sbuf", [128, Q], U16)
-    for _k, _d in (("S", I32), ("V", F32), ("B", F32)):
-        SCRATCH["o%s%d" % (_k, _t % 2)] = ("sbuf", [128, 12, 17], _d)
-    if _t:
-        for _k in "LC":
-            SCRATCH["a%s%d" % (_k, _t)] = ("sbuf", [128, Q], U16)
-        for _k, _d in (("S", I32), ("V", F32)):
-            SCRATCH["a%s%d" % (_k, _t)] = ("sbuf", [128, 12, 17], _d)
-SEMAPHORES = (["sv", "ss", "st", "sg", "dA"] + ["d%s%d" % (k, t) for k in "BC" for t in range(1, TV)] + ["l" + k + i for k in "LCSV" for i in "01"] + ["d%d" % i for i in range(16)]
-              + ["q%s%d" % (k, t) for k in "LCSV" for t in range(1, TV)])
-CY, PE, FX, FS, WK, WX = 0.00085, 0.00062, 0.04, 0.06, 0.06, 0.12
-BONUS = 4.0
-LBON = 1.5
+    for _k, _w, _d in (("V", [12, 17], F32), ("Z", [36], F32), ("L", [Q], U16), ("C", [Q], U16)):
+        SCRATCH["o%s%d" % (_k, _t % 2)] = SCRATCH["a%s%d" % (_k, _t)] = ("sbuf", [128] + _w, _d)
+SEMAPHORES = (["sv", "ss", "st", "sg"] + ["l" + k + i for k in "CVLZ" for i in "01"] + ["d%d" % i for i in range(16)]
+              + ["q%s%d" % (k, t) for k in "CVLZ" for t in range(1, TV)])
+CY, PE, FX, FS, WK, WX = 0.00093, 0.0005, 0.04, 0.06, 0.06, 0.12
 EARLY = 10.0
 PLAT = 7.0
-VLAT = 6.0
 
 
 def rank_program(g, core, T, topo):
@@ -86,19 +83,19 @@ def rank_program(g, core, T, topo):
         at = np.arange(int(np.prod(shape))).reshape(shape)[ix].reshape(-1)
         return (name, int(at.min()), int(at.max()) + 1, T[name][(sl(None),) + ix], len(at), frozenset(at.tolist()))
 
-    def meet(x, y, e):
-        if y[1]["e"] == e or (x[0] not in psum and e in "vst" and y[1]["e"] in "vst"):
+    def meet(x, y, e, computes):
+        if y[1]["e"] == e or (x[0] not in psum and computes and y[1]["inc"] == 1):
             return x[1] < y[0][2] and y[0][1] < x[2] and not x[5].isdisjoint(y[0][5])
         return x[0] in psum or (x[1] < y[0][2] and y[0][1] < x[2])
 
     def emit(e, fn, R, Wt, cost, sem=None, inc=1, lat=0.0):
         need = []
         for x in R:
-            need += [y[1] for y in wr.get(x[0], []) if meet(x, y, e)]
+            need += [y[1] for y in wr.get(x[0], []) if meet(x, y, e, inc == 1)]
             if x[0] in psum:
                 need += [y[1] for y in rd.get(x[0], []) if y[1]["e"] != e]
         for x in Wt:
-            need += [y[1] for y in wr.get(x[0], []) + rd.get(x[0], []) if meet(x, y, e)]
+            need += [y[1] for y in wr.get(x[0], []) + rd.get(x[0], []) if meet(x, y, e, inc == 1)]
         me = {"e": e, "fn": fn, "need": need, "cost": cost, "sem": sem or semof.get(e), "inc": inc, "lat": lat, "i": len(ops), "soft": [], "bonus": 0.0}
         ops.append(me)
         for x in Wt:
@@ -158,15 +155,19 @@ def rank_program(g, core, T, topo):
     def const(o, c):
         return iota(o, [[0, o[4]]], c)
 
-    def mms(o, terms, first=True, last=True):
-        R = [x for t in terms for x in t]
+    def gcopy(o, i):
+        return emit("g", lambda q: q.affine_select(o[3], i[3], [[0, o[4]]], op.is_ge, 0.0, 0, 0), [i], [o], 0.17 + 2 * CY * o[4])
 
+    def mmx(terms, first=True, last=True):
         def go(q):
-            for j, (l, r) in enumerate(terms):
+            for j, (o, l, r) in enumerate(terms):
                 ins = q.matmul(o[3], l[3], r[3], first and j == 0, last and j == len(terms) - 1)
             return ins
-        k = 4 if SCRATCH[terms[0][0][0]][2] == F32 else 1
-        return emit("t", go, R, [o], FX + PE * k * max(64, o[4]) * len(terms))
+        return emit("t", go, [x for t in terms for x in t[1:]], list({t[0][1:3]: t[0] for t in terms}.values()),
+                    FX + PE * sum(max(64, o[4]) * (4 if SCRATCH[l[0]][2] == F32 else 1) for o, l, r in terms))
+
+    def mms(o, terms, first=True, last=True):
+        return mmx([(o, l, r) for l, r in terms], first, last)
 
     nd = [0]
 
@@ -185,24 +186,22 @@ def rank_program(g, core, T, topo):
     def LF(j, n=1):
         return A("LF", 12 * j, 12 * (j + n))
 
-    def send(k, nxt, lat, more=()):
+    def send(k, nxt, lat):
         o, i, s, r = A("a%s%d" % (k, nxt)), A("o%s%d" % (k, nxt % 2)), "l%s%d" % (k, nxt % 2), "q%s%d" % (k, nxt)
-        if more:
-            tr = [RemoteDMATransfer(dst_ids=[DstId(rid=rid, pnc=pid)], dma_engine_mask=emask, remote_sem=T.sem[r], srcs=[i[3]] + [x[3] for x in more], dsts=[o[3]], alu_op=1)]
-            me = emit("g", lambda q: q.remote_dma_fused(tr, local_sem=T.sem[s]), [i] + more, [], 0.6, sem=s, inc=-neng, lat=lat)
-        else:
-            me = emit("g", lambda q: q.remote_dma(out_ap=o[3], in_ap=i[3], remote_sem=T.sem[r], local_sem=T.sem[s],
-                                                  pid=pid, routing_id=rid, dma_engine_mask=emask), [i], [], 0.6, sem=s, inc=-neng, lat=lat)
+        me = emit("g", lambda q: q.remote_dma(out_ap=o[3], in_ap=i[3], remote_sem=T.sem[r], local_sem=T.sem[s],
+                                              pid=pid, routing_id=rid, dma_engine_mask=emask), [i], [], 0.6, sem=s, inc=-neng, lat=lat)
         net = {"e": "net", "need": [me], "cost": 0.0, "sem": r, "v": neng, "inc": 0, "lat": 0.0, "i": len(ops), "soft": [], "bonus": 0.0}
         ops.append(net)
-        wr[o[0]] = [(o, net)]
+        wr.setdefault(o[0], []).append((o, net))
         return me
 
     chain([dma("y", T.inL[:, :], T.lem[:, :], [], [A("inL")], 2.2),
            dma("y", T.inC[:, :], T.con[:, :], [], [A("inC")], 2.2),
            dma("y", T.P[:, 0:W], T.prop[:, :], [], [A("P", 0, W)], PLAT),
            dma("y", T.inLim[:, 0:TV], T.lim[:, :], [], [A("inLim", 0, TV)], 2.2)])
-    chain([dma("s", T.y0[:, :], T.ex[:, :], [], [A("y0")], 2.2),
+    def Y(p, a=0, b=12):
+        return A("SG", 14 - 14 * p, (16 * a, 16 * b))
+    chain([dma("s", Y(0)[3], T.ex[:, :], [], [Y(0)], 2.2),
            dma("s", T.inO[:, :], T.org[:, :], [], [A("inO")], 2.2),
            dma("s", T.inB[:, :], T.cnt[:, :], [], [A("inB")], 2.2)])
 
@@ -212,8 +211,8 @@ def rank_program(g, core, T, topo):
     def kF(a, n=1):
         return A("kF", a, a + n)
 
-    def rows(x):
-        return A(x, (0, 12), (0, 16))
+    def rows(x, n=16):
+        return A(x, (0, 12), (0, n))
     iota(A("mpI"), [[1, 160]], -16, -1)
     iota(A("sI", 0, 1), [[0, 1]], 0, 1)
     iota(A("sI", 16, 25), [[-16, 9]], 0, 1)
@@ -221,83 +220,95 @@ def rank_program(g, core, T, topo):
     iota(A("sI", 48, 72), [[1, 24]], 0)
     iota(A("gI"), [[16, 8], [0, 16]], 15, -1)
     b0, b1, qF = kF(0), kF(1), kF(2)
-    fill(A("X1", 0, Q), 0.0)
+    fill(A("X1", 0, R18), 0.0)
     ts(kI(0), A("sI", 0, 1), 16, op.bitwise_and)
     ts(kI(1), A("sI", 0, 1), 15, op.bitwise_and)
     ts(b0, kI(0), 0, op.is_equal)
     ts(b1, kI(0), 16, op.is_equal)
     cp(qF, kI(1))
     ts(A("ID"), A("mpI"), 0, op.is_equal)
+    IDF = A("ID", 16, 144)
     for j, (at, b) in enumerate(((16, b0), (0, b0), (32, b1), (16, b1))):
         act(A("SM", j), A("ID", at, at + 128), af.Copy, scale=b)
     ts(kI(16, 9), A("sI", 16, 25), 4, op.arith_shift_right)
     fill(A("ZF"), 0.0)
     ts(A("ZF", 15, 144, 16), kI(16, 9), 0, op.is_equal)
-    for z, s in (("Z1", 1.0), ("ZL", 2.0 ** 26), ("ZS", -2.0 ** 17), ("ZC", 2.0 ** 31)):
+    for z, s in (("ZL", 2.0 ** 27), ("ZS", -2.0 ** 17), ("ZC", 2.0 ** 31)):
         act(A(z), A("ZF"), af.Copy, scale=s)
-    act(A("EY"), A("ID", 16, 144), af.Copy)
+    act(A("EY"), IDF, af.Copy)
     act(A("NE"), A("EY"), af.Copy, scale=-1.0)
     act(A("NW"), A("EY"), af.Copy, scale=-2.0 ** 18)
-    const(A("Bf", 36, 48), 2)
-    sfill(A("ONE"), 1.0 / 128)
-    sfill(A("CL"), 2.0 ** 26)
-    sfill(A("CC"), -7.5 * 2.0 ** 31)
+    act(A("I2"), A("EY"), af.Copy, scale=2.0)
+    const(A("Bf", 36, 48), -130)
+    fill(A("ONE"), 1.0 / 128)
+    fill(A("CL", (1, 14)), -7.5 * 2.0 ** 27)
+    const(A("CL", (0, 15, 14)), 0)
+    fill(A("CC"), -7.5 * 2.0 ** 31)
     for kind, h, a, b in PLAN:
-        if kind == "over":
-            sfill(A("CL", (a, b), (8 * h, 8 * h + 8)), -7.5 * 2.0 ** 26)
+        if kind == "sign":
+            fill(A("CL", (a + 1, b + 1), (8 * h, 8 * h + 8)), 2.0 ** 27)
+        if kind == "csign":
+            fill(A("CC", (a, b), (8 * h, 8 * h + 8)), 2.0 ** 31)
+    const(A("CK"), 6 << 16)
     ts(A("KX", 0, 128), A("mpI", 16, 144), 15, op.bitwise_and)
-    ts(A("GW"), A("KX", 0, 128), 0, op.is_equal, 2.0 ** 17, op.mult)
+    ts(A("GW"), A("KX", 0, 128), 0, op.is_equal, 2.0 ** -4, op.mult)
     ts(A("KX", 128, 256), A("gI"), 4, op.arith_shift_right)
-    ts(A("BO"), A("KX", 128, 256), 0, op.is_equal, 2.0 ** 17, op.mult)
+    ts(A("BO"), A("KX", 128, 256), 0, op.is_equal, 2.0 ** 16, op.mult)
     const(A("P", W, PW), 0)
+    const(A("P", DUMP - 1, DUMP), -(1 << 20))
 
-    ts(kF(16, 14), A("sI", 32, 46), qF, op.add)
-    act(A("cv", 0, 12), kF(16, 12), af.Copy)
-    for n, m, at in ((4, 12, 32), (14, 17, 48)):
-        ts(kI(at, n), kF(16, n), -(m - 1) / 2.0, op.add, 1.0 / m, op.mult)
-        ts(kF(at, n), kI(at, n), -m, op.mult)
-        tt(kF(at + 32, n), kF(at, n), kF(16, n), op.add)
-    ts(A("GL"), kF(64, 4), 16, op.mult, 15, op.add)
-    ts(A("BL"), kF(64, 4), 17, op.mult, 16, op.add)
-    cp(A("EL"), kF(80, 14))
+    ts(kF(16, 12), A("sI", 32, 44), qF, op.add)
+    const(A("cB", 0, 12), 0)
+    act(A("cB", 12, 24), kF(16, 12), af.Copy)
+    ts(kI(32, 2), kF(16, 2), -5.5, op.add, 1.0 / 12, op.mult)
+    ts(kF(32, 2), kI(32, 2), -12, op.mult)
+    tt(kF(64, 2), kF(32, 2), kF(16, 2), op.add)
+    ts(A("BL"), kF(64, 2), 17, op.mult, 16, op.add)
 
     const(A("DS"), 8192)
-    sfill(A("DS", 0, Q, 16), -BIG)
-    sfill(A("SLT", (0, 12), 16), -2 * BIG)
+    const(A("DS", 16, R17, 17), 0)
+    const(A("DS", R17 + 16, 2 * R17, 17), -15 << 17)
+    sfill(A("DS", 0, 2 * R17, 17), -BIG)
     cp(A("limF", 0, TV), A("inLim", 0, TV))
-    ts(kF(96, 24), A("sI", 48, 72), qF, op.subtract)
-    ts(A("TX", 0, 24), kF(96, 24), 0, op.is_equal)
-    ts(A("TX", 24, 48), kF(96, 24), 1, op.is_equal)
-    tt(A("PM"), A("TX", 0, 24), A("TX", 24, 48), op.subtract)
+    ts(kF(96, 17), A("sI", 48, 65), qF, op.subtract)
+    ts(A("TX", 0, 17), kF(96, 17), 0, op.is_equal)
+    ts(A("TX", 24, 41), kF(96, 17), 1, op.is_equal)
+    tt(A("PM", 0, 17), A("TX", 0, 17), A("TX", 24, 41), op.subtract)
     for t in range(TV):
-        act(A("PM1", 24 * t, 24 * t + 24), A("PM"), af.Copy, scale=A("limF", t, t + 1))
-    mms(A("MS", 64, 208), [(A("BO"), A("PM1"))])
-    const(A("CT"), 1 << 21)
-    const(A("CT", 16, 144, 24), (8 << 17) + 4096)
-    sfill(A("CT", 0, 144, 24), -BIG)
-    tt(A("LT"), A("MS", 64, 208), A("CT"), op.add)
-
-    def steps(t):
-        return act(A("DC%d" % (t % 2)), A("LT", 24 * t, 24 * t + 24), af.Copy, off=A("EL", 0, 13))
-    steps(0)["bonus"] = EARLY
+        act(A("PM1", 17 * t, 17 * t + 17), A("PM", 0, 17), af.Copy, scale=A("limF", t, t + 1))
+    mms(A("XL", 256, 358), [(A("BO"), A("PM1"))])
+    const(A("CT"), 1 << 20)
+    const(A("CT", 16, 102, 17), 8 << 16)
+    sfill(A("CT", 0, 102, 17), -BIG)
+    tt(A("DC", (0, TV), (0, 17)), A("XL", 256, 358), A("CT"), op.add)
+    for a, b in ((17, 34), (34, 68), (68, 136), (136, 204)):
+        gcopy(A("DC", (0, TV), (a, b)), A("DC", (0, TV), (0, b - a)))
 
     def Z(x, j, c=None, n=1):
-        return A(x, R17 * j, R17 * (j + n)) if c is None else A(x, R17 * j + c, R17 * (j + n), 17)
-    const(Z("M", 0, None, 3), 1)
-    const(Z("M", 0, 0, 3), 0)
-    const(Z("Dd", 0), 8192)
-    const(Z("Dd", 1), 0)
-    const(Z("Dd", 2), 2)
-    const(Z("Dd", 2, 9), -30)
+        x, at = ("MS", 80 + R18 * j) if x == "Dd" else (x, 6 + R18 * j)
+        if c is None:
+            return A(x, at, at + R18) if j else A(x, at - 5, at + R18 - 5, 6)
+        return A(x, at + c, at + c + R18 * n - 17, 18)
+    const(A("M", 0, 6 + 2 * R18), 1)
+    const(Z("M", 0, -5), 0)
+    const(Z("M", 1, 0), 0)
+    sfill(Z("Dd", 0, 7), -2.0 ** 20)
+    sfill(Z("Dd", 1), 2.0 ** 20)
+    const(A("ML"), 1)
+    const(A("ML", 0, Q, 16), 0)
+    const(A("DdL"), 8192)
+    const(A("DL"), 0)
+    const(A("DL", (0, 12), 16), 8192)
+    const(A("L2", (0, 12), 16), 0)
+    const(A("AB", (0, 12), (256, 272)), 0)
+    const(A("SG", (1, 13), (256, 272)), 0)
+    const(A("SG", (0, 15, 14), (Q, 272)), 0)
+    const(A("SG", 13), 0)
+    const(LI(19), -KEEP - (1 << 20))
     const(A("cD", 0, 12), W)
     act(A("cD", 12, 24), kF(16, 12), af.Copy, bias=float(DUMP))
-    const(A("cD", 24, 36), W)
-    const(A("cD", 36, 48), DUMP)
-    sfill(A("cE", 0, 12), -OFF)
-    const(A("cE", 12, 24), 0)
-    for x in ("oS0", "oS1"):
+    for x in ("aV0", "oV0", "oV1"):
         const(A(x, (0, 12), 16), 0)
-    sfill(A("aV0", (0, 12), 16), -2.0 ** 30)
 
     def turn(x, t, s, out):
         n = x[4] // 16
@@ -306,47 +317,46 @@ def rank_program(g, core, T, topo):
         mms(A(out, (1, n, 2)), [(A(s, 2), A(t, (0, n, 2))), (A(s, 3), A(t, (1, n, 2)))])
         return A(out, (0, n))
 
-    def lists(o, x):
-        return [cp(A(o, 96 * h, 96 * h + 96), A(x, (0, 12), (8 * h, 8 * h + 8))) for h in (0, 1)]
+    def lists(o, x, s, o_):
+        return [ts(A(o, 96 * h, 96 * h + 96), A(x, (0, 12), (8 * h, 8 * h + 8)), s, o_) for h in (0, 1)]
 
     cp(A("X0", 0, Q), A("inL"))
-    turn(A("X0", 0, Q), "TL", "SM", "S1")
-    lists("oL0", "S1")
-    cp(rows("oS0"), A("S1", (0, 12)))
+    turn(A("X0", 0, Q), "TL", "SM", "S4")
+    lists("oL1", "S4", 1, op.mult)
+    act(rows("L2"), A("S4", (0, 12)), af.Copy, scale=2.0)
     TXs = [A("TX", Q * j, Q * j + Q) for j in range(3)]
-    early = [act(A("XS", 0, Q), A("inB"), af.Copy, scale=2.0 ** 17),
-             act(A("S3", (0, 12)), A("inB"), af.Copy, bias=2.0 ** 20 + 4096),
-             act(A("XL", 0, Q), A("inO"), af.Copy, scale=-8192.0, bias=15 * 8192.0 - OFF)]
+    early = [act(A("XS", 0, Q), A("inB"), af.Copy, scale=2.0 ** 16),
+             act(A("S3", (0, 12)), A("inB"), af.Copy, bias=2.0 ** 19),
+             act(A("XL", 0, Q), A("inO"), af.Copy, scale=-4096.0, bias=15 * 4096.0)]
     ts(TXs[1], A("inC"), -2.0 ** 22, op.mult)
     tt(TXs[0], A("XS", 0, Q), A("inC"), op.add)
-    tt(A("VT", 0, Q), A("S3", (0, 12)), TXs[1], op.min)
-    tt(TXs[2], A("VT", 0, Q), TXs[0], op.max)
+    tt(A("S3", (0, 12)), A("S3", (0, 12)), TXs[1], op.min)
+    tt(TXs[2], A("S3", (0, 12)), TXs[0], op.max)
     tt(A("X0", Q, 2 * Q), A("XL", 0, Q), TXs[2], op.add)
-    cp(rows("sV"), turn(A("X0", Q, 2 * Q), "TV", "SM", "S2"))
-    act(rows("aV0"), A("S2", (0, 12)), af.Copy)
+    first = {"word": cp(A("sV"), turn(A("X0", Q, 2 * Q), "TV", "SM", "S3"))}
+    gcopy(rows("aV0"), A("sV"))
     sfill(A("XC", (0, 12), 16), -2 * BIG)
-    for x in ("VT", "XL", "XS"):
-        sfill(A(x, R17, R17 + 1), 0.0)
+    const(A("rB", (0, 12), 16), 1 << 20)
+    const(A("wC", R18, R18 + 2), 0)
 
-    def clist(t):
-        ts(A("sC"), rows("sV"), 8191, op.bitwise_and)
-        return lists("oC%d" % (t % 2), "sC")
-    for x in clist(0):
-        x["bonus"] = EARLY
+    def names():
+        return ts(A("sC"), A("sV"), 4095 + (1 << 19), op.bitwise_and)
+    first["name"] = names()
+    first["list0"], first["list1"] = lists("aC0", "sC", W, op.min)
 
-    pe = {}
+    def yrep(bank, p, a, b, last):
+        def go(q):
+            for k in range(8):
+                ins = q.matmul(A(bank, (k, 8 * (b - a), 8))[3], A("NE")[3], Y(p, a, b)[3], k == 0, last and k == 7)
+            return ins
+        return emit("t", go, [A("NE"), Y(p, a, b)], [A(bank, (0, 8 * (b - a)))], FX + PE * 512)
 
     def yexp(p):
-        seq = []
-        for j, (a, bank) in enumerate(YB):
-            def go(q, a=a, bank=bank):
-                for k in range(8):
-                    ins = q.matmul(A(bank, (k, 32, 8))[3], A("NE")[3], A("y%d" % p, 16 * a, 16 * a + 64)[3], k == 0, k == 7)
-                return ins
-            pe["%d" % j] = emit("t", go, [A("NE"), A("y%d" % p)], [A(bank)], FX + PE * 512)
-            seq.append(act(A("YE", 128 * a, 128 * a + 512), A(bank), af.Copy, scale=-1.0))
-        seq[0]["bonus"] = BONUS
-        return seq
+        made = {}
+        for a, b, bank in YB:
+            made["ty%d" % a] = yrep(bank, p, a, b, True)
+            made["y%d" % a] = act(A("YE", 128 * a, 128 * b), A(bank, (0, 8 * (b - a))), af.Copy, scale=-1.0)
+        return made
 
     def span(x, h, a, b):
         return A(x, HALF * h + 128 * a, HALF * h + 128 * b)
@@ -357,173 +367,176 @@ def rank_program(g, core, T, topo):
     def weights(z):
         return [A(z, 15 - q, 143 - q) for q in range(16)]
 
-    def usum(p):
-        pe["u"] = mms(A("MS", 0, 12), [(z, A("y%d" % p, q, Q, 16)) for q, z in enumerate(weights("Z1"))])
+    def change(c, z, old):
+        c["gz"] = cp(A("DdL", 0, Q, 16), z)
+        c["tL"] = mms(A("S4", (0, 12)), [old], last=False)
+        c["wL"] = scan(A("wL"), A("ML"), A("DdL"), op.mult, op.add)
+        c["AL"] = act(A("zL"), A("wL"), af.Abs, scale=2.0, bias=-30.0 * 8192)
+        c["DL"] = act(rows("DL"), A("zL"), af.Relu, scale=-8192.0, bias=8192.0 * 8192)
+        c["tE"] = mms(A("S4", (0, 12)), [(A("EY"), rows("DL"))], first=False)
+        c["min"] = tt(rows("L2"), A("S4", (0, 12)), A("zL"), op.min)
 
-    chain(early + yexp(0)[1:])
-    usum(0)
-    sbefore = []
+    chain(early)
+    yexp(0)
+    visits = []
     for t in range(TV):
         p, nxt = t % 2, t + 1
         last = nxt == TV
-        lL, lC, L = [("a%s%d" if t else "o%s%d") % (k, t) for k in "LCS"]
-        V = "aV%d" % t
-        LH = A("LH", (12 * t, 12 * t + 12))
-        const(LH, 8192)
-        emit("g", lambda q, x=A(L), o=LH: q.dma_start(o[3], x[3], accum_op=op.add), [A(L), LH], [LH], 0.3, sem="dA", inc=16, lat=3.0)
-        order, diff, final = {"v": [], "s": list(sbefore), "t": []}, {}, {x[0]: x for x in PLAN}
-        mms(A("XL", 0, Q), [(A("ONE"), A("CL"))], last=False)
-        mms(rows("XC"), [(A("ONE"), A("CC"))], last=False)
+        lL, lC, V = ["a%s%d" % (k, t) for k in "LCV"]
+        oL, oC, oV, oZ = ["o%s%d" % (k, nxt % 2) for k in "LCVZ"]
+        IC, yv, yn = "IC", Y(p), Y(1 - p)
+        c = {} if t else first
+        if t:
+            z = A("aZ%d" % t, 2, 36, 3)
+            c["nL0"], c["nL1"] = [gcopy(A("Lf", (0, 12), (8 * h, 8 * h + 8)), A(lL, 96 * h, 96 * h + 96)) for h in (0, 1)]
+            change(c, z, (A("I2"), A("Lf")))
+            if not last:
+                c["lL0"], c["lL1"] = lists(oL, "L2", 0.5, op.mult)
+            c["cz"] = cp(LI(26), z)
+            c["az"] = ts(LI(27), LI(26), 8191 + (1 << 20), op.bitwise_and)
+            c["lz"] = ts(A("NL"), LI(27), DUMP - 1, op.min)
+            c["wz"] = tt(A("L2", (0, 12), 16), LI(26), LI(27), op.add)
+            c["fz"] = act(A("DL", (0, 12), 16), z, af.Identity, scale=-2.0 ** -18, bias=7.5 + 1.0 / 128)
+            c["N"] = tt(A("DN"), A("P"), yv, op.subtract, off=A("NL"))
+            c["overN"] = ts(A("SG", 13, (0, Q)), A("DN"), 0, op.is_gt)
+            c["absN"] = act(A("AB", (0, 12), (256, 272)), A("DN"), af.Abs)
+        else:
+            lL = oL
+        if not last:
+            c["sendL"] = send("L", nxt, 3.0)
+        diff, final = {}, {x[0]: x for x in PLAN}
+        XL = A("XL", 17, 17 + R17)
+        c["kL"] = mms(A("XL", 0, 15 * 17), [(A("ONE"), A("CL"))], last=False)
+        c["kC"] = mms(rows("XC"), [(A("ONE"), A("CC"))], last=False)
+        c["xS"] = mms(A("XS", 0, R17), [(A("NW"), A("DL"))], last=False)
         for x in PLAN:
             kind, h, a, b = x
             ye, at = A("YE", 128 * a, 128 * b), (96 * h + 8 * a, 96 * h + 8 * b)
             if kind == "L":
-                diff[h, a] = span("D", h, a, b)
-                me = tt(diff[h, a], A("P"), ye, op.subtract, off=A(lL, *at))
+                diff[h, a, "l"] = span("D", h, a, b)
+                me = tt(span("D", h, a, b), A("P"), ye, op.subtract, off=A(lL, *at))
             elif kind == "C":
-                me = tt(span("IC", h, a, b), A("P"), ye, op.is_gt, off=A(lC, *at))
-            elif kind[0] == "l":
-                diff[h, a] = ps = A("S" + kind[1], (0, 8 * (b - a)))
-                mms(ps, [(A("NE"), ye)], last=False)
-                order["s"].append(act(span("LR", h, a, b), A("P"), af.Copy, off=A(lL, *at)))
-                me = mms(ps, [(A("EY"), span("LR", h, a, b))], first=False)
+                me = tt(span(IC, h, a, b), A("P"), ye, op.is_gt, off=A(lC, *at))
+            elif kind[1:].isdigit():
+                raw = span(kind[0].upper() + "R", h, a, b)
+                diff[h, a, kind[0]] = ps = A("S" + kind[1], (0, 8 * (b - a)))
+                c["n%s%d%d" % (kind[0], h, a)] = yrep(ps[0], p, a, b, False) if b > YB[-1][1] else mms(ps, [(A("NE"), ye)], last=False)
+                me = act(raw, A("P"), af.Copy, off=A(lL if kind[0] == "l" else lC, *at))
+                c["e%s%d%d" % (kind[0], h, a)] = mms(ps, [(A("EY"), raw)], first=False)
+                kind = kind[0]
             elif kind == "abs":
-                me = act(piece("AB", h, a, b), diff[h, a], af.Abs)
+                me = act(piece("AB", h, a, b), diff[h, a, "l"], af.Abs)
             elif kind == "sign":
-                me = act(piece("SG", h, a, b), diff[h, a], af.Sign, bias=-0.5)
+                me = act(piece("SG", h, a + 1, b + 1), diff[h, a, "l"], af.Sign, bias=-0.5)
+            elif kind == "csign":
+                me = act(span(IC, h, a, b), diff[h, a, "c"], af.Sign, bias=-0.5)
             elif kind == "over":
-                me = ts(piece("SG", h, a, b), diff[h, a], 0, op.is_gt)
+                me = ts(piece("SG", h, a + 1, b + 1), diff[h, a, "l"], 0, op.is_gt)
             elif kind == "XS":
-                me = mms(A("XS", 16 * a, 16 * b), [(z, A("AB", (a, b), (q, 256, 16))) for q, z in enumerate(weights("ZS"))])
+                me = mms(A("XS", 17 * a, 17 * b), [(w, A("AB", (a, b), (q, 272, 16))) for q, w in enumerate(weights("ZS"))], False, x == final[kind])
             elif kind == "XL":
-                me = mms(A("XL", 16 * a, 16 * b), [(z, A("SG", (a, b), (q, 256, 16))) for q, z in enumerate(weights("ZL"))], False, x == final[kind])
+                lo, hi = a + 1 - (p and a == 0), b + 1 + (2 - p) * (b == 12)
+                me = mms(A("XL", 17 * lo, 17 * hi), [(w, A("SG", (lo, hi), (q, 272, 16))) for q, w in enumerate(weights("ZL"))], False, False)
             else:
-                lo, hi = span("IC", h, a, b)[1:3]
-                part = sl(*{"XC": (0, 16), "XD": (0, 8), "XE": (8, 16)}[kind])
-                me = mms(A("XC", (a, b), (8 * h, 8 * h + 8)), [(z, A("IC", lo + q, hi, 16)) for q, z in enumerate(weights("ZC"))][part], False, x == PLAN[-1])
-            order[me["e"]].append(me)
-        for e in order:
-            chain(order[e])
-        idle = [act(A("RLS", 15, Q, 16), A("MS", 0, 12), af.Copy), act(LF(0), A("MS", 0, 12), af.Copy, scale=37.0, bias=float(t))]
-        idle += [act(A("uF", 12 * j, 12 * j + 12), A("MS", 0, 12), af.Copy) for j in (0, 1)]
+                me = mms(A("XC", (0, 12), (8 * h, 8 * h + 8)), [(w, A("IC", HALF * h + q, HALF * (h + 1), 16)) for q, w in enumerate(weights("ZC"))], False, x == final[kind])
+            c["%s%d%d" % (kind, h, a)] = me
+        c["xL"] = mms(XL, [(A("NW"), A("DL"))], first=False)
         if t:
-            idle += [act(A("Bf", 12 * j, 12 * j + 12), A("MS", 48, 60), af.Sign, bias=(0.5 - 4 * j) * 2 ** 17) for j in (1, 2)]
-        chain(order["s"][-1:] + idle)
-        RL = A("RLS", Q + 15, 2 * Q, 16)
-        tt(A("mkL"), A("XL", 0, Q), rows(L), op.min)
-        scan(A("RLS", Q, 2 * Q), A("DS"), A("mkL"), op.add, op.max)
-        scan(A("RLS", 2 * Q, 3 * Q), A("DS"), A("XS", 0, Q), op.add, op.max)
-        cp(LI(0, 2), A("RLS", 15, 2 * Q, 16))
-        cp(LI(2), A("RLS", 2 * Q + 15, 3 * Q, 16))
-        act(LF(1), RL, af.Identity, bias=97.0 * t)["bonus"] = 1.0
-        ts(LI(3, 2), LI(0, 2), 4095, op.bitwise_and)
-        tt(LI(7, 2), LI(3, 2), A("uF"), op.mult)
-        ts(LI(9, 2), LI(7, 2), 5, op.arith_shift_right)
-        tt(LI(11, 2), LI(9, 2), LF(0, 2), op.add)
-        ts(LI(5), LI(12), 3840 - (1 << 31), op.bitwise_and)
-        ts(LI(6), LI(11), 4095, op.bitwise_and)
-        ts(LI(14, 2), LI(1, 2), 15 << 13, op.bitwise_and)
-        act(A("GF", 32, 64), A("RLS", Q, 2 * Q), af.Sign, bias=0.5, off=A("GL", 0, 2))
-        flag = act(A("cv", 12, 24), A("GF", 32, 44), af.Identity, scale=-2.0 ** 19, bias=-2.0 ** 19)
-        act(A("GF", 0, 32), A("GF", 32, 64), af.Relu)
-        tt(LF(4, 2), LI(14, 2), A("cv"), op.add)
-        tt(LF(2, 2), LF(4, 2), LI(5, 2), op.add)
-        tt(Z("Dd", 0, 0), LF(2), LF(3), op.max)
-        tt(LF(6, 2), LI(4, 2), A("cD", 24, 48), op.subtract)
-        tt(LF(8, 2), LF(6, 2), A("GF", 0, 24), op.mult)
-        act(Z("Dd", 1, 0), RL, af.Copy, bias=-4096.0 - 2.0 ** 20)
-        chain([act(Z("Dd", 2, 0), RL, af.Relu, scale=-2.0 ** -19)] + [steps(j) for j in range(nxt, TV)[:1]])
-        chain([flag, act(A("tB"), rows(V), af.Identity, scale=2.0 ** -17, bias=260 - 0.5 + 1.0 / 64)])
-        act(rows("SLT"), A("tB"), af.Identity, scale=2.0 ** 25, bias=(-150 - 0.5 + 6.0 / 256) * 2.0 ** 25)
-        tt(rows("XC"), rows("XC"), rows(V), op.min)
-        tt(A("mk"), A("XC", (0, 12), (0, 17)), A("SLT"), op.max)
-        scan(A("RC"), A("DC%d" % p, 0, R17), A("mk"), op.add, op.max)
+            c["b4"] = act(A("Bf", 24, 36), A("MS", 48, 60), af.Identity, scale=2.0 ** -18, bias=130 - 0.375)
+            c["tw"] = mms(A("MS", 32, 44), [(A("GW"), A("Bf", 0, 12))] + [(A("NW"), A("Bf", 12 * j, 12 * j + 12)) for j in (2, 3)])
+        u, RL = A("RLS", 16, R17, 17), A("RLS", R17 + 16, 2 * R17, 17)
+        c["u"] = act(u, A("XL", 238 - 238 * p, 250 - 238 * p), af.Copy, scale=2.0 ** -26)
+        c["uu"] = act(A("uF"), A("RLS", 0, R17), af.Copy, scale=0.5, off=A("BL", 0, 2))
+        c["mkL"] = tt(A("mkL"), XL, A("L2"), op.min)
+        c["mkN"] = tt(A("mkL", 16, R17, 17), A("XL", 221, 233), A("L2", (0, 12), 16), op.min)
+        c["scanL"] = scan(A("RLS", R17, 2 * R17), A("DS", 0, R17), A("mkL"), op.add, op.max)
+        c["flag"] = act(LF(0), RL, af.Relu, bias=2.0 ** 24)
+        c["u37"] = act(LF(6), u, af.Identity, scale=18.5, bias=float(t))
+        c["a97"] = act(LF(7), RL, af.Identity, scale=0.5, bias=97.0 * t)
+        c["G"] = act(Z("Dd", 1, 0), RL, af.Identity, scale=0.5, bias=-2.0 ** 19)
+        c["cpu"] = ts(LI(0, 2), A("RLS", 16, 2 * R17, 17), -(1 << 18), op.max)
+        c["and2"] = ts(LI(3, 2), LI(0, 2), 8191 + (1 << 18), op.bitwise_and, 1, op.arith_shift_right)
+        c["mul"] = tt(LI(7, 2), LI(3, 2), A("uF", 0, 24), op.mult)
+        c["shf"] = ts(LI(9, 2), LI(7, 2), 5, op.arith_shift_right)
+        c["add"] = tt(LI(11, 2), LI(9, 2), LF(6, 2), op.add)
+        c["n5"] = ts(LI(5), LI(12), 3840 + (1 << 30), op.bitwise_and)
+        c["m6"] = ts(LI(13), LI(11), 4095, op.bitwise_and)
+        c["m7"] = tt(LI(25), LI(13), LF(0), op.add)
+        VP, slot, BB = A("S3", (0, 12)), A("XL", 256, 256 + R17), A("XL", 464, 488)
+        c["tV"] = mms(VP, [(IDF, rows(V))], last=False)
+        c["r0"] = act(rows("rF"), rows(V), af.Identity, bias=-32767.5)
+        c["r"] = act(rows("rF"), rows("rF"), af.Identity, scale=2.0 ** -16, bias=1.5 * 2 ** 23)
+        c["r1"] = act(rows("rB"), rows("rF"), af.Identity, scale=-128.0, bias=128 * (1.5 * 2 ** 23 + 19))
+        c["slot"] = mms(slot, [(A("NW"), A("rB")), (A("ONE"), A("CK"))])
+        c["cmin"] = tt(A("mk"), rows("XC", 17), A(V), op.min)
+        c["mk"] = tt(A("mk"), slot, A("mk"), op.max)
+        c["rc"] = scan(A("RC"), A("DC", t), A("mk"), op.add, op.max)
         RC = A("RC", 16, R17, 17)
-        ts(A("M", 1, 48 * 17, 17), A("RC"), -2 * OFF, op.is_lt, off=A("BL", 0, 3))
-        if t:
-            chain([order["t"][-1], mms(A("MS", 32, 44), [(A("GW"), A("Bf", 0, 12))] + [(A("NW"), A("Bf", 12 * j, 12 * j + 12)) for j in (1, 2, 3)])])
-            tt(LI(16), RC, A("MS", 32, 44), op.subtract)
-        else:
-            cp(LI(16), RC)
-        tt(LF(10, 2), LF(8, 2), Z("M", 0, 1, 2), op.mult)
-        tt(LF(6, 2), LF(10, 2), A("cD", 0, 24), op.add)
-        cp(A("LST"), LF(6, 2))
-        PL, NL = A("LST", 0, 12), A("LST", 12, 24)
-        yv, dy = A("y%d" % p), rows("XC")
-        tail = {"p": act(A("pa"), A("P"), af.Copy, off=PL)}
-        mms(dy, [(A("NE"), yv), (A("EY"), A("pa"))])
-        tail["y"] = act(A("y%d" % (1 - p)), dy, af.Abs)
-        if last:
-            tt(A("md"), A("P"), yv, op.min, off=PL)
-        else:
-            pe["m"] = mms(dy, [(A("EY"), yv), (A("EY"), A("pa")), (A("NE"), A("y%d" % (1 - p)))])
-            tail["m"] = act(A("md"), dy, af.Copy, scale=0.5)
-        write = emit("v", lambda q, to=NL: q.tensor_copy(T.P[:, :].indirect(to[3]), T.md[:, :]), [A("md"), NL], [A("P")], 0.05 + 3.8 * CY * Q)
-        write["bonus"] = 2 * BONUS * last
-        oS, oV, oB = ["o%s%d" % (k, nxt % 2) for k in "SVB"]
-        ts(LI(17), LI(16), (1 << 20) + (1 << 17) - 1, op.bitwise_and)
-        ts(LI(18), LI(16), (1 << 20) + (31 << 12), op.bitwise_and)
-        ts(LI(19), LI(16), 20, op.arith_shift_right, 31, op.bitwise_and)
-        ts(Z("Dd", 0, 1), LI(17), -(1 << 20) - LOW, op.add)
-        tt(Z("Dd", 1, 1, 2), LI(18, 2), A("cE"), op.add)
-        scan(A("VT", 0, R17), Z("M", 0), Z("Dd", 0), op.mult, op.add)
-        zl = A("VT", 1, R17 + 1)
-        tt(zl, zl, A(L), op.max)
-        tt(A("sL"), zl, LH, op.min)
-        ts(rows(oS), rows("sL"), 4095, op.bitwise_and)
-        way = []
+        c["nb"] = ts(A("M", 7, 6 + 32 * 18, 18), A("RC"), 0, op.is_lt, off=A("BL", 0, 2))
+        c["B"] = act(A("Bf", 0, 24), Z("M", 0, 1, 2), af.Copy, scale=-2.0 ** 20, bias=2.0 ** 20)
+        c["bb"] = mms(BB, [(A("EY"), A("cB")), (A("EY"), A("Bf", 0, 24))])
+        c["k16"] = tt(LI(16), RC, A("MS", 32, 44), op.subtract) if t else cp(LI(16), RC)
+        c["a23"] = ts(LI(17), LI(16), (1 << 19) + (1 << 16) - 1, op.bitwise_and)
+        c["a2"] = ts(LI(18), LI(16), (1 << 19) + (15 << 12), op.bitwise_and)
+        c["a1"] = ts(LI(22), LI(16), (1 << 19) + (15 << 20), op.bitwise_and)
+        c["of"] = ts(Z("M", 1, 2), LI(18), 1 << 19, op.is_ge, 0.5, op.mult)
+        c["conv"] = tt(Z("Dd", 0, 1, 2), LI(17, 2), LI(18, 2), op.add)
+        c["conv2"] = ts(Z("Dd", 1, 2), LI(22), KEEP // 2 + MID - (15 << 20), op.add)
+        c["wC"] = scan(A("wC", 0, R18), Z("M", 1), Z("Dd", 1), op.mult, op.add)
         if not last:
-            way = lists("oL%d" % (nxt % 2), oS)[:1]
-            sends = [send("L", nxt, 2.4), send("S", nxt, 4.0)]
-            sends[0]["bonus"] = LBON
-        chain(way + [scan(A(x, 0, R17), Z("M", j), Z("Dd", j), op.mult, op.add) for x, j in (("XL", 2), ("XS", 1))])
-        zn, zr = A("XS", 1, R17 + 1), A("XL", 1, R17 + 1)
-        tt(zn, zn, A(V), op.subtract)
+            c["tB"] = mms(A("MS", 48, 60), [(A("GW"), A("Bf", 0, 12))])
+        c["A"] = act(A("zC"), A("wC", 2, R18 + 2), af.Abs, scale=2.0, bias=-2.0 * MID)
+        c["D1"] = act(A("D1"), rows("zC"), af.Relu, scale=-16.0, bias=16.0 * KEEP + 2 ** 16)
+        c["tD"] = mms(VP, [(A("EY"), A("D1"))], first=False)
         if last:
-            ts(A("VT", 256, 256 + R17), zr, 14, op.is_equal, 2.0 ** 17, op.mult)
-            tt(A(oB), A("VT", 256, 256 + R17), A(V), op.add)
-            ts(A("hot"), zr, 15, op.is_equal)
+            c["out"] = tt(A("X0", Q, 2 * Q), VP, rows("zC"), op.min)
         else:
-            ts(A("hot"), zr, 15, op.is_equal)
-            ts(A("bp"), zr, 14, op.is_equal, 2.0 ** 17, op.mult)
-        tt(zn, zn, A("hot"), op.mult)
-        tt(A("sV"), zn, A(oB if last else V), op.add)
-        if last:
-            break
-        tail["v"] = act(A(oV), zn, af.Copy)
-        clist(nxt)
-        emit("y", lambda q, o=A(oB), i=A(V): q.dma_start(o[3], i[3]), [A(V)], [A(oB)], 0.05, sem="dC%d" % nxt, inc=16, lat=2.5)
-        sends.append(emit("g", lambda q, o=A(oB): q.dma_start(o[3], A("bp")[3], accum_op=op.add), [A("bp"), A(oB)], [A(oB)], 0.3, sem="dB%d" % nxt, inc=16, lat=2.5))
-        chain(sends + [send("C", nxt, 2.4), send("V", nxt, VLAT, [A(oB)])])
-        for j, x in enumerate(yexp(1 - p)):
-            tail["%d" % j] = x
-        tail["B"] = act(A("Bf", 0, 12), Z("M", 0, 1), af.Copy, scale=-1.0, bias=1.0)
-        mms(A("MS", 48, 60), [(A("GW"), A("Bf", 0, 12))])
-        usum(1 - p)
-        chain([pe[k] for k in TT.split()])
-        sbefore = [tail[k] for k in TAIL.split()]
+            c["cmn"] = tt(A("sV"), VP, rows("zC"), op.min)
+            c["andC"] = names()
+            c["lC0"], c["lC1"] = lists(oC, "sC", W, op.min)
+            c["sendC"] = send("C", nxt, 3.0)
+            c["gV"] = gcopy(rows(oV), A("sV"))
+            c["sendV"] = send("V", nxt, 3.5)
+        c["an"] = tt(LI(23, 2), LI(4, 2), BB, op.add)
+        c["adr"] = tt(LF(2, 2), LI(23, 2), A("cD"), op.min)
+        c["LST"] = cp(A("LST"), LF(2, 2))
+        PL, NL = A("LST", 0, 12), A("LST", 12, 24)
+        c["d"] = tt(A("pa"), A("P"), yv, op.subtract, off=PL)
+        c["y"] = act(yn, A("pa"), af.Abs)
+        c["md0" if last else "md"] = ts(A("md"), A("pa"), 0, op.min)
+        c["end" if last else "write"] = emit("v", lambda q, to=NL, y=yv: q.tensor_tensor(T.P[:, :].indirect(to[3]), y[3], T.md[:, :], op.add), [A("md"), yv, NL], [A("P")], 0.05 + 3.8 * CY * Q)
+        c["scanS"] = scan(A("RS"), A("DS", R17, 2 * R17), A("XS", 0, R17), op.add, op.max)
+        c["cps"] = cp(LI(2), A("RS", 16, R17, 17))
+        c["cod"] = ts(LI(14, 2), LI(1, 2), 15 << 13, op.bitwise_and)
+        c["w2"] = tt(LF(4, 2), LI(14, 2), LI(24, 2), op.add)
+        c["w0"] = tt(Z("Dd", 0, -5), LF(4), LF(5), op.min)
+        c["z"] = scan(A(oZ), Z("M", 0), Z("Dd", 0), op.mult, op.add)
+        if not last:
+            c["sendZ"] = send("Z", nxt, 2.5)
+            c.update(yexp(1 - p))
+        visits.append(c)
+    change({}, A(oZ, 2, 36, 3), (IDF, rows("L2")))
+    for e in ORDER:
+        names_ = [(k.rstrip("+"), int(k[-1] == "+")) for k in ORDER[e].split()]
+        chain([visits[t + d][k] for t in range(-1, TV) for k, d in names_ if 0 <= t + d < TV and k in visits[t + d]])
 
     dma("y", T.zp[:, :], T.P[:, 0:W], [A("P", 0, W)], [], 6.0)
-    dma("y", T.zy[:, :], T["y%d" % (TV % 2)][:, :], [A("y%d" % (TV % 2))], [], 2.0)
-    TB, TC = A("VT", 0, Q), A("VT", 256, 256 + Q)
-    for j in range(4):
-        chain([order["s"][-1], act(A("BM", j), A("SM", j), af.Copy)])
-    cp(A("X0", 0, Q), rows(oS))
-    act(A("E0", 0, Q), turn(A("X0", 0, Q), "TL", "SM", "S1"), af.Copy)
-    dma("y", T.zl[:, :], T.E0[:, 0:Q], [A("E0", 0, Q)], [], 2.0)
-    ts(A("tF"), rows("sV"), 8191, op.bitwise_and)
-    ts(TB, A("tF"), 4096, op.is_ge, -8192, op.mult)
-    tt(A("X0", Q, 2 * Q), TB, A("tF"), op.add)
-    ts(A("E0", Q, 2 * Q), turn(A("X0", Q, 2 * Q), "TV", "SM", "S2"), -1, op.max)
+    dma("y", T.zy[:, :], yn[3], [yn], [], 2.0)
+    word = turn(A("X0", Q, 2 * Q), "TV", "SM", "S2")
+    act(A("E0", 0, Q), turn(rows("L2"), "TL", "SM", "S1"), af.Copy, scale=0.5)
+    dma("s", T.zl[:, :], T.E0[:, 0:Q], [A("E0", 0, Q)], [], 2.0)
+    cp(A("sV"), word)
+    names()
+    act(A("TX", 0, Q), word, af.Sign, scale=-1.0, bias=2.0 ** 19 - 0.5)
+    act(rows("XC"), A("TX", 0, Q), af.Identity, scale=2048.5, bias=2047.5)
+    tt(A("E0", Q, 2 * Q), rows("XC"), A("sC"), op.min)
     dma("y", T.zc[:, :], T.E0[:, Q:2 * Q], [A("E0", Q, 2 * Q)], [], 2.0)
-    ts(A("tS"), rows("sV"), 13, op.arith_shift_right, 15, op.bitwise_and)
-    ts(A("X1", 0, Q), A("tS"), -1, op.mult, 15, op.add)
-    act(A("oB", 0, Q), turn(A("X1", 0, Q), "TO", "BM", "S3"), af.Copy)
-    dma("s", T.zo[:, :], T.oB[:, 0:Q], [A("oB", 0, Q)], [], 2.0)
-    ts(A("sC"), rows("sV"), 17, op.arith_shift_right, 7, op.bitwise_and)
-    ts(TC, A("tF"), -4096, op.add, 0, op.max)
-    tt(A("X1", Q, 2 * Q), TC, A("sC"), op.add)
-    act(A("oB", Q, 2 * Q), turn(A("X1", Q, 2 * Q), "TP", "BM", "S1"), af.Copy)
+    ts(A("tS"), A("sV"), 12, op.arith_shift_right, 15, op.bitwise_and)
+    ts(A("oB", 0, Q), A("tS"), -1, op.mult, 15, op.add)
+    dma("y", T.zo[:, :], T.oB[:, 0:Q], [A("oB", 0, Q)], [], 2.0)
+    ts(A("inL"), A("sV"), 16, op.arith_shift_right, 7, op.bitwise_and)
+    ts(A("S3", (0, 12)), A("sC"), -(1 << 19), op.add, 0, op.max)
+    tt(A("oB", Q, 2 * Q), A("S3", (0, 12)), A("inL"), op.add)
     dma("y", T.zb[:, :], T.oB[:, Q:2 * Q], [A("oB", Q, 2 * Q)], [], 2.0)
 
     succ = [[] for _ in ops]
@@ -538,6 +551,7 @@ def rank_program(g, core, T, topo):
             left[s["i"]] -= 1
             if not left[s["i"]]:
                 line.append(s)
+    assert len(line) == len(ops)
     for o in reversed(line):
         o["pri"] = o["bonus"] + o["cost"] + o["lat"] + max([0.0] + [s["pri"] + (WK if s["e"] == o["e"] else WX) for s in succ[o["i"]]])
     left = {o["i"]: len(o["all"]) for o in ops}

import numpy as np
from concourse.bass import DstId, RemoteDMATransfer
from concourse.mybir import AluOpType, ActivationFunctionType

N, W, Q, TV, HOP = 8, 4096, 192, 6, 3
NPOS = 16 * Q
HALF = NPOS // 2
PW = 4304
DUMP = 4112
R17, R18 = 12 * 17, 12 * 18
PLAN = [("l1", 0, 8, 12), ("l2", 1, 8, 12), ("sign", 0, 8, 12), ("sign", 1, 8, 12), ("L", 0, 0, 4), ("L", 0, 4, 8), ("L", 1, 0, 4), ("L", 1, 4, 8),
        ("sign", 0, 0, 4), ("over", 1, 0, 4), ("over", 0, 4, 8), ("over", 1, 4, 8), ("XL", 0, 8, 12), ("XL", 0, 0, 4), ("XL", 0, 4, 8),
        ("c3", 0, 8, 12), ("csign", 0, 8, 12), ("c4", 1, 8, 12), ("csign", 1, 8, 12), ("C", 0, 0, 4), ("C", 0, 4, 8), ("C", 1, 0, 4), ("C", 1, 4, 8), ("XC", 0, 0, 12), ("XC", 1, 0, 12),
        ("abs", 0, 8, 12), ("abs", 1, 8, 12), ("abs", 0, 0, 4), ("abs", 0, 4, 8), ("abs", 1, 0, 4), ("abs", 1, 4, 8), ("XS", 0, 8, 12), ("XS", 0, 0, 4), ("XS", 0, 4, 8)]
YB = [(0, 4, "S1"), (4, 8, "S2")]
ORDER = {
    "v": "L10 L00 word L04 cz gz name over10 wL az list0 L14 list1 lz wz over04 over14 N min overN C00 C04 C14 C10 mkL lL0 mkN lL1 scanL cpu cmin and2 mk mul rc shf k16 nb add a2 a23 a1 n5 m6 "
         "of conv2 conv m7 an wC adr scanS LST cps d cod md0 w2 end md w0 cmn z out andC write lC1 lC0",
    "s": "l18 abs10 sign00 abs00 AL sign08 DL fz c08 sign18 c18 csign08 abs04 u csign18 r0 absN r uu u37 r1 abs08 a97 abs18 G abs14 B flag A D1 y y0 b4+ y4 l08+",
    "t": "el08 nl18 nc08 XL00 el18 tE XL04 nc18 ec08 XL08 ec18 xL XC00 xS XC10 slot XS00 kC+ XS08 bb XS04 kL+ tB tV tD ty0 ty4 nl08+ tw+ tL+",
    "g": "sendL sendZ nL1+ nL0+ sendC gV sendV"}
BIG = 2.0 ** 33
KEEP = 10 << 16
MID = 15 << 19

F32, BF, I32, U16 = "float32", "bfloat16", "int32", "uint16"
SCRATCH = {}
for _n, _w, _d in (
        ("P", PW, BF), ("D", NPOS, BF), ("AB", [12, 272], BF), ("SG", [15, 272], BF), ("IC", NPOS, BF),
        ("YE", HALF, BF), ("LR", NPOS, BF), ("CR", NPOS, BF), ("BL", 2, U16),
        ("inL", Q, I32), ("inC", Q, I32), ("inO", Q, BF), ("inB", Q, BF), ("inLim", 8, I32), ("limF", 8, F32),
        ("CL", [15, 17], BF), ("CC", [12, 16], BF), ("ONE", 128, BF), ("CK", R17, BF), ("I2", 128, F32),
        ("ZF", 144, BF), ("ZL", 144, BF), ("ZC", 144, BF), ("ZS", 144, BF),
        ("GW", 128, BF), ("NW", 128, BF), ("BO", 128, BF), ("EY", 128, BF), ("NE", 128, BF),
        ("PM", 24, BF), ("PM1", 102, BF), ("CT", 102, F32), ("DC", [TV, R17], F32),
        ("ID", 160, F32), ("SM", [4, 128], F32),
        ("mpI", 160, I32), ("gI", 128, I32), ("sI", 96, I32), ("KX", 256, I32), ("kI", 128, I32), ("kF", 128, F32),
        ("cB", 24, BF), ("cD", 24, F32), ("X0", 384, F32), ("X1", 384, BF), ("E0", 384, F32), ("oB", 384, BF), ("TX", 3 * Q, F32),
        ("TL", [12, 16], F32), ("TV", [12, 16], F32),
        ("DS", 2 * R17, F32), ("mkL", R17, F32), ("mk", R17, F32), ("RLS", 2 * R17, F32), ("RS", R17, F32), ("RC", R17, F32),
        ("tS", Q, I32), ("rF", [12, 17], F32), ("sV", [12, 16], I32), ("D1", Q, BF), ("zC", [12, 18], F32), ("wC", R18 + 2, F32),
        ("ML", Q, F32), ("DdL", Q, F32), ("wL", Q, F32), ("zL", Q, F32), ("DL", [12, 17], BF), ("Lf", [12, 16], F32), ("L2", [12, 17], F32),
        ("DN", Q, BF), ("rB", [12, 17], BF), ("NL", 12, U16), ("sC", [12, 16], I32), ("M", 6 + 32 * 18, F32), ("uF", 32, F32),
        ("LI", 336, I32), ("LF", 96, F32), ("Bf", 48, BF), ("LST", 24, U16), ("pa", Q, BF), ("md", Q, BF)):
    SCRATCH[_n] = ("sbuf", [128] + (_w if isinstance(_w, list) else [_w]), _d)
for _n in ("XL", "XS", "MS"):
    SCRATCH[_n] = ("psum", [128, 512], F32)
SCRATCH["XC"] = ("psum", [128, 16, 32], F32)
for _n in ("S1", "S2", "S3", "S4"):
    SCRATCH[_n] = ("psum", [128, 32, 16], F32)
for _t in range(TV):
    for _k, _w, _d in (("V", [12, 17], F32), ("Z", [36], F32), ("L", [Q], U16), ("C", [Q], U16)):
        SCRATCH["o%s%d" % (_k, _t % 2)] = SCRATCH["a%s%d" % (_k, _t)] = ("sbuf", [128] + _w, _d)
SEMAPHORES = (["sv", "ss", "st", "sg"] + ["l" + k + i for k in "CVLZ" for i in "01"] + ["d%d" % i for i in range(16)]
              + ["q%s%d" % (k, t) for k in "CVLZ" for t in range(1, TV)])
CY, PE, FX, FS, WK, WX = 0.00093, 0.0005, 0.04, 0.06, 0.06, 0.12
EARLY = 10.0
PLAT = 7.0


def rank_program(g, core, T, topo):
    rank = T.rank_of(core)
    if rank is None:
        return
    dst = T.cores[(rank + HOP) % N]
    rid, pid = topo.addr(dst)[:2]
    emask = topo.mask(core, dst)
    neng = len(topo.engines(core, dst))
    op = AluOpType
    af = ActivationFunctionType
    queues = {"v": g.vector, "s": g.scalar, "t": g.tensor, "g": g, "y": g.sync}
    semof = {"v": "sv", "s": "ss", "t": "st", "g": "sg"}
    ops, wr, rd = [], {}, {}
    psum = {k for k in SCRATCH if SCRATCH[k][0] == "psum"}
    sl = slice

    def A(name, *ix):
        shape = SCRATCH[name][1][1:]
        if len(shape) == 1:
            ix = (sl(*ix),) if len(ix) > 1 else (sl(None),)
        else:
            ix = tuple(sl(*x) if isinstance(x, tuple) else x for x in ix) + (sl(None),) * (2 - len(ix))
        at = np.arange(int(np.prod(shape))).reshape(shape)[ix].reshape(-1)
        return (name, int(at.min()), int(at.max()) + 1, T[name][(sl(None),) + ix], len(at), frozenset(at.tolist()))

    def meet(x, y, e, computes):
        if y[1]["e"] == e or (x[0] not in psum and computes and y[1]["inc"] == 1):
            return x[1] < y[0][2] and y[0][1] < x[2] and not x[5].isdisjoint(y[0][5])
        return x[0] in psum or (x[1] < y[0][2] and y[0][1] < x[2])

    def emit(e, fn, R, Wt, cost, sem=None, inc=1, lat=0.0):
        need = []
        for x in R:
            need += [y[1] for y in wr.get(x[0], []) if meet(x, y, e, inc == 1)]
            if x[0] in psum:
                need += [y[1] for y in rd.get(x[0], []) if y[1]["e"] != e]
        for x in Wt:
            need += [y[1] for y in wr.get(x[0], []) + rd.get(x[0], []) if meet(x, y, e, inc == 1)]
        me = {"e": e, "fn": fn, "need": need, "cost": cost, "sem": sem or semof.get(e), "inc": inc, "lat": lat, "i": len(ops), "soft": [], "bonus": 0.0}
        ops.append(me)
        for x in Wt:
            wr[x[0]] = [y for y in wr.get(x[0], []) if not y[0][5] <= x[5]] + [(x, me)]
            rd[x[0]] = [y for y in rd.get(x[0], []) if not y[0][5] <= x[5]]
        for x in R:
            rd.setdefault(x[0], []).append((x, me))
        return me

    def vc(o, ins):
        n = max([x[4] for x in [o] + ins])
        return FX + CY * max(64, n * (0.5 if all(SCRATCH[x[0]][2] in (BF, U16) for x in [o] + ins) else 1))

    def ts(o, i, s1, op0, s2=None, op1=None, off=None):
        R = [i] + [s for s in (s1, s2, off) if isinstance(s, tuple)]
        a1, a2 = [s[3] if isinstance(s, tuple) else s for s in (s1, s2)]
        src = i[3].indirect(off[3]) if off else i[3]
        cost = 0.05 + 1.56 * CY * o[4] if off else vc(o, [i])
        if op1 is None:
            return emit("v", lambda q: q.tensor_scalar(o[3], src, a1, None, op0), R, [o], cost)
        return emit("v", lambda q: q.tensor_scalar(o[3], src, a1, a2, op0, op1), R, [o], cost)

    def tt(o, a, b, o_, off=None):
        if off:
            return emit("v", lambda q: q.tensor_tensor(o[3], a[3].indirect(off[3]), b[3], o_), [a, b, off], [o], 0.05 + 1.56 * CY * o[4])
        k = 1 if a[0] in psum or b[0] in psum else 2
        return emit("v", lambda q: q.tensor_tensor(o[3], a[3], b[3], o_), [a, b], [o], FX + CY * max(64, k * o[4]))

    def cp(o, i):
        return emit("v", lambda q: q.tensor_copy(o[3], i[3]), [i], [o], vc(o, [i]))

    def fill(o, c):
        return emit("v", lambda q: q.memset(o[3], c), [], [o], vc(o, []))

    def scan(o, d0, d1, p0, p1):
        return emit("v", lambda q: q.tensor_tensor_scan(o[3], d0[3], d1[3], 0.0, p0, p1), [d0, d1], [o], vc(o, [d0, d1]))

    def vtr(o, i):
        return emit("v", lambda q: q.transpose(o[3], i[3]), [i], [o], vc(o, [i]))

    def act(o, i, f, bias=0.0, scale=1.0, off=None):
        src = i[3].indirect(off[3]) if off else i[3]
        f = af.Identity if f == af.Copy and bias else f
        sc, extra = (scale[3], [scale]) if isinstance(scale, tuple) else (scale, [])
        return emit("s", lambda q: q.activation(o[3], src, f, bias=bias, scale=sc), [i] + ([off] if off else []) + extra, [o],
                    (0.065 + 1.56 * CY * o[4]) if off else FS + CY * max(64, o[4]))

    def sfill(o, c):
        return act(o, A("X1", 0, o[4]), af.Identity, scale=0.0, bias=c)

    def iota(o, pattern, base, cm=0):
        cost = 0.13 + 2 * CY * o[4]
        if SCRATCH[o[0]][2] == I32:
            return emit("g", lambda q: q.iota(o[3], pattern, base, cm), [], [o], cost)
        return emit("g", lambda q: q.iota(o[3], pattern, base, cm, allow_small_or_imprecise_dtypes=True), [], [o], cost)

    def const(o, c):
        return iota(o, [[0, o[4]]], c)

    def gcopy(o, i):
        return emit("g", lambda q: q.affine_select(o[3], i[3], [[0, o[4]]], op.is_ge, 0.0, 0, 0), [i], [o], 0.17 + 2 * CY * o[4])

    def mmx(terms, first=True, last=True):
        def go(q):
            for j, (o, l, r) in enumerate(terms):
                ins = q.matmul(o[3], l[3], r[3], first and j == 0, last and j == len(terms) - 1)
            return ins
        return emit("t", go, [x for t in terms for x in t[1:]], list({t[0][1:3]: t[0] for t in terms}.values()),
                    FX + PE * sum(max(64, o[4]) * (4 if SCRATCH[l[0]][2] == F32 else 1) for o, l, r in terms))

    def mms(o, terms, first=True, last=True):
        return mmx([(o, l, r) for l, r in terms], first, last)

    nd = [0]

    def dma(e, o, i, R, Wt, lat):
        s = "d%d" % nd[0]
        nd[0] += 1
        return emit(e, lambda q: q.dma_start(o, i), R, Wt, 0.05, sem=s, inc=16, lat=lat)

    def chain(seq):
        for x, y in zip(seq, seq[1:]):
            y["soft"].append(x)

    def LI(j, n=1):
        return A("LI", 12 * j, 12 * (j + n))

    def LF(j, n=1):
        return A("LF", 12 * j, 12 * (j + n))

    def send(k, nxt, lat):
        o, i, s, r = A("a%s%d" % (k, nxt)), A("o%s%d" % (k, nxt % 2)), "l%s%d" % (k, nxt % 2), "q%s%d" % (k, nxt)
        me = emit("g", lambda q: q.remote_dma(out_ap=o[3], in_ap=i[3], remote_sem=T.sem[r], local_sem=T.sem[s],
                                              pid=pid, routing_id=rid, dma_engine_mask=emask), [i], [], 0.6, sem=s, inc=-neng, lat=lat)
        net = {"e": "net", "need": [me], "cost": 0.0, "sem": r, "v": neng, "inc": 0, "lat": 0.0, "i": len(ops), "soft": [], "bonus": 0.0}
        ops.append(net)
        wr.setdefault(o[0], []).append((o, net))
        return me

    chain([dma("y", T.inL[:, :], T.lem[:, :], [], [A("inL")], 2.2),
           dma("y", T.inC[:, :], T.con[:, :], [], [A("inC")], 2.2),
           dma("y", T.P[:, 0:W], T.prop[:, :], [], [A("P", 0, W)], PLAT),
           dma("y", T.inLim[:, 0:TV], T.lim[:, :], [], [A("inLim", 0, TV)], 2.2)])
    def Y(p, a=0, b=12):
        return A("SG", 14 - 14 * p, (16 * a, 16 * b))
    chain([dma("s", Y(0)[3], T.ex[:, :], [], [Y(0)], 2.2),
           dma("s", T.inO[:, :], T.org[:, :], [], [A("inO")], 2.2),
           dma("s", T.inB[:, :], T.cnt[:, :], [], [A("inB")], 2.2)])

    def kI(a, n=1):
        return A("kI", a, a + n)

    def kF(a, n=1):
        return A("kF", a, a + n)

    def rows(x, n=16):
        return A(x, (0, 12), (0, n))
    iota(A("mpI"), [[1, 160]], -16, -1)
    iota(A("sI", 0, 1), [[0, 1]], 0, 1)
    iota(A("sI", 16, 25), [[-16, 9]], 0, 1)
    iota(A("sI", 32, 46), [[16, 14]], 0)
    iota(A("sI", 48, 72), [[1, 24]], 0)
    iota(A("gI"), [[16, 8], [0, 16]], 15, -1)
    b0, b1, qF = kF(0), kF(1), kF(2)
    fill(A("X1", 0, R18), 0.0)
    ts(kI(0), A("sI", 0, 1), 16, op.bitwise_and)
    ts(kI(1), A("sI", 0, 1), 15, op.bitwise_and)
    ts(b0, kI(0), 0, op.is_equal)
    ts(b1, kI(0), 16, op.is_equal)
    cp(qF, kI(1))
    ts(A("ID"), A("mpI"), 0, op.is_equal)
    IDF = A("ID", 16, 144)
    for j, (at, b) in enumerate(((16, b0), (0, b0), (32, b1), (16, b1))):
        act(A("SM", j), A("ID", at, at + 128), af.Copy, scale=b)
    ts(kI(16, 9), A("sI", 16, 25), 4, op.arith_shift_right)
    fill(A("ZF"), 0.0)
    ts(A("ZF", 15, 144, 16), kI(16, 9), 0, op.is_equal)
    for z, s in (("ZL", 2.0 ** 27), ("ZS", -2.0 ** 17), ("ZC", 2.0 ** 31)):
        act(A(z), A("ZF"), af.Copy, scale=s)
    act(A("EY"), IDF, af.Copy)
    act(A("NE"), A("EY"), af.Copy, scale=-1.0)
    act(A("NW"), A("EY"), af.Copy, scale=-2.0 ** 18)
    act(A("I2"), A("EY"), af.Copy, scale=2.0)
    const(A("Bf", 36, 48), -130)
    fill(A("ONE"), 1.0 / 128)
    fill(A("CL", (1, 14)), -7.5 * 2.0 ** 27)
    const(A("CL", (0, 15, 14)), 0)
    fill(A("CC"), -7.5 * 2.0 ** 31)
    for kind, h, a, b in PLAN:
        if kind == "sign":
            fill(A("CL", (a + 1, b + 1), (8 * h, 8 * h + 8)), 2.0 ** 27)
        if kind == "csign":
            fill(A("CC", (a, b), (8 * h, 8 * h + 8)), 2.0 ** 31)
    const(A("CK"), 6 << 16)
    ts(A("KX", 0, 128), A("mpI", 16, 144), 15, op.bitwise_and)
    ts(A("GW"), A("KX", 0, 128), 0, op.is_equal, 2.0 ** -4, op.mult)
    ts(A("KX", 128, 256), A("gI"), 4, op.arith_shift_right)
    ts(A("BO"), A("KX", 128, 256), 0, op.is_equal, 2.0 ** 16, op.mult)
    const(A("P", W, PW), 0)
    const(A("P", DUMP - 1, DUMP), -(1 << 20))

    ts(kF(16, 12), A("sI", 32, 44), qF, op.add)
    const(A("cB", 0, 12), 0)
    act(A("cB", 12, 24), kF(16, 12), af.Copy)
    ts(kI(32, 2), kF(16, 2), -5.5, op.add, 1.0 / 12, op.mult)
    ts(kF(32, 2), kI(32, 2), -12, op.mult)
    tt(kF(64, 2), kF(32, 2), kF(16, 2), op.add)
    ts(A("BL"), kF(64, 2), 17, op.mult, 16, op.add)

    const(A("DS"), 8192)
    const(A("DS", 16, R17, 17), 0)
    const(A("DS", R17 + 16, 2 * R17, 17), -15 << 17)
    sfill(A("DS", 0, 2 * R17, 17), -BIG)
    cp(A("limF", 0, TV), A("inLim", 0, TV))
    ts(kF(96, 17), A("sI", 48, 65), qF, op.subtract)
    ts(A("TX", 0, 17), kF(96, 17), 0, op.is_equal)
    ts(A("TX", 24, 41), kF(96, 17), 1, op.is_equal)
    tt(A("PM", 0, 17), A("TX", 0, 17), A("TX", 24, 41), op.subtract)
    for t in range(TV):
        act(A("PM1", 17 * t, 17 * t + 17), A("PM", 0, 17), af.Copy, scale=A("limF", t, t + 1))
    mms(A("XL", 256, 358), [(A("BO"), A("PM1"))])
    const(A("CT"), 1 << 20)
    const(A("CT", 16, 102, 17), 8 << 16)
    sfill(A("CT", 0, 102, 17), -BIG)
    tt(A("DC", (0, TV), (0, 17)), A("XL", 256, 358), A("CT"), op.add)
    for a, b in ((17, 34), (34, 68), (68, 136), (136, 204)):
        gcopy(A("DC", (0, TV), (a, b)), A("DC", (0, TV), (0, b - a)))

    def Z(x, j, c=None, n=1):
        x, at = ("MS", 80 + R18 * j) if x == "Dd" else (x, 6 + R18 * j)
        if c is None:
            return A(x, at, at + R18) if j else A(x, at - 5, at + R18 - 5, 6)
        return A(x, at + c, at + c + R18 * n - 17, 18)
    const(A("M", 0, 6 + 2 * R18), 1)
    const(Z("M", 0, -5), 0)
    const(Z("M", 1, 0), 0)
    sfill(Z("Dd", 0, 7), -2.0 ** 20)
    sfill(Z("Dd", 1), 2.0 ** 20)
    const(A("ML"), 1)
    const(A("ML", 0, Q, 16), 0)
    const(A("DdL"), 8192)
    const(A("DL"), 0)
    const(A("DL", (0, 12), 16), 8192)
    const(A("L2", (0, 12), 16), 0)
    const(A("AB", (0, 12), (256, 272)), 0)
    const(A("SG", (1, 13), (256, 272)), 0)
    const(A("SG", (0, 15, 14), (Q, 272)), 0)
    const(A("SG", 13), 0)
    const(LI(19), -KEEP - (1 << 20))
    const(A("cD", 0, 12), W)
    act(A("cD", 12, 24), kF(16, 12), af.Copy, bias=float(DUMP))
    for x in ("aV0", "oV0", "oV1"):
        const(A(x, (0, 12), 16), 0)

    def turn(x, t, s, out):
        n = x[4] // 16
        vtr(A(t), x)
        mms(A(out, (0, n, 2)), [(A(s, 0), A(t, (0, n, 2))), (A(s, 1), A(t, (1, n, 2)))])
        mms(A(out, (1, n, 2)), [(A(s, 2), A(t, (0, n, 2))), (A(s, 3), A(t, (1, n, 2)))])
        return A(out, (0, n))

    def lists(o, x, s, o_):
        return [ts(A(o, 96 * h, 96 * h + 96), A(x, (0, 12), (8 * h, 8 * h + 8)), s, o_) for h in (0, 1)]

    cp(A("X0", 0, Q), A("inL"))
    turn(A("X0", 0, Q), "TL", "SM", "S4")
    lists("oL1", "S4", 1, op.mult)
    act(rows("L2"), A("S4", (0, 12)), af.Copy, scale=2.0)
    TXs = [A("TX", Q * j, Q * j + Q) for j in range(3)]
    early = [act(A("XS", 0, Q), A("inB"), af.Copy, scale=2.0 ** 16),
             act(A("S3", (0, 12)), A("inB"), af.Copy, bias=2.0 ** 19),
             act(A("XL", 0, Q), A("inO"), af.Copy, scale=-4096.0, bias=15 * 4096.0)]
    ts(TXs[1], A("inC"), -2.0 ** 22, op.mult)
    tt(TXs[0], A("XS", 0, Q), A("inC"), op.add)
    tt(A("S3", (0, 12)), A("S3", (0, 12)), TXs[1], op.min)
    tt(TXs[2], A("S3", (0, 12)), TXs[0], op.max)
    tt(A("X0", Q, 2 * Q), A("XL", 0, Q), TXs[2], op.add)
    first = {"word": cp(A("sV"), turn(A("X0", Q, 2 * Q), "TV", "SM", "S3"))}
    gcopy(rows("aV0"), A("sV"))
    sfill(A("XC", (0, 12), 16), -2 * BIG)
    const(A("rB", (0, 12), 16), 1 << 20)
    const(A("wC", R18, R18 + 2), 0)

    def names():
        return ts(A("sC"), A("sV"), 4095 + (1 << 19), op.bitwise_and)
    first["name"] = names()
    first["list0"], first["list1"] = lists("aC0", "sC", W, op.min)

    def yrep(bank, p, a, b, last):
        def go(q):
            for k in range(8):
                ins = q.matmul(A(bank, (k, 8 * (b - a), 8))[3], A("NE")[3], Y(p, a, b)[3], k == 0, last and k == 7)
            return ins
        return emit("t", go, [A("NE"), Y(p, a, b)], [A(bank, (0, 8 * (b - a)))], FX + PE * 512)

    def yexp(p):
        made = {}
        for a, b, bank in YB:
            made["ty%d" % a] = yrep(bank, p, a, b, True)
            made["y%d" % a] = act(A("YE", 128 * a, 128 * b), A(bank, (0, 8 * (b - a))), af.Copy, scale=-1.0)
        return made

    def span(x, h, a, b):
        return A(x, HALF * h + 128 * a, HALF * h + 128 * b)

    def piece(x, h, a, b):
        return A(x, (a, b), (128 * h, 128 * h + 128))

    def weights(z):
        return [A(z, 15 - q, 143 - q) for q in range(16)]

    def change(c, z, old):
        c["gz"] = cp(A("DdL", 0, Q, 16), z)
        c["tL"] = mms(A("S4", (0, 12)), [old], last=False)
        c["wL"] = scan(A("wL"), A("ML"), A("DdL"), op.mult, op.add)
        c["AL"] = act(A("zL"), A("wL"), af.Abs, scale=2.0, bias=-30.0 * 8192)
        c["DL"] = act(rows("DL"), A("zL"), af.Relu, scale=-8192.0, bias=8192.0 * 8192)
        c["tE"] = mms(A("S4", (0, 12)), [(A("EY"), rows("DL"))], first=False)
        c["min"] = tt(rows("L2"), A("S4", (0, 12)), A("zL"), op.min)

    chain(early)
    yexp(0)
    visits = []
    for t in range(TV):
        p, nxt = t % 2, t + 1
        last = nxt == TV
        lL, lC, V = ["a%s%d" % (k, t) for k in "LCV"]
        oL, oC, oV, oZ = ["o%s%d" % (k, nxt % 2) for k in "LCVZ"]
        IC, yv, yn = "IC", Y(p), Y(1 - p)
        c = {} if t else first
        if t:
            z = A("aZ%d" % t, 2, 36, 3)
            c["nL0"], c["nL1"] = [gcopy(A("Lf", (0, 12), (8 * h, 8 * h + 8)), A(lL, 96 * h, 96 * h + 96)) for h in (0, 1)]
            change(c, z, (A("I2"), A("Lf")))
            if not last:
                c["lL0"], c["lL1"] = lists(oL, "L2", 0.5, op.mult)
            c["cz"] = cp(LI(26), z)
            c["az"] = ts(LI(27), LI(26), 8191 + (1 << 20), op.bitwise_and)
            c["lz"] = ts(A("NL"), LI(27), DUMP - 1, op.min)
            c["wz"] = tt(A("L2", (0, 12), 16), LI(26), LI(27), op.add)
            c["fz"] = act(A("DL", (0, 12), 16), z, af.Identity, scale=-2.0 ** -18, bias=7.5 + 1.0 / 128)
            c["N"] = tt(A("DN"), A("P"), yv, op.subtract, off=A("NL"))
            c["overN"] = ts(A("SG", 13, (0, Q)), A("DN"), 0, op.is_gt)
            c["absN"] = act(A("AB", (0, 12), (256, 272)), A("DN"), af.Abs)
        else:
            lL = oL
        if not last:
            c["sendL"] = send("L", nxt, 3.0)
        diff, final = {}, {x[0]: x for x in PLAN}
        XL = A("XL", 17, 17 + R17)
        c["kL"] = mms(A("XL", 0, 15 * 17), [(A("ONE"), A("CL"))], last=False)
        c["kC"] = mms(rows("XC"), [(A("ONE"), A("CC"))], last=False)
        c["xS"] = mms(A("XS", 0, R17), [(A("NW"), A("DL"))], last=False)
        for x in PLAN:
            kind, h, a, b = x
            ye, at = A("YE", 128 * a, 128 * b), (96 * h + 8 * a, 96 * h + 8 * b)
            if kind == "L":
                diff[h, a, "l"] = span("D", h, a, b)
                me = tt(span("D", h, a, b), A("P"), ye, op.subtract, off=A(lL, *at))
            elif kind == "C":
                me = tt(span(IC, h, a, b), A("P"), ye, op.is_gt, off=A(lC, *at))
            elif kind[1:].isdigit():
                raw = span(kind[0].upper() + "R", h, a, b)
                diff[h, a, kind[0]] = ps = A("S" + kind[1], (0, 8 * (b - a)))
                c["n%s%d%d" % (kind[0], h, a)] = yrep(ps[0], p, a, b, False) if b > YB[-1][1] else mms(ps, [(A("NE"), ye)], last=False)
                me = act(raw, A("P"), af.Copy, off=A(lL if kind[0] == "l" else lC, *at))
                c["e%s%d%d" % (kind[0], h, a)] = mms(ps, [(A("EY"), raw)], first=False)
                kind = kind[0]
            elif kind == "abs":
                me = act(piece("AB", h, a, b), diff[h, a, "l"], af.Abs)
            elif kind == "sign":
                me = act(piece("SG", h, a + 1, b + 1), diff[h, a, "l"], af.Sign, bias=-0.5)
            elif kind == "csign":
                me = act(span(IC, h, a, b), diff[h, a, "c"], af.Sign, bias=-0.5)
            elif kind == "over":
                me = ts(piece("SG", h, a + 1, b + 1), diff[h, a, "l"], 0, op.is_gt)
            elif kind == "XS":
                me = mms(A("XS", 17 * a, 17 * b), [(w, A("AB", (a, b), (q, 272, 16))) for q, w in enumerate(weights("ZS"))], False, x == final[kind])
            elif kind == "XL":
                lo, hi = a + 1 - (p and a == 0), b + 1 + (2 - p) * (b == 12)
                me = mms(A("XL", 17 * lo, 17 * hi), [(w, A("SG", (lo, hi), (q, 272, 16))) for q, w in enumerate(weights("ZL"))], False, False)
            else:
                me = mms(A("XC", (0, 12), (8 * h, 8 * h + 8)), [(w, A("IC", HALF * h + q, HALF * (h + 1), 16)) for q, w in enumerate(weights("ZC"))], False, x == final[kind])
            c["%s%d%d" % (kind, h, a)] = me
        c["xL"] = mms(XL, [(A("NW"), A("DL"))], first=False)
        if t:
            c["b4"] = act(A("Bf", 24, 36), A("MS", 48, 60), af.Identity, scale=2.0 ** -18, bias=130 - 0.375)
            c["tw"] = mms(A("MS", 32, 44), [(A("GW"), A("Bf", 0, 12))] + [(A("NW"), A("Bf", 12 * j, 12 * j + 12)) for j in (2, 3)])
        u, RL = A("RLS", 16, R17, 17), A("RLS", R17 + 16, 2 * R17, 17)
        c["u"] = act(u, A("XL", 238 - 238 * p, 250 - 238 * p), af.Copy, scale=2.0 ** -26)
        c["uu"] = act(A("uF"), A("RLS", 0, R17), af.Copy, scale=0.5, off=A("BL", 0, 2))
        c["mkL"] = tt(A("mkL"), XL, A("L2"), op.min)
        c["mkN"] = tt(A("mkL", 16, R17, 17), A("XL", 221, 233), A("L2", (0, 12), 16), op.min)
        c["scanL"] = scan(A("RLS", R17, 2 * R17), A("DS", 0, R17), A("mkL"), op.add, op.max)
        c["flag"] = act(LF(0), RL, af.Relu, bias=2.0 ** 24)
        c["u37"] = act(LF(6), u, af.Identity, scale=18.5, bias=float(t))
        c["a97"] = act(LF(7), RL, af.Identity, scale=0.5, bias=97.0 * t)
        c["G"] = act(Z("Dd", 1, 0), RL, af.Identity, scale=0.5, bias=-2.0 ** 19)
        c["cpu"] = ts(LI(0, 2), A("RLS", 16, 2 * R17, 17), -(1 << 18), op.max)
        c["and2"] = ts(LI(3, 2), LI(0, 2), 8191 + (1 << 18), op.bitwise_and, 1, op.arith_shift_right)
        c["mul"] = tt(LI(7, 2), LI(3, 2), A("uF", 0, 24), op.mult)
        c["shf"] = ts(LI(9, 2), LI(7, 2), 5, op.arith_shift_right)
        c["add"] = tt(LI(11, 2), LI(9, 2), LF(6, 2), op.add)
        c["n5"] = ts(LI(5), LI(12), 3840 + (1 << 30), op.bitwise_and)
        c["m6"] = ts(LI(13), LI(11), 4095, op.bitwise_and)
        c["m7"] = tt(LI(25), LI(13), LF(0), op.add)
        VP, slot, BB = A("S3", (0, 12)), A("XL", 256, 256 + R17), A("XL", 464, 488)
        c["tV"] = mms(VP, [(IDF, rows(V))], last=False)
        c["r0"] = act(rows("rF"), rows(V), af.Identity, bias=-32767.5)
        c["r"] = act(rows("rF"), rows("rF"), af.Identity, scale=2.0 ** -16, bias=1.5 * 2 ** 23)
        c["r1"] = act(rows("rB"), rows("rF"), af.Identity, scale=-128.0, bias=128 * (1.5 * 2 ** 23 + 19))
        c["slot"] = mms(slot, [(A("NW"), A("rB")), (A("ONE"), A("CK"))])
        c["cmin"] = tt(A("mk"), rows("XC", 17), A(V), op.min)
        c["mk"] = tt(A("mk"), slot, A("mk"), op.max)
        c["rc"] = scan(A("RC"), A("DC", t), A("mk"), op.add, op.max)
        RC = A("RC", 16, R17, 17)
        c["nb"] = ts(A("M", 7, 6 + 32 * 18, 18), A("RC"), 0, op.is_lt, off=A("BL", 0, 2))
        c["B"] = act(A("Bf", 0, 24), Z("M", 0, 1, 2), af.Copy, scale=-2.0 ** 20, bias=2.0 ** 20)
        c["bb"] = mms(BB, [(A("EY"), A("cB")), (A("EY"), A("Bf", 0, 24))])
        c["k16"] = tt(LI(16), RC, A("MS", 32, 44), op.subtract) if t else cp(LI(16), RC)
        c["a23"] = ts(LI(17), LI(16), (1 << 19) + (1 << 16) - 1, op.bitwise_and)
        c["a2"] = ts(LI(18), LI(16), (1 << 19) + (15 << 12), op.bitwise_and)
        c["a1"] = ts(LI(22), LI(16), (1 << 19) + (15 << 20), op.bitwise_and)
        c["of"] = ts(Z("M", 1, 2), LI(18), 1 << 19, op.is_ge, 0.5, op.mult)
        c["conv"] = tt(Z("Dd", 0, 1, 2), LI(17, 2), LI(18, 2), op.add)
        c["conv2"] = ts(Z("Dd", 1, 2), LI(22), KEEP // 2 + MID - (15 << 20), op.add)
        c["wC"] = scan(A("wC", 0, R18), Z("M", 1), Z("Dd", 1), op.mult, op.add)
        if not last:
            c["tB"] = mms(A("MS", 48, 60), [(A("GW"), A("Bf", 0, 12))])
        c["A"] = act(A("zC"), A("wC", 2, R18 + 2), af.Abs, scale=2.0, bias=-2.0 * MID)
        c["D1"] = act(A("D1"), rows("zC"), af.Relu, scale=-16.0, bias=16.0 * KEEP + 2 ** 16)
        c["tD"] = mms(VP, [(A("EY"), A("D1"))], first=False)
        if last:
            c["out"] = tt(A("X0", Q, 2 * Q), VP, rows("zC"), op.min)
        else:
            c["cmn"] = tt(A("sV"), VP, rows("zC"), op.min)
            c["andC"] = names()
            c["lC0"], c["lC1"] = lists(oC, "sC", W, op.min)
            c["sendC"] = send("C", nxt, 3.0)
            c["gV"] = gcopy(rows(oV), A("sV"))
            c["sendV"] = send("V", nxt, 3.5)
        c["an"] = tt(LI(23, 2), LI(4, 2), BB, op.add)
        c["adr"] = tt(LF(2, 2), LI(23, 2), A("cD"), op.min)
        c["LST"] = cp(A("LST"), LF(2, 2))
        PL, NL = A("LST", 0, 12), A("LST", 12, 24)
        c["d"] = tt(A("pa"), A("P"), yv, op.subtract, off=PL)
        c["y"] = act(yn, A("pa"), af.Abs)
        c["md0" if last else "md"] = ts(A("md"), A("pa"), 0, op.min)
        c["end" if last else "write"] = emit("v", lambda q, to=NL, y=yv: q.tensor_tensor(T.P[:, :].indirect(to[3]), y[3], T.md[:, :], op.add), [A("md"), yv, NL], [A("P")], 0.05 + 3.8 * CY * Q)
        c["scanS"] = scan(A("RS"), A("DS", R17, 2 * R17), A("XS", 0, R17), op.add, op.max)
        c["cps"] = cp(LI(2), A("RS", 16, R17, 17))
        c["cod"] = ts(LI(14, 2), LI(1, 2), 15 << 13, op.bitwise_and)
        c["w2"] = tt(LF(4, 2), LI(14, 2), LI(24, 2), op.add)
        c["w0"] = tt(Z("Dd", 0, -5), LF(4), LF(5), op.min)
        c["z"] = scan(A(oZ), Z("M", 0), Z("Dd", 0), op.mult, op.add)
        if not last:
            c["sendZ"] = send("Z", nxt, 2.5)
            c.update(yexp(1 - p))
        visits.append(c)
    change({}, A(oZ, 2, 36, 3), (IDF, rows("L2")))
    for e in ORDER:
        names_ = [(k.rstrip("+"), int(k[-1] == "+")) for k in ORDER[e].split()]
        chain([visits[t + d][k] for t in range(-1, TV) for k, d in names_ if 0 <= t + d < TV and k in visits[t + d]])

    dma("y", T.zp[:, :], T.P[:, 0:W], [A("P", 0, W)], [], 6.0)
    dma("y", T.zy[:, :], yn[3], [yn], [], 2.0)
    word = turn(A("X0", Q, 2 * Q), "TV", "SM", "S2")
    act(A("E0", 0, Q), turn(rows("L2"), "TL", "SM", "S1"), af.Copy, scale=0.5)
    dma("s", T.zl[:, :], T.E0[:, 0:Q], [A("E0", 0, Q)], [], 2.0)
    cp(A("sV"), word)
    names()
    act(A("TX", 0, Q), word, af.Sign, scale=-1.0, bias=2.0 ** 19 - 0.5)
    act(rows("XC"), A("TX", 0, Q), af.Identity, scale=2048.5, bias=2047.5)
    tt(A("E0", Q, 2 * Q), rows("XC"), A("sC"), op.min)
    dma("y", T.zc[:, :], T.E0[:, Q:2 * Q], [A("E0", Q, 2 * Q)], [], 2.0)
    ts(A("tS"), A("sV"), 12, op.arith_shift_right, 15, op.bitwise_and)
    ts(A("oB", 0, Q), A("tS"), -1, op.mult, 15, op.add)
    dma("y", T.zo[:, :], T.oB[:, 0:Q], [A("oB", 0, Q)], [], 2.0)
    ts(A("inL"), A("sV"), 16, op.arith_shift_right, 7, op.bitwise_and)
    ts(A("S3", (0, 12)), A("sC"), -(1 << 19), op.add, 0, op.max)
    tt(A("oB", Q, 2 * Q), A("S3", (0, 12)), A("inL"), op.add)
    dma("y", T.zb[:, :], T.oB[:, Q:2 * Q], [A("oB", Q, 2 * Q)], [], 2.0)

    succ = [[] for _ in ops]
    for o in ops:
        o["need"] = list({x["i"]: x for x in o["need"]}.values())
        o["all"] = list({x["i"]: x for x in o["need"] + o["soft"]}.values())
        for x in o["all"]:
            succ[x["i"]].append(o)
    left, line = {o["i"]: len(o["all"]) for o in ops}, [o for o in ops if not o["all"]]
    for o in line:
        for s in succ[o["i"]]:
            left[s["i"]] -= 1
            if not left[s["i"]]:
                line.append(s)
    assert len(line) == len(ops)
    for o in reversed(line):
        o["pri"] = o["bonus"] + o["cost"] + o["lat"] + max([0.0] + [s["pri"] + (WK if s["e"] == o["e"] else WX) for s in succ[o["i"]]])
    left = {o["i"]: len(o["all"]) for o in ops}
    free = {e: 0.0 for e in list(queues) + ["net"]}
    ready = {e: [] for e in free}
    for o in ops:
        if not left[o["i"]]:
            ready[o["e"]].append((0.0, o))
    done = []
    while len(done) < len(ops):
        best = None
        for e in ready:
            for (r, o) in ready[e]:
                k = (max(r, free[e] if e != "net" else 0.0), -o["pri"], o["i"])
                if best is None or k < best[0]:
                    best = (k, e, r, o)
        k, e, r, o = best
        ready[e].remove((r, o))
        o["st"] = k[0]
        o["fin"] = k[0] + o["cost"] + o["lat"]
        free[e] = k[0] + o["cost"]
        done.append(o)
        for s in succ[o["i"]]:
            left[s["i"]] -= 1
            if not left[s["i"]]:
                ready[s["e"]].append((max([0.0] + [x["fin"] + (WK if s["e"] == x["e"] else WX) for x in s["need"]] + [x["st"] + x["cost"] for x in s["soft"]]), s))
    count = {}
    clock = {e: {} for e in queues}
    for o in done:
        e = o["e"]
        if e == "net":
            o["c"] = {}
            continue
        want = {}
        for x in o["need"]:
            if x["v"] > want.get(x["sem"], (0, None))[0]:
                want[x["sem"]] = (x["v"], x)
        ck = clock[e]
        for s in sorted(want, key=lambda s: -len(want[s][1]["c"])):
            v, x = want[s]
            if ck.get(s, 0) >= v:
                continue
            queues[e].wait_ge(T.sem[s], v)
            for k, y in x["c"].items():
                ck[k] = max(ck.get(k, 0), y)
            ck[s] = v
        ins = o["fn"](queues[e])
        if o["inc"] > 0:
            ins.then_inc(T.sem[o["sem"]], o["inc"])
        count[o["sem"]] = count.get(o["sem"], 0) + abs(o["inc"])
        o["v"] = count[o["sem"]]
        o["c"] = dict(ck)
    for s in sorted(count):
        if clock["g"].get(s, 0) < count[s]:
            g.wait_ge(T.sem[s], count[s])
